import numpy as np
import ml_dtypes


def mxq(x, axis, fmt="e4m3"):
    dtype, down = {"e4m3": (ml_dtypes.float8_e4m3fn, 7), "e5m2": (ml_dtypes.float8_e5m2, 14)}[fmt]
    v = np.moveaxis(np.asarray(x, np.float32).astype(ml_dtypes.bfloat16).astype(np.float64), axis, -1)
    blocks = v.reshape(v.shape[:-1] + (-1, 32))
    amax = np.abs(blocks).max(-1, keepdims=True)
    byte = np.maximum(np.where(amax > 0, np.frexp(amax)[1] - 1 + 127, 0) - down, 1)
    scale = np.exp2(byte - 127.0)
    codes = (blocks / scale).astype(np.float32).astype(dtype).astype(np.float64)
    return np.moveaxis((codes * scale).reshape(v.shape), -1, axis)


WIDE = False


def mx_kscale(k):
    if not WIDE:
        return np.ones(k)
    levels = np.array([10, -10, 5, -5, 0])
    if k % 512:
        return np.exp2(np.random.permutation(np.resize(levels, k // 32))).repeat(32)
    a = np.empty((k // 512, 16))
    for p in range(k // 512):
        a[p, :8] = np.random.permutation(np.resize(levels, 8))
        for g in range(8):
            far = levels[np.abs(levels - a[p, g]) >= 10]
            a[p, g + 8] = far[np.random.randint(len(far))]
    return np.exp2(a.ravel()).repeat(32)


def f64(x):
    return np.asarray(x).astype(np.float64)


def striped(idx):
    return np.tile(idx.reshape(-1, 16).T, (8, 1)).astype(np.uint16)


def unstriped(offs):
    return offs[:16].T.reshape(-1).astype(np.int64)


def pack_weight(w):
    k, n = w.shape
    w = f64(np.asarray(w, np.float32).astype(ml_dtypes.bfloat16)).reshape(k // 32, 32, n)
    amax = np.abs(w).max(1)
    byte = np.clip(np.where(amax > 0, np.frexp(amax)[1] - 1 + 127 - 7, 1), 1, 254)
    scaled = (w * np.exp2(127.0 - byte)[:, None, :]).reshape(k, n).astype(np.float32)
    words = np.ascontiguousarray(scaled.reshape(k // 512, 128, 4, n).transpose(0, 1, 3, 2)).astype(ml_dtypes.float8_e4m3fn).view(np.uint8)
    return words, np.ascontiguousarray(byte.astype(np.uint8).reshape(k // 512, 16, n))


def unpack_weight(words, scales):
    g, p, n, _ = words.shape
    vals = np.ascontiguousarray(words).view(ml_dtypes.float8_e4m3fn).astype(np.float64) * np.repeat(np.exp2(scales.astype(np.float64) - 127.0), 8, axis=1)[..., None]
    return vals.transpose(0, 1, 3, 2).reshape(g * 512, n)


K, T, S, V, H, N = 1024, 1024, 512, 256, 512, 128


def setup_inputs():
    n = np.random.standard_normal
    s = mx_kscale(K)[:, None]
    u = mx_kscale(H)
    near = np.random.permutation(S)
    packed_xT = pack_weight(n((K, T)) * s)
    return {
        "x_words": packed_xT[0],
        "x_scales": packed_xT[1],
        "w1": (n((K, H)) / np.sqrt(K) / s * u).astype(np.float32),
        "w3": (n((K, H)) / np.sqrt(K) / s).astype(np.float32),
        "w2": (n((H, N)) / np.sqrt(H) / u[:, None]).astype(np.float32),
        "offs": striped(np.random.permutation(T)[:S]),
        "pos1": striped(near[:V]),
        "pos2": striped(near[V:]),
        "pos3": striped(np.random.permutation(S)[:V]),
    }


def reference(x_words, x_scales, w1, w3, w2, offs, pos1, pos2, pos3):
    xq = unpack_weight(x_words, x_scales)[:, unstriped(offs)]
    a = mxq(f64(w1), 0, "e4m3").T @ xq
    a0 = a[:, unstriped(pos1)]
    ee = mxq(f64(w3), 0, "e4m3").T @ xq
    e0 = ee[:, unstriped(pos1)]
    a1 = a[:, unstriped(pos2)]
    e1 = ee[:, unstriped(pos2)]
    a2 = a[:, unstriped(pos3)]
    e2 = ee[:, unstriped(pos3)]
    ma = (a0 + a1 + a2) / 3
    me = (e0 + e1 + e2) / 3
    z = (a0 * e0 + a1 * e1 + a2 * e2) / 3 - (ma * me)
    rr = z / (np.sqrt(((e0) ** 2 + (e1) ** 2 + (e2) ** 2) / 3 - ((me) ** 2) + 0.1))
    return mxq(f64(w2), 0, "e4m3").T @ mxq(rr, 0, "e4m3")

@@ -1,0 +1,302 @@
+import math
+from contextlib import ExitStack
+
+import concourse.mybir as mybir
+from concourse.masks import make_identity
+
+K, T, S, V, H, N = 1024, 1024, 512, 256, 512, 128
+FLOPS = 2 * (2 * K * H * S + H * N * V)
+
+F32 = mybir.dt.float32
+BF16 = mybir.dt.bfloat16
+I32 = mybir.dt.int32
+U32 = mybir.dt.uint32
+U16 = mybir.dt.uint16
+U8 = mybir.dt.uint8
+FP8X4 = mybir.dt.float8_e4m3fn_x4
+ALU = mybir.AluOpType
+ACT = mybir.ActivationFunctionType
+
+P = 128
+PACK = 4
+K_PASS = P * PACK
+PASSES = K // K_PASS
+HALF = H // 2
+TILES = H // P
+VH = V // P
+
+
+def tile_picked_ycovn_corr_p_kernel(
+    tc, x_words, x_scales, w1, w3, w2, offs, pos1, pos2, pos3, out
+):
+    nc = tc.nc
+    with ExitStack() as ctx:
+        keep = ctx.enter_context(tc.tile_pool(name="keep", bufs=1))
+        mm_ps = ctx.enter_context(tc.psum_pool(name="mm_ps", bufs=3))
+        one_ps = ctx.enter_context(tc.psum_pool(name="one_ps", bufs=1))
+
+        def sb(name, shape, dtype):
+            return keep.tile(shape, dtype, name=name, align_bytes=64)
+
+        offs_t = sb("offs_t", [P, S // 16], U16)
+        pos_t = [sb("pos_t%d" % i, [P, V // 16], U16) for i in range(3)]
+        xw = [sb("xw%d" % g, [P, T], I32) for g in range(PASSES)]
+        xs = sb("xs", [P, T], U8)
+
+        raw = {}
+
+        def load_w(name, w, hf, g):
+            t = sb("raw_%s_%d_%d" % (name, hf, g), [P, PACK * HALF], F32)
+            rows = w[g * K_PASS : (g + 1) * K_PASS, hf * HALF : (hf + 1) * HALF]
+            nc.sync.dma_start(
+                t[:].rearrange("p (j c) -> p j c", j=PACK), rows.rearrange("(p j) c -> p j c", j=PACK)
+            )
+            raw[(name, hf, g)] = t
+
+        def load_x(g):
+            nc.sync.dma_start(xw[g][:], x_words[g].rearrange("p n t -> p (n t)").bitcast(I32))
+
+        nc.gpsimd.memset(xs[:].bitcast(I32), 0)
+        nc.sync.dma_start(offs_t[:], offs)
+        load_x(0)
+        for q in range(4):
+            nc.scalar.dma_start(
+                xs[32 * q : 32 * q + 4 * PASSES, :].bitcast(I32),
+                x_scales[:, 4 * q : 4 * q + 4, :].bitcast(I32),
+            )
+        load_w("e", w3, 0, 0)
+        load_x(1)
+        load_w("e", w3, 0, 1)
+        w2_raw = sb("w2_raw", [P, PACK, N], F32)
+        nc.sync.dma_start(w2_raw[:], w2.rearrange("(p j) c -> p j c", j=PACK))
+        for t, src in zip(pos_t, (pos1, pos2, pos3)):
+            nc.sync.dma_start(t[:], src)
+        for name, w, hf in (("e", w3, 1), ("a", w1, 0), ("a", w1, 1)):
+            for g in range(PASSES):
+                load_w(name, w, hf, g)
+
+        warm = sb("warm", [P, 2], F32)
+        nc.vector.memset(warm[:, 0:1], 1.0)
+        nc.scalar.activation(warm[:, 1:2], warm[:, 0:1], ACT.Abs_reciprocal_sqrt)
+
+        ident = sb("ident", [P, P], F32)
+        make_identity(nc, ident[:])
+
+        xg = [sb("xg%d" % g, [P, S], U32) for g in range(PASSES)]
+        xsg = sb("xsg", [P, S], U8)
+
+        def cast(dst, src, copy):
+            copy(
+                dst.rearrange("p (c i j) -> p c j i", i=4, j=PACK),
+                src.rearrange("p j (c i) -> p c j i", i=4),
+            )
+
+        def quant(name, grp, width):
+            codes = sb("codes_" + name, [P, width], U32)
+            scales = sb("scales_" + name, [P, width], U8)
+            nc.vector.quantize_mx(out=codes[:].bitcast(FP8X4), scales=scales[:], in_=grp)
+            return codes, scales
+
+        wq = {}
+        stage = {}
+
+        def cast_w(name, hf, g, lo, width, copy):
+            st = sb("stage_%s_%d_%d_%d" % (name, hf, g, lo), [P, V + 2 * width], F32)
+            src = raw[(name, hf, g)][:].rearrange("p (j c) -> p j c", j=PACK)
+            cast(st[:, V:].bitcast(BF16), src[:, :, lo : lo + width], copy)
+            stage[(name, hf, g, lo)] = st
+
+        def quant_w(name, hf, g, lo, width):
+            nm = "%s_%d_%d_%d" % (name, hf, g, lo)
+            codes, scales = quant(nm, stage[(name, hf, g, lo)][:, V:].bitcast(BF16), width)
+            for c in range(0, width, P):
+                wq[(name, 2 * hf + (lo + c) // P, g)] = (codes[:, c : c + P], scales[:, c : c + P])
+
+        accs = {}
+
+        def mm_pass(name, t, g):
+            if g == 0:
+                accs[(name, t)] = mm_ps.tile([P, S], F32, name="acc")
+            codes, scales = wq[(name, t, g)]
+            nc.tensor.matmul_mx(
+                out=accs[(name, t)][:],
+                lhsT=codes.bitcast(FP8X4),
+                lhsT_scale=scales,
+                rhs=xg[g][:].bitcast(FP8X4),
+                rhs_scale=xsg[4 * g : P, :],
+                start=(g == 0),
+                stop=(g == PASSES - 1),
+            )
+
+        win = {}
+
+        def evac(name, t, copy):
+            w = sb("win_%s_%d" % (name, t), [P, S], F32)
+            copy(w[:], accs[(name, t)][:])
+            win[(name, t)] = w
+
+        def quant_mm(name, hf, g):
+            quant_w(name, hf, g, 0, HALF)
+            for i in range(2):
+                mm_pass(name, 2 * hf + i, g)
+
+        def add_transposed(dst, srcs):
+            for i, s in enumerate(srcs):
+                nc.tensor.matmul(
+                    dst, lhsT=s, rhs=ident[:], is_transpose=True, start=(i == 0), stop=(i == len(srcs) - 1)
+                )
+
+        coef = {}
+        diff2 = {}
+        rT = {}
+
+        def e_side(hf, nxt):
+            e0 = [sb("e0_%d" % hf, [P, V], F32)[:], stage[nxt + (0, 0)][:, V : 2 * V]]
+            d1 = sb("d1_%d" % hf, [P, 2 * V], F32)[:]
+            d2 = stage[nxt + (1, 0)][:, 0 : 2 * V]
+            for i in range(2):
+                w = win[("e", 2 * hf + i)]
+                cols = slice(i * V, (i + 1) * V)
+                if i == 1:
+                    quant_mm(nxt[0], nxt[1], 0)
+                nc.vector.tensor_copy(e0[i], w[:].indirect(pos_t[0][:]))
+                nc.vector.tensor_tensor(d1[:, cols], w[:].indirect(pos_t[1][:]), e0[i], ALU.subtract)
+                if i == 1:
+                    quant_mm(nxt[0], nxt[1], 1)
+                nc.vector.tensor_tensor(d2[:, cols], w[:].indirect(pos_t[2][:]), e0[i], ALU.subtract)
+            c = [sb("c%d_%d" % (n, hf), [P, 2 * V], F32) for n in range(3)]
+            nc.vector.scalar_tensor_tensor(c[1][:], d1, 2.0, d2, ALU.mult, ALU.subtract)
+            nc.vector.scalar_tensor_tensor(c[0][:], d1, -1.0, d2, ALU.mult, ALU.subtract)
+            nc.vector.scalar_tensor_tensor(c[2][:], d2, 2.0, d1, ALU.mult, ALU.subtract)
+            coef[hf] = c
+            diff2[hf] = d2
+
+        vT = {}
+
+        def squares(hf):
+            sq = raw[("a", 1, hf)]
+            nc.scalar.activation(sq[:, 0 : 2 * V], diff2[hf], ACT.Square, scale=math.sqrt(3.0))
+            nc.scalar.activation(sq[:, 2 * V : 4 * V], coef[hf][1][:], ACT.Square)
+            vT[hf] = one_ps.tile([P, VH, 2, P], F32, name="vT")
+            for h in range(VH):
+                for i in range(2):
+                    lo = i * V + h * P
+                    add_transposed(vT[hf][:, h, i, :], [sq[:, o + lo : o + lo + P] for o in (0, 2 * V)])
+
+        def rsqrt(hf):
+            r = sb("rT_%d" % hf, [P, VH, 2 * P], F32)
+            nc.scalar.activation(
+                r[:], vT[hf][:].rearrange("p h i f -> p h (i f)"), ACT.Abs_reciprocal_sqrt, bias=8.1, scale=4.5
+            )
+            rT[hf] = r
+
+        zT = [one_ps.tile([P, H], F32, name="zT%d" % h) for h in range(VH)]
+
+        def product(t, n, dst, h=None):
+            lo, width = (0, V) if h is None else (h * P, P)
+            base = (t % 2) * V + lo
+            nc.vector.tensor_tensor(
+                dst[:, lo : lo + width],
+                win[("a", t)][:].indirect(pos_t[n][:, lo // 16 : (lo + width) // 16]),
+                coef[t // 2][n][:, base : base + width],
+                ALU.mult,
+            )
+
+        def z_sum(t, m, h):
+            add_transposed(zT[h][:, t * P : (t + 1) * P], [x[:, h * P : (h + 1) * P] for x in m])
+
+        def scale(hf, h):
+            cols = slice(hf * HALF, (hf + 1) * HALF)
+            nc.vector.tensor_tensor(rrT[h][:, cols], zT[h][:, cols], rT[hf][:, h, :], ALU.mult)
+
+        def m_tiles(t):
+            return [sb("m_%d_%d" % (t, n), [P, V], F32)[:] for n in range(3)]
+
+        nc.vector.tensor_copy(xg[0][:], xw[0][:].bitcast(U32).indirect(offs_t[:]))
+        nc.vector.tensor_copy(xsg[:], xs[:].indirect(offs_t[:]))
+        cast_w("e", 0, 0, 0, HALF, nc.scalar.copy)
+        quant_mm("e", 0, 0)
+        nc.vector.tensor_copy(xg[1][:], xw[1][:].bitcast(U32).indirect(offs_t[:]))
+        cast_w("e", 0, 1, 0, P, nc.vector.tensor_copy)
+        cast_w("e", 0, 1, P, P, nc.scalar.copy)
+        for i in range(2):
+            quant_w("e", 0, 1, i * P, P)
+            mm_pass("e", i, 1)
+        w2_grp = sb("w2_grp", [P, PACK * N], BF16)
+        cast(w2_grp[:], w2_raw[:], nc.scalar.copy)
+        w2_codes, w2_scales = quant("w2", w2_grp[:], N)
+        evac("e", 0, nc.vector.tensor_copy)
+        evac("e", 1, nc.scalar.copy)
+
+        for g in range(PASSES):
+            cast_w("e", 1, g, 0, HALF, nc.scalar.copy)
+        cast_w("a", 0, 0, 0, HALF, nc.scalar.copy)
+        e_side(0, ("e", 1))
+        evac("e", 2, nc.scalar.copy)
+        evac("e", 3, nc.scalar.copy)
+        cast_w("a", 0, 1, 0, HALF, nc.scalar.copy)
+        cast_w("a", 1, 0, 0, HALF, nc.scalar.copy)
+        e_side(1, ("a", 0))
+        squares(0)
+        evac("a", 0, nc.scalar.copy)
+        evac("a", 1, nc.scalar.copy)
+        cast_w("a", 1, 1, 0, HALF, nc.scalar.copy)
+        rsqrt(0)
+
+        m = m_tiles(0)
+        m[1] = stage[("a", 1, 0, 0)][:, V : 2 * V]
+        product(0, 0, m[0])
+        quant_mm("a", 1, 0)
+        product(0, 1, m[1])
+        product(0, 2, m[2])
+        m1 = m_tiles(1)
+        m1[0] = stage[("a", 1, 1, 0)][:, V : 2 * V]
+        quant_mm("a", 1, 1)
+        for h in range(VH):
+            z_sum(0, m, h)
+        squares(1)
+        evac("a", 2, nc.scalar.copy)
+        evac("a", 3, nc.scalar.copy)
+        rsqrt(1)
+        for n in range(3):
+            product(1, n, m1[n])
+        for h in range(VH):
+            z_sum(1, m1, h)
+
+        rrT = [coef[1][n][:, 0:V].bitcast(BF16) for n in (0, 2)]
+        m = m_tiles(2)
+        product(2, 0, m[0])
+        scale(0, 0)
+        product(2, 1, m[1])
+        product(2, 2, m[2])
+        scale(0, 1)
+        for h in range(VH):
+            z_sum(2, m, h)
+        m = m_tiles(3)
+        for h in range(VH):
+            for n in range(3):
+                product(3, n, m[n], h)
+            z_sum(3, m, h)
+
+        for h in range(VH):
+            scale(1, h)
+            words = rrT[h].bitcast(F32)
+            back = one_ps.tile([P, 2, P], F32, name="back%d" % h)
+            for u in range(2):
+                nc.tensor.transpose(back[:, u, :], words[:, u : H // 2 : 2], ident[:])
+            rr = sb("rr%d" % h, [P, P * PACK], BF16)
+            nc.scalar.copy(rr[:].bitcast(F32).rearrange("p (v u) -> p v u", u=2), back[:].rearrange("p u v -> p v u"))
+            rr_codes, rr_scales = quant("rr%d" % h, rr[:], P)
+            res = mm_ps.tile([P, P], F32, name="acc")
+            nc.tensor.matmul_mx(
+                out=res[:],
+                lhsT=w2_codes[:].bitcast(FP8X4),
+                lhsT_scale=w2_scales[:],
+                rhs=rr_codes[:].bitcast(FP8X4),
+                rhs_scale=rr_scales[:],
+                start=True,
+                stop=True,
+            )
+            res_sb = sb("res_sb%d" % h, [P, P], F32)
+            nc.scalar.copy(res_sb[:], res[:])
+            nc.sync.dma_start(out[:, h * P : (h + 1) * P], res_sb[:])

@@ -45,35 +45,35 @@ def tile_picked_ycovn_corr_p_kernel(
 
         raw = {}
 
-        def load_w(name, w, hf, g):
-            t = sb("raw_%s_%d_%d" % (name, hf, g), [P, PACK * HALF], F32)
-            rows = w[g * K_PASS : (g + 1) * K_PASS, hf * HALF : (hf + 1) * HALF]
+        def load_w(name, w, lo, width, g):
+            t = sb("raw_%s_%d_%d" % (name, lo, g), [P, PACK * width], F32)
+            rows = w[g * K_PASS : (g + 1) * K_PASS, lo : lo + width]
             nc.sync.dma_start(
                 t[:].rearrange("p (j c) -> p j c", j=PACK), rows.rearrange("(p j) c -> p j c", j=PACK)
             )
-            raw[(name, hf, g)] = t
-
-        def load_x(g):
-            nc.sync.dma_start(xw[g][:], x_words[g].rearrange("p n t -> p (n t)").bitcast(I32))
+            view = t[:].rearrange("p (j c) -> p j c", j=PACK)
+            for c in range(0, width, P):
+                raw[(name, (lo + c) // P, g)] = (t, view[:, :, c:])
 
         nc.gpsimd.memset(xs[:].bitcast(I32), 0)
         nc.sync.dma_start(offs_t[:], offs)
-        load_x(0)
         for q in range(4):
-            nc.scalar.dma_start(
+            nc.sync.dma_start(
                 xs[32 * q : 32 * q + 4 * PASSES, :].bitcast(I32),
                 x_scales[:, 4 * q : 4 * q + 4, :].bitcast(I32),
             )
-        load_w("e", w3, 0, 0)
-        load_x(1)
-        load_w("e", w3, 0, 1)
-        w2_raw = sb("w2_raw", [P, PACK, N], F32)
-        nc.sync.dma_start(w2_raw[:], w2.rearrange("(p j) c -> p j c", j=PACK))
-        for t, src in zip(pos_t, (pos1, pos2, pos3)):
-            nc.sync.dma_start(t[:], src)
+        for g in range(PASSES):
+            nc.sync.dma_start(xw[g][:], x_words[g].rearrange("p n t -> p (n t)").bitcast(I32))
+        for t in range(2):
+            for g in range(PASSES):
+                load_w("e", w3, t * P, P, g)
+            if t == 0:
+                for tile, src in zip(pos_t, (pos1, pos2, pos3)):
+                    nc.sync.dma_start(tile[:], src)
+        load_w("o", w2, 0, N, 0)
         for name, w, hf in (("e", w3, 1), ("a", w1, 0), ("a", w1, 1)):
             for g in range(PASSES):
-                load_w(name, w, hf, g)
+                load_w(name, w, hf * HALF, HALF, g)
 
         warm = sb("warm", [P, 2], F32)
         nc.vector.memset(warm[:, 0:1], 1.0)
@@ -85,12 +85,6 @@ def tile_picked_ycovn_corr_p_kernel(
         xg = [sb("xg%d" % g, [P, S], U32) for g in range(PASSES)]
         xsg = sb("xsg", [P, S], U8)
 
-        def cast(dst, src, copy):
-            copy(
-                dst.rearrange("p (c i j) -> p c j i", i=4, j=PACK),
-                src.rearrange("p j (c i) -> p c j i", i=4),
-            )
-
         def quant(name, grp, width):
             codes = sb("codes_" + name, [P, width], U32)
             scales = sb("scales_" + name, [P, width], U8)
@@ -100,45 +94,44 @@ def tile_picked_ycovn_corr_p_kernel(
         wq = {}
         stage = {}
 
-        def cast_w(name, hf, g, lo, width, copy):
-            st = sb("stage_%s_%d_%d_%d" % (name, hf, g, lo), [P, V + 2 * width], F32)
-            src = raw[(name, hf, g)][:].rearrange("p (j c) -> p j c", j=PACK)
-            cast(st[:, V:].bitcast(BF16), src[:, :, lo : lo + width], copy)
-            stage[(name, hf, g, lo)] = st
-
-        def quant_w(name, hf, g, lo, width):
-            nm = "%s_%d_%d_%d" % (name, hf, g, lo)
-            codes, scales = quant(nm, stage[(name, hf, g, lo)][:, V:].bitcast(BF16), width)
-            for c in range(0, width, P):
-                wq[(name, 2 * hf + (lo + c) // P, g)] = (codes[:, c : c + P], scales[:, c : c + P])
+        def cast_w(name, t, g, tiles, st=None):
+            width = tiles * P
+            if st is None:
+                st = sb("stage_%s_%d_%d" % (name, t, g), [P, 2 * width], F32)[:]
+            nc.scalar.copy(
+                st.bitcast(BF16).rearrange("p (c i j) -> p c j i", i=2, j=PACK),
+                raw[(name, t, g)][1][:, :, 0:width].rearrange("p j (c i) -> p c j i", i=2),
+            )
+            stage[(name, t, g)] = (st, tiles)
 
         accs = {}
 
-        def mm_pass(name, t, g):
-            if g == 0:
-                accs[(name, t)] = mm_ps.tile([P, S], F32, name="acc")
-            codes, scales = wq[(name, t, g)]
-            nc.tensor.matmul_mx(
-                out=accs[(name, t)][:],
-                lhsT=codes.bitcast(FP8X4),
-                lhsT_scale=scales,
-                rhs=xg[g][:].bitcast(FP8X4),
-                rhs_scale=xsg[4 * g : P, :],
-                start=(g == 0),
-                stop=(g == PASSES - 1),
-            )
+        def quant_w(name, t, g):
+            st, tiles = stage[(name, t, g)]
+            codes, scales = quant("%s_%d_%d" % (name, t, g), st.bitcast(BF16), tiles * P)
+            return [(codes[:, i * P : (i + 1) * P], scales[:, i * P : (i + 1) * P]) for i in range(tiles)]
+
+        def quant_mm(name, t0, g):
+            for i, (codes, scales) in enumerate(quant_w(name, t0, g)):
+                t = t0 + i
+                if g == 0:
+                    accs[(name, t)] = mm_ps.tile([P, S], F32, name="acc")
+                nc.tensor.matmul_mx(
+                    out=accs[(name, t)][:],
+                    lhsT=codes.bitcast(FP8X4),
+                    lhsT_scale=scales,
+                    rhs=xg[g][:].bitcast(FP8X4),
+                    rhs_scale=xsg[4 * g : P, :],
+                    start=(g == 0),
+                    stop=(g == PASSES - 1),
+                )
 
         win = {}
 
-        def evac(name, t, copy):
+        def evac(name, t, copy=nc.scalar.copy):
             w = sb("win_%s_%d" % (name, t), [P, S], F32)
             copy(w[:], accs[(name, t)][:])
             win[(name, t)] = w
-
-        def quant_mm(name, hf, g):
-            quant_w(name, hf, g, 0, HALF)
-            for i in range(2):
-                mm_pass(name, 2 * hf + i, g)
 
         def add_transposed(dst, srcs):
             for i, s in enumerate(srcs):
@@ -146,37 +139,26 @@ def tile_picked_ycovn_corr_p_kernel(
                     dst, lhsT=s, rhs=ident[:], is_transpose=True, start=(i == 0), stop=(i == len(srcs) - 1)
                 )
 
-        coef = {}
-        diff2 = {}
-        rT = {}
+        e0 = [sb("e0_%d" % t, [P, V], F32)[:] for t in range(TILES)]
 
-        def e_side(hf, nxt):
-            e0 = [sb("e0_%d" % hf, [P, V], F32)[:], stage[nxt + (0, 0)][:, V : 2 * V]]
-            d1 = sb("d1_%d" % hf, [P, 2 * V], F32)[:]
-            d2 = stage[nxt + (1, 0)][:, 0 : 2 * V]
-            for i in range(2):
-                w = win[("e", 2 * hf + i)]
-                cols = slice(i * V, (i + 1) * V)
-                if i == 1:
-                    quant_mm(nxt[0], nxt[1], 0)
-                nc.vector.tensor_copy(e0[i], w[:].indirect(pos_t[0][:]))
-                nc.vector.tensor_tensor(d1[:, cols], w[:].indirect(pos_t[1][:]), e0[i], ALU.subtract)
-                if i == 1:
-                    quant_mm(nxt[0], nxt[1], 1)
-                nc.vector.tensor_tensor(d2[:, cols], w[:].indirect(pos_t[2][:]), e0[i], ALU.subtract)
-            c = [sb("c%d_%d" % (n, hf), [P, 2 * V], F32) for n in range(3)]
-            nc.vector.scalar_tensor_tensor(c[1][:], d1, 2.0, d2, ALU.mult, ALU.subtract)
-            nc.vector.scalar_tensor_tensor(c[0][:], d1, -1.0, d2, ALU.mult, ALU.subtract)
-            nc.vector.scalar_tensor_tensor(c[2][:], d2, 2.0, d1, ALU.mult, ALU.subtract)
-            coef[hf] = c
-            diff2[hf] = d2
+        def pick(t):
+            nc.vector.tensor_copy(e0[t], win[("e", t)][:].indirect(pos_t[0][:]))
+
+        def diff(t, n, dst):
+            nc.vector.tensor_tensor(dst, win[("e", t)][:].indirect(pos_t[n][:]), e0[t], ALU.subtract)
+
+        def centre(c0, c1, c2, d1, d2):
+            nc.vector.scalar_tensor_tensor(c1, d1, 2.0, d2, ALU.mult, ALU.subtract)
+            nc.vector.scalar_tensor_tensor(c0, d1, -1.0, d2, ALU.mult, ALU.subtract)
+            nc.vector.scalar_tensor_tensor(c2, d2, 2.0, d1, ALU.mult, ALU.subtract)
 
         vT = {}
+        rT = {}
 
-        def squares(hf):
-            sq = raw[("a", 1, hf)]
-            nc.scalar.activation(sq[:, 0 : 2 * V], diff2[hf], ACT.Square, scale=math.sqrt(3.0))
-            nc.scalar.activation(sq[:, 2 * V : 4 * V], coef[hf][1][:], ACT.Square)
+        def squares(hf, d2, c1):
+            sq = raw[("a", 2, hf)][0]
+            nc.scalar.activation(sq[:, 0 : 2 * V], d2, ACT.Square, scale=math.sqrt(3.0))
+            nc.scalar.activation(sq[:, 2 * V : 4 * V], c1, ACT.Square)
             vT[hf] = one_ps.tile([P, VH, 2, P], F32, name="vT")
             for h in range(VH):
                 for i in range(2):
@@ -194,11 +176,10 @@ def tile_picked_ycovn_corr_p_kernel(
 
         def product(t, n, dst, h=None):
             lo, width = (0, V) if h is None else (h * P, P)
-            base = (t % 2) * V + lo
             nc.vector.tensor_tensor(
                 dst[:, lo : lo + width],
                 win[("a", t)][:].indirect(pos_t[n][:, lo // 16 : (lo + width) // 16]),
-                coef[t // 2][n][:, base : base + width],
+                coef[(n, t)][:, lo : lo + width],
                 ALU.mult,
             )
 
@@ -212,58 +193,100 @@ def tile_picked_ycovn_corr_p_kernel(
         def m_tiles(t):
             return [sb("m_%d_%d" % (t, n), [P, V], F32)[:] for n in range(3)]
 
-        nc.vector.tensor_copy(xg[0][:], xw[0][:].bitcast(U32).indirect(offs_t[:]))
-        nc.vector.tensor_copy(xsg[:], xs[:].indirect(offs_t[:]))
-        cast_w("e", 0, 0, 0, HALF, nc.scalar.copy)
-        quant_mm("e", 0, 0)
-        nc.vector.tensor_copy(xg[1][:], xw[1][:].bitcast(U32).indirect(offs_t[:]))
-        cast_w("e", 0, 1, 0, P, nc.vector.tensor_copy)
-        cast_w("e", 0, 1, P, P, nc.scalar.copy)
-        for i in range(2):
-            quant_w("e", 0, 1, i * P, P)
-            mm_pass("e", i, 1)
-        w2_grp = sb("w2_grp", [P, PACK * N], BF16)
-        cast(w2_grp[:], w2_raw[:], nc.scalar.copy)
-        w2_codes, w2_scales = quant("w2", w2_grp[:], N)
-        evac("e", 0, nc.vector.tensor_copy)
-        evac("e", 1, nc.scalar.copy)
+        ar_a = sb("ar_a", [P, 4 * V], F32)
+        ar_b = sb("ar_b", [P, 2 * V], F32)
+        ar_c = [sb("ar_c%d" % hf, [P, 6 * V], F32) for hf in range(2)]
+        d1_hi = sb("d1_hi", [P, 2 * V], F32)
 
+        def at(tile, lo, n=1):
+            return tile[:, lo * V : (lo + n) * V]
+
+        coef = {}
+        for (n, t), slot in zip(((1, 0), (1, 1), (0, 1), (0, 0), (2, 0), (2, 1)), range(6)):
+            coef[(n, t)] = at(ar_c[0], slot)
+        for (n, t), slot in zip(((1, 2), (1, 3), (0, 2), (0, 3), (2, 2), (2, 3)), range(6)):
+            coef[(n, t)] = at(ar_c[1], slot)
+        mid = slice(3 * V // 2, 5 * V // 2)
+
+        nc.vector.tensor_copy(xsg[:], xs[:].indirect(offs_t[:]))
         for g in range(PASSES):
-            cast_w("e", 1, g, 0, HALF, nc.scalar.copy)
-        cast_w("a", 0, 0, 0, HALF, nc.scalar.copy)
-        e_side(0, ("e", 1))
-        evac("e", 2, nc.scalar.copy)
-        evac("e", 3, nc.scalar.copy)
-        cast_w("a", 0, 1, 0, HALF, nc.scalar.copy)
-        cast_w("a", 1, 0, 0, HALF, nc.scalar.copy)
-        e_side(1, ("a", 0))
-        squares(0)
-        evac("a", 0, nc.scalar.copy)
-        evac("a", 1, nc.scalar.copy)
-        cast_w("a", 1, 1, 0, HALF, nc.scalar.copy)
+            nc.vector.tensor_copy(xg[g][:], xw[g][:].bitcast(U32).indirect(offs_t[:]))
+        for g in range(PASSES):
+            cast_w("e", 0, g, 1)
+            quant_mm("e", 0, g)
+        cast_w("e", 1, 0, 1, at(ar_a, 0))
+        evac("e", 0, nc.vector.tensor_copy)
+        cast_w("e", 1, 1, 1, at(ar_b, 0))
+        cast_w("o", 0, 0, 1)
+
+        quant_mm("e", 1, 0)
+        pick(0)
+        diff(0, 1, at(ar_a, 0))
+        quant_mm("e", 1, 1)
+        evac("e", 1)
+        diff(0, 2, at(ar_b, 0))
+        w2_codes, w2_scales = quant_w("o", 0, 0)[0]
+        centre(coef[(0, 0)], coef[(1, 0)], coef[(2, 0)], at(ar_a, 0), at(ar_b, 0))
+
+        cast_w("e", 2, 0, 2, at(ar_a, 1, 2))
+        cast_w("e", 2, 1, 1, at(ar_b, 1))
+        cast_w("e", 3, 1, 1, ar_c[0][:, mid])
+        pick(1)
+        quant_mm("e", 2, 0)
+        diff(1, 1, at(ar_a, 1))
+        quant_mm("e", 2, 1)
+        evac("e", 2)
+        diff(1, 2, at(ar_b, 1))
+        quant_mm("e", 3, 1)
+        evac("e", 3)
+        centre(coef[(0, 1)], coef[(1, 1)], coef[(2, 1)], at(ar_a, 1), at(ar_b, 1))
+
+        cast_w("a", 0, 0, 2, at(ar_a, 1, 2))
+        cast_w("a", 0, 1, 1, at(ar_a, 3))
+        cast_w("a", 1, 1, 1, ar_c[1][:, mid])
+        cast_w("a", 2, 0, 2)
+        pick(2)
+        pick(3)
+        diff(2, 1, at(d1_hi, 0))
+        quant_mm("a", 0, 0)
+        diff(2, 2, at(ar_a, 2))
+        diff(3, 1, at(d1_hi, 1))
+        quant_mm("a", 0, 1)
+        evac("a", 0)
+        diff(3, 2, at(ar_a, 3))
+        quant_mm("a", 1, 1)
+        evac("a", 1)
+        centre(at(ar_c[1], 2, 2), at(ar_c[1], 0, 2), at(ar_c[1], 4, 2), d1_hi[:], at(ar_a, 2, 2))
+
+        squares(0, ar_b[:], at(ar_c[0], 0, 2))
+        cast_w("a", 2, 1, 1)
+        cast_w("a", 3, 1, 1)
         rsqrt(0)
 
         m = m_tiles(0)
-        m[1] = stage[("a", 1, 0, 0)][:, V : 2 * V]
+        m[1] = stage[("a", 2, 0)][0][:, 0:V]
         product(0, 0, m[0])
-        quant_mm("a", 1, 0)
+        quant_mm("a", 2, 0)
         product(0, 1, m[1])
         product(0, 2, m[2])
-        m1 = m_tiles(1)
-        m1[0] = stage[("a", 1, 1, 0)][:, V : 2 * V]
-        quant_mm("a", 1, 1)
+        quant_mm("a", 2, 1)
+        evac("a", 2)
         for h in range(VH):
             z_sum(0, m, h)
-        squares(1)
-        evac("a", 2, nc.scalar.copy)
-        evac("a", 3, nc.scalar.copy)
+        m = m_tiles(1)
+        m[0] = stage[("a", 2, 1)][0]
+        m[1] = stage[("a", 3, 1)][0]
+        product(1, 0, m[0])
+        quant_mm("a", 3, 1)
+        squares(1, at(ar_a, 2, 2), at(ar_c[1], 0, 2))
+        evac("a", 3)
         rsqrt(1)
-        for n in range(3):
-            product(1, n, m1[n])
+        product(1, 1, m[1])
+        product(1, 2, m[2])
         for h in range(VH):
-            z_sum(1, m1, h)
+            z_sum(1, m, h)
 
-        rrT = [coef[1][n][:, 0:V].bitcast(BF16) for n in (0, 2)]
+        rrT = [coef[(n, 2)].bitcast(BF16) for n in (0, 2)]
         m = m_tiles(2)
         product(2, 0, m[0])
         scale(0, 0)
@@ -290,8 +313,8 @@ def tile_picked_ycovn_corr_p_kernel(
             res = mm_ps.tile([P, P], F32, name="acc")
             nc.tensor.matmul_mx(
                 out=res[:],
-                lhsT=w2_codes[:].bitcast(FP8X4),
-                lhsT_scale=w2_scales[:],
+                lhsT=w2_codes.bitcast(FP8X4),
+                lhsT_scale=w2_scales,
                 rhs=rr_codes[:].bitcast(FP8X4),
                 rhs_scale=rr_scales[:],
                 start=True,

@@ -32,7 +32,7 @@ def tile_picked_ycovn_corr_p_kernel(
     nc = tc.nc
     with ExitStack() as ctx:
         keep = ctx.enter_context(tc.tile_pool(name="keep", bufs=1))
-        mm_ps = ctx.enter_context(tc.psum_pool(name="mm_ps", bufs=3))
+        mm_ps = ctx.enter_context(tc.psum_pool(name="mm_ps", bufs=4))
         one_ps = ctx.enter_context(tc.psum_pool(name="one_ps", bufs=1))
 
         def sb(name, shape, dtype):
@@ -57,19 +57,23 @@ def tile_picked_ycovn_corr_p_kernel(
 
         nc.gpsimd.memset(xs[:].bitcast(I32), 0)
         nc.sync.dma_start(offs_t[:], offs)
+
+        def load_x(g):
+            nc.sync.dma_start(xw[g][:], x_words[g].rearrange("p n t -> p (n t)").bitcast(I32))
+
         for q in range(4):
             nc.sync.dma_start(
                 xs[32 * q : 32 * q + 4 * PASSES, :].bitcast(I32),
                 x_scales[:, 4 * q : 4 * q + 4, :].bitcast(I32),
             )
+        load_x(0)
+        load_w("e", w3, 0, P, 0)
+        load_x(1)
+        load_w("e", w3, 0, P, 1)
+        for tile, src in zip(pos_t, (pos1, pos2, pos3)):
+            nc.sync.dma_start(tile[:], src)
         for g in range(PASSES):
-            nc.sync.dma_start(xw[g][:], x_words[g].rearrange("p n t -> p (n t)").bitcast(I32))
-        for t in range(2):
-            for g in range(PASSES):
-                load_w("e", w3, t * P, P, g)
-            if t == 0:
-                for tile, src in zip(pos_t, (pos1, pos2, pos3)):
-                    nc.sync.dma_start(tile[:], src)
+            load_w("e", w3, P, P, g)
         load_w("o", w2, 0, N, 0)
         for name, w, hf in (("e", w3, 1), ("a", w1, 0), ("a", w1, 1)):
             for g in range(PASSES):
@@ -83,6 +87,7 @@ def tile_picked_ycovn_corr_p_kernel(
         make_identity(nc, ident[:])
 
         xg = [sb("xg%d" % g, [P, S], U32) for g in range(PASSES)]
+        SH = S // 2
         xsg = sb("xsg", [P, S], U8)
 
         def quant(name, grp, width):
@@ -152,27 +157,22 @@ def tile_picked_ycovn_corr_p_kernel(
             nc.vector.scalar_tensor_tensor(c0, d1, -1.0, d2, ALU.mult, ALU.subtract)
             nc.vector.scalar_tensor_tensor(c2, d2, 2.0, d1, ALU.mult, ALU.subtract)
 
-        vT = {}
         rT = {}
+        zT = [one_ps.tile([P, H], F32, name="zT%d" % h) for h in range(VH)]
+        spare = [one_ps.tile([P, SH], F32, name="spare%d" % h) for h in range(2)]
 
-        def squares(hf, d2, c1):
-            sq = raw[("a", 2, hf)][0]
+        def squares(hf, d2, c1, place):
+            sq = raw[("a", 2, 1 - hf)][0]
             nc.scalar.activation(sq[:, 0 : 2 * V], d2, ACT.Square, scale=math.sqrt(3.0))
             nc.scalar.activation(sq[:, 2 * V : 4 * V], c1, ACT.Square)
-            vT[hf] = one_ps.tile([P, VH, 2, P], F32, name="vT")
             for h in range(VH):
                 for i in range(2):
-                    lo = i * V + h * P
-                    add_transposed(vT[hf][:, h, i, :], [sq[:, o + lo : o + lo + P] for o in (0, 2 * V)])
+                    lo = place[i] * V + h * P
+                    add_transposed(zT[h][:, (2 * hf + i) * P : (2 * hf + i + 1) * P], [sq[:, o + lo : o + lo + P] for o in (0, 2 * V)])
 
-        def rsqrt(hf):
-            r = sb("rT_%d" % hf, [P, VH, 2 * P], F32)
-            nc.scalar.activation(
-                r[:], vT[hf][:].rearrange("p h i f -> p h (i f)"), ACT.Abs_reciprocal_sqrt, bias=8.1, scale=4.5
-            )
-            rT[hf] = r
-
-        zT = [one_ps.tile([P, H], F32, name="zT%d" % h) for h in range(VH)]
+        def rsqrt(h):
+            rT[h] = sb("rT_%d" % h, [P, H], F32)
+            nc.scalar.activation(rT[h][:], zT[h][:], ACT.Abs_reciprocal_sqrt, bias=8.1, scale=4.5)
 
         def product(t, n, dst, h=None):
             lo, width = (0, V) if h is None else (h * P, P)
@@ -188,114 +188,124 @@ def tile_picked_ycovn_corr_p_kernel(
 
         def scale(hf, h):
             cols = slice(hf * HALF, (hf + 1) * HALF)
-            nc.vector.tensor_tensor(rrT[h][:, cols], zT[h][:, cols], rT[hf][:, h, :], ALU.mult)
+            nc.vector.tensor_tensor(rrT[h][:, cols], zT[h][:, cols], rT[h][:, cols], ALU.mult)
 
         def m_tiles(t):
             return [sb("m_%d_%d" % (t, n), [P, V], F32)[:] for n in range(3)]
 
-        ar_a = sb("ar_a", [P, 4 * V], F32)
-        ar_b = sb("ar_b", [P, 2 * V], F32)
+        d_lo = [sb("d%d_lo" % n, [P, 3 * V], F32) for n in (1, 2)]
+        d_hi = [sb("d%d_hi" % n, [P, 3 * V], F32) for n in (1, 2)]
         ar_c = [sb("ar_c%d" % hf, [P, 6 * V], F32) for hf in range(2)]
-        d1_hi = sb("d1_hi", [P, 2 * V], F32)
 
         def at(tile, lo, n=1):
             return tile[:, lo * V : (lo + n) * V]
 
         coef = {}
-        for (n, t), slot in zip(((1, 0), (1, 1), (0, 1), (0, 0), (2, 0), (2, 1)), range(6)):
+        for (n, t), slot in zip(((1, 1), (1, 0), (0, 0), (0, 1), (2, 0), (2, 1)), range(6)):
             coef[(n, t)] = at(ar_c[0], slot)
         for (n, t), slot in zip(((1, 2), (1, 3), (0, 2), (0, 3), (2, 2), (2, 3)), range(6)):
             coef[(n, t)] = at(ar_c[1], slot)
-        mid = slice(3 * V // 2, 5 * V // 2)
+
+        def gather_x(g, lo, width):
+            nc.vector.tensor_copy(
+                xg[g][:, lo : lo + width], xw[g][:].bitcast(U32).indirect(offs_t[:, lo // 16 : (lo + width) // 16])
+            )
+
+        first = spare
+
+        def first_mm(g, h, codes, scales):
+            cols = slice(h * SH, (h + 1) * SH)
+            nc.tensor.matmul_mx(
+                out=first[h][:],
+                lhsT=codes.bitcast(FP8X4),
+                lhsT_scale=scales,
+                rhs=xg[g][:, cols].bitcast(FP8X4),
+                rhs_scale=xsg[4 * g : P, cols],
+                start=(g == 0),
+                stop=(g == PASSES - 1),
+            )
 
         nc.vector.tensor_copy(xsg[:], xs[:].indirect(offs_t[:]))
-        for g in range(PASSES):
-            nc.vector.tensor_copy(xg[g][:], xw[g][:].bitcast(U32).indirect(offs_t[:]))
-        for g in range(PASSES):
-            cast_w("e", 0, g, 1)
-            quant_mm("e", 0, g)
-        cast_w("e", 1, 0, 1, at(ar_a, 0))
-        evac("e", 0, nc.vector.tensor_copy)
-        cast_w("e", 1, 1, 1, at(ar_b, 0))
+        gather_x(0, 0, S)
+        cast_w("e", 0, 0, 1)
+        cast_w("e", 0, 1, 1)
+        ops = quant_w("e", 0, 0)[0]
+        for h in range(2):
+            first_mm(0, h, *ops)
+        gather_x(1, 0, SH)
+        ops = quant_w("e", 0, 1)[0]
+        first_mm(1, 0, *ops)
+        gather_x(1, SH, SH)
+        first_mm(1, 1, *ops)
+        win[("e", 0)] = sb("win_e_0", [P, S], F32)
+        for h in range(2):
+            nc.vector.tensor_copy(win[("e", 0)][:, h * SH : (h + 1) * SH], first[h][:])
+        cast_w("e", 1, 0, 1, at(d_lo[0], 0))
+        cast_w("e", 1, 1, 1, at(d_lo[1], 2))
         cast_w("o", 0, 0, 1)
 
-        quant_mm("e", 1, 0)
         pick(0)
-        diff(0, 1, at(ar_a, 0))
+        quant_mm("e", 1, 0)
+        diff(0, 1, at(d_lo[0], 0))
         quant_mm("e", 1, 1)
         evac("e", 1)
-        diff(0, 2, at(ar_b, 0))
-        w2_codes, w2_scales = quant_w("o", 0, 0)[0]
-        centre(coef[(0, 0)], coef[(1, 0)], coef[(2, 0)], at(ar_a, 0), at(ar_b, 0))
-
-        cast_w("e", 2, 0, 2, at(ar_a, 1, 2))
-        cast_w("e", 2, 1, 1, at(ar_b, 1))
-        cast_w("e", 3, 1, 1, ar_c[0][:, mid])
-        pick(1)
+        cast_w("e", 2, 0, 2, at(ar_c[0], 1, 2))
+        cast_w("e", 2, 1, 2, at(d_lo[0], 1, 2))
+        diff(0, 2, at(d_lo[1], 2))
         quant_mm("e", 2, 0)
-        diff(1, 1, at(ar_a, 1))
+        centre(coef[(0, 0)], coef[(1, 0)], coef[(2, 0)], at(d_lo[0], 0), at(d_lo[1], 2))
+
+        cast_w("a", 0, 0, 2, at(d_lo[1], 0, 2))
+        w2_codes, w2_scales = quant_w("o", 0, 0)[0]
+        pick(1)
         quant_mm("e", 2, 1)
         evac("e", 2)
-        diff(1, 2, at(ar_b, 1))
-        quant_mm("e", 3, 1)
         evac("e", 3)
-        centre(coef[(0, 1)], coef[(1, 1)], coef[(2, 1)], at(ar_a, 1), at(ar_b, 1))
-
-        cast_w("a", 0, 0, 2, at(ar_a, 1, 2))
-        cast_w("a", 0, 1, 1, at(ar_a, 3))
-        cast_w("a", 1, 1, 1, ar_c[1][:, mid])
-        cast_w("a", 2, 0, 2)
-        pick(2)
-        pick(3)
-        diff(2, 1, at(d1_hi, 0))
+        diff(1, 1, at(d_lo[0], 1))
         quant_mm("a", 0, 0)
-        diff(2, 2, at(ar_a, 2))
-        diff(3, 1, at(d1_hi, 1))
+        diff(1, 2, at(d_lo[1], 1))
+        cast_w("a", 0, 1, 2)
+        e0[3] = stage[("a", 0, 1)][0][:, 0:V]
+        cast_w("a", 2, 0, 2, at(d_hi[1], 0, 2))
+        pick(2)
+        centre(coef[(0, 1)], coef[(1, 1)], coef[(2, 1)], at(d_lo[0], 1), at(d_lo[1], 1))
         quant_mm("a", 0, 1)
         evac("a", 0)
-        diff(3, 2, at(ar_a, 3))
-        quant_mm("a", 1, 1)
         evac("a", 1)
-        centre(at(ar_c[1], 2, 2), at(ar_c[1], 0, 2), at(ar_c[1], 4, 2), d1_hi[:], at(ar_a, 2, 2))
-
-        squares(0, ar_b[:], at(ar_c[0], 0, 2))
-        cast_w("a", 2, 1, 1)
-        cast_w("a", 3, 1, 1)
-        rsqrt(0)
-
-        m = m_tiles(0)
-        m[1] = stage[("a", 2, 0)][0][:, 0:V]
-        product(0, 0, m[0])
+        cast_w("a", 2, 1, 2, at(ar_c[1], 1, 2))
+        pick(3)
+        diff(2, 1, at(d_hi[0], 0))
+        diff(3, 1, at(d_hi[0], 1))
         quant_mm("a", 2, 0)
-        product(0, 1, m[1])
-        product(0, 2, m[2])
+        diff(2, 2, at(d_hi[1], 0))
+        diff(3, 2, at(d_hi[1], 1))
         quant_mm("a", 2, 1)
+        squares(0, at(d_lo[1], 1, 2), at(ar_c[0], 0, 2), (1, 0))
         evac("a", 2)
-        for h in range(VH):
-            z_sum(0, m, h)
-        m = m_tiles(1)
-        m[0] = stage[("a", 2, 1)][0]
-        m[1] = stage[("a", 3, 1)][0]
-        product(1, 0, m[0])
-        quant_mm("a", 3, 1)
-        squares(1, at(ar_a, 2, 2), at(ar_c[1], 0, 2))
         evac("a", 3)
-        rsqrt(1)
-        product(1, 1, m[1])
-        product(1, 2, m[2])
-        for h in range(VH):
-            z_sum(1, m, h)
+        centre(at(ar_c[1], 2, 2), at(ar_c[1], 0, 2), at(ar_c[1], 4, 2), at(d_hi[0], 0, 2), at(d_hi[1], 0, 2))
 
-        rrT = [coef[(n, 2)].bitcast(BF16) for n in (0, 2)]
-        m = m_tiles(2)
+        squares(1, at(d_hi[1], 0, 2), at(ar_c[1], 0, 2), (0, 1))
+        rsqrt(0)
+        rsqrt(1)
+
+        for t in range(2):
+            m = m_tiles(t)
+            for n in range(3):
+                product(t, n, m[n])
+            for h in range(VH):
+                z_sum(t, m, h)
+
+        rrT = [sb("rrT%d" % h, [P, H], BF16)[:] for h in range(VH)]
+        m = [sb("m_2_0", [P, V], F32)[:], at(rT[0], 0), at(rT[1], 0)]
         product(2, 0, m[0])
         scale(0, 0)
         product(2, 1, m[1])
-        product(2, 2, m[2])
         scale(0, 1)
+        product(2, 2, m[2])
         for h in range(VH):
             z_sum(2, m, h)
-        m = m_tiles(3)
+        m = [coef[(2, 2)], at(win[("a", 2)], 0), at(win[("a", 2)], 1)]
         for h in range(VH):
             for n in range(3):
                 product(3, n, m[n], h)
@@ -304,11 +314,11 @@ def tile_picked_ycovn_corr_p_kernel(
         for h in range(VH):
             scale(1, h)
             words = rrT[h].bitcast(F32)
-            back = one_ps.tile([P, 2, P], F32, name="back%d" % h)
+            back = spare[h][:].rearrange("p (u v) -> p u v", u=2)
             for u in range(2):
                 nc.tensor.transpose(back[:, u, :], words[:, u : H // 2 : 2], ident[:])
             rr = sb("rr%d" % h, [P, P * PACK], BF16)
-            nc.scalar.copy(rr[:].bitcast(F32).rearrange("p (v u) -> p v u", u=2), back[:].rearrange("p u v -> p v u"))
+            nc.scalar.copy(rr[:].bitcast(F32).rearrange("p (v u) -> p v u", u=2), back.rearrange("p u v -> p v u"))
             rr_codes, rr_scales = quant("rr%d" % h, rr[:], P)
             res = mm_ps.tile([P, P], F32, name="acc")
             nc.tensor.matmul_mx(

@@ -24,6 +24,7 @@ PASSES = K // K_PASS
 HALF = H // 2
 TILES = H // P
 VH = V // P
+ORDER = (1, 2, 0)
 
 
 def tile_picked_ycovn_corr_p_kernel(
@@ -32,7 +33,7 @@ def tile_picked_ycovn_corr_p_kernel(
     nc = tc.nc
     with ExitStack() as ctx:
         keep = ctx.enter_context(tc.tile_pool(name="keep", bufs=1))
-        mm_ps = ctx.enter_context(tc.psum_pool(name="mm_ps", bufs=4))
+        mm_ps = ctx.enter_context(tc.psum_pool(name="mm_ps", bufs=3))
         one_ps = ctx.enter_context(tc.psum_pool(name="one_ps", bufs=1))
 
         def sb(name, shape, dtype):
@@ -74,10 +75,10 @@ def tile_picked_ycovn_corr_p_kernel(
             nc.sync.dma_start(tile[:], src)
         for g in range(PASSES):
             load_w("e", w3, P, P, g)
-        load_w("o", w2, 0, N, 0)
         for name, w, hf in (("e", w3, 1), ("a", w1, 0), ("a", w1, 1)):
             for g in range(PASSES):
                 load_w(name, w, hf * HALF, HALF, g)
+        load_w("o", w2, 0, N, 0)
 
         warm = sb("warm", [P, 2], F32)
         nc.vector.memset(warm[:, 0:1], 1.0)
@@ -152,27 +153,40 @@ def tile_picked_ycovn_corr_p_kernel(
         def diff(t, n, dst):
             nc.vector.tensor_tensor(dst, win[("e", t)][:].indirect(pos_t[n][:]), e0[t], ALU.subtract)
 
-        def centre(c0, c1, c2, d1, d2):
+        def sum_diffs(hf, d1, d2):
+            for i in range(2):
+                for h in range(VH):
+                    b = i * VH + h
+                    add_transposed(spare[0][:, b * P : (b + 1) * P], [d[i][:, h * P : (h + 1) * P] for d in (d1, d2)])
+            neg = sb("neg_%d" % hf, [P, 2 * V], F32)
+            nc.scalar.activation(neg[:], spare[0][:], ACT.Copy, scale=-1.0)
+            for b in range(2 * VH):
+                nc.tensor.transpose(spare[1][:, b * P : (b + 1) * P], neg[:, b * P : (b + 1) * P], ident[:])
+
+        def centre0(hf):
+            nc.scalar.copy(c0_t[hf][:], spare[1][:])
+
+        def centre(c1, c2, d1, d2):
             nc.vector.scalar_tensor_tensor(c1, d1, 2.0, d2, ALU.mult, ALU.subtract)
-            nc.vector.scalar_tensor_tensor(c0, d1, -1.0, d2, ALU.mult, ALU.subtract)
             nc.vector.scalar_tensor_tensor(c2, d2, 2.0, d1, ALU.mult, ALU.subtract)
 
-        rT = {}
         zT = [one_ps.tile([P, H], F32, name="zT%d" % h) for h in range(VH)]
-        spare = [one_ps.tile([P, SH], F32, name="spare%d" % h) for h in range(2)]
+        spare = [one_ps.tile([P, S], F32, name="spare%d" % h) for h in range(2)]
+        var_hi = one_ps.tile([P, 2 * V], F32, name="var_hi")
+        rT = [sb("rT_%d" % hf, [P, 2 * V], F32) for hf in range(2)]
 
         def squares(hf, d2, c1, place):
-            sq = raw[("a", 2, 1 - hf)][0]
+            sq = raw[("a", 2, hf)][0]
             nc.scalar.activation(sq[:, 0 : 2 * V], d2, ACT.Square, scale=math.sqrt(3.0))
             nc.scalar.activation(sq[:, 2 * V : 4 * V], c1, ACT.Square)
             for h in range(VH):
                 for i in range(2):
                     lo = place[i] * V + h * P
-                    add_transposed(zT[h][:, (2 * hf + i) * P : (2 * hf + i + 1) * P], [sq[:, o + lo : o + lo + P] for o in (0, 2 * V)])
+                    dst = zT[h][:, i * P : (i + 1) * P] if hf == 0 else var_hi[:, h * V + i * P : h * V + (i + 1) * P]
+                    add_transposed(dst, [sq[:, o + lo : o + lo + P] for o in (0, 2 * V)])
 
-        def rsqrt(h):
-            rT[h] = sb("rT_%d" % h, [P, H], F32)
-            nc.scalar.activation(rT[h][:], zT[h][:], ACT.Abs_reciprocal_sqrt, bias=8.1, scale=4.5)
+        def rsqrt(dst, src):
+            nc.scalar.activation(dst, src, ACT.Abs_reciprocal_sqrt, bias=8.1, scale=4.5)
 
         def product(t, n, dst, h=None):
             lo, width = (0, V) if h is None else (h * P, P)
@@ -184,39 +198,42 @@ def tile_picked_ycovn_corr_p_kernel(
             )
 
         def z_sum(t, m, h):
-            add_transposed(zT[h][:, t * P : (t + 1) * P], [x[:, h * P : (h + 1) * P] for x in m])
+            add_transposed(zT[h][:, t * P : (t + 1) * P], [m[n][:, h * P : (h + 1) * P] for n in ORDER])
 
         def scale(hf, h):
             cols = slice(hf * HALF, (hf + 1) * HALF)
-            nc.vector.tensor_tensor(rrT[h][:, cols], zT[h][:, cols], rT[h][:, cols], ALU.mult)
+            nc.vector.tensor_tensor(rrT[h][:, cols], zT[h][:, cols], at(rT[hf], h), ALU.mult)
 
         def m_tiles(t):
             return [sb("m_%d_%d" % (t, n), [P, V], F32)[:] for n in range(3)]
 
         d_lo = [sb("d%d_lo" % n, [P, 3 * V], F32) for n in (1, 2)]
         d_hi = [sb("d%d_hi" % n, [P, 3 * V], F32) for n in (1, 2)]
-        ar_c = [sb("ar_c%d" % hf, [P, 6 * V], F32) for hf in range(2)]
+        ar_c = [sb("ar_c%d" % hf, [P, 4 * V], F32) for hf in range(2)]
+        c0_t = [sb("c0_%d" % hf, [P, 2 * V], F32) for hf in range(2)]
 
         def at(tile, lo, n=1):
             return tile[:, lo * V : (lo + n) * V]
 
         coef = {}
-        for (n, t), slot in zip(((1, 1), (1, 0), (0, 0), (0, 1), (2, 0), (2, 1)), range(6)):
+        for (n, t), slot in zip(((1, 1), (1, 0), (2, 0), (2, 1)), range(4)):
             coef[(n, t)] = at(ar_c[0], slot)
-        for (n, t), slot in zip(((1, 2), (1, 3), (0, 2), (0, 3), (2, 2), (2, 3)), range(6)):
+        for (n, t), slot in zip(((1, 2), (1, 3), (2, 2), (2, 3)), range(4)):
             coef[(n, t)] = at(ar_c[1], slot)
+        for t in range(TILES):
+            coef[(0, t)] = at(c0_t[t // 2], t % 2)
 
         def gather_x(g, lo, width):
             nc.vector.tensor_copy(
                 xg[g][:, lo : lo + width], xw[g][:].bitcast(U32).indirect(offs_t[:, lo // 16 : (lo + width) // 16])
             )
 
-        first = spare
+        first = [spare[h][:, 0:SH] for h in range(2)]
 
         def first_mm(g, h, codes, scales):
             cols = slice(h * SH, (h + 1) * SH)
             nc.tensor.matmul_mx(
-                out=first[h][:],
+                out=first[h],
                 lhsT=codes.bitcast(FP8X4),
                 lhsT_scale=scales,
                 rhs=xg[g][:, cols].bitcast(FP8X4),
@@ -239,10 +256,9 @@ def tile_picked_ycovn_corr_p_kernel(
         first_mm(1, 1, *ops)
         win[("e", 0)] = sb("win_e_0", [P, S], F32)
         for h in range(2):
-            nc.vector.tensor_copy(win[("e", 0)][:, h * SH : (h + 1) * SH], first[h][:])
+            nc.vector.tensor_copy(win[("e", 0)][:, h * SH : (h + 1) * SH], first[h])
         cast_w("e", 1, 0, 1, at(d_lo[0], 0))
         cast_w("e", 1, 1, 1, at(d_lo[1], 2))
-        cast_w("o", 0, 0, 1)
 
         pick(0)
         quant_mm("e", 1, 0)
@@ -253,10 +269,9 @@ def tile_picked_ycovn_corr_p_kernel(
         cast_w("e", 2, 1, 2, at(d_lo[0], 1, 2))
         diff(0, 2, at(d_lo[1], 2))
         quant_mm("e", 2, 0)
-        centre(coef[(0, 0)], coef[(1, 0)], coef[(2, 0)], at(d_lo[0], 0), at(d_lo[1], 2))
+        centre(coef[(1, 0)], coef[(2, 0)], at(d_lo[0], 0), at(d_lo[1], 2))
 
         cast_w("a", 0, 0, 2, at(d_lo[1], 0, 2))
-        w2_codes, w2_scales = quant_w("o", 0, 0)[0]
         pick(1)
         quant_mm("e", 2, 1)
         evac("e", 2)
@@ -266,55 +281,65 @@ def tile_picked_ycovn_corr_p_kernel(
         diff(1, 2, at(d_lo[1], 1))
         cast_w("a", 0, 1, 2)
         e0[3] = stage[("a", 0, 1)][0][:, 0:V]
-        cast_w("a", 2, 0, 2, at(d_hi[1], 0, 2))
+        cast_w("a", 2, 0, 2, at(ar_c[1], 1, 2))
         pick(2)
-        centre(coef[(0, 1)], coef[(1, 1)], coef[(2, 1)], at(d_lo[0], 1), at(d_lo[1], 1))
+        centre(coef[(1, 1)], coef[(2, 1)], at(d_lo[0], 1), at(d_lo[1], 1))
         quant_mm("a", 0, 1)
         evac("a", 0)
         evac("a", 1)
-        cast_w("a", 2, 1, 2, at(ar_c[1], 1, 2))
+        sum_diffs(0, [at(d_lo[0], 0), at(d_lo[0], 1)], [at(d_lo[1], 2), at(d_lo[1], 1)])
+        squares(0, at(d_lo[1], 1, 2), at(ar_c[0], 0, 2), (1, 0))
+        centre0(0)
+        cast_w("a", 2, 1, 2)
+        for h in range(VH):
+            rsqrt(at(rT[0], h), zT[h][:, 0:HALF])
         pick(3)
         diff(2, 1, at(d_hi[0], 0))
         diff(3, 1, at(d_hi[0], 1))
-        quant_mm("a", 2, 0)
         diff(2, 2, at(d_hi[1], 0))
         diff(3, 2, at(d_hi[1], 1))
+        quant_mm("a", 2, 0)
+        centre(at(ar_c[1], 0, 2), at(ar_c[1], 2, 2), at(d_hi[0], 0, 2), at(d_hi[1], 0, 2))
+
+        m0 = m_tiles(0)
+        for n in ORDER:
+            product(0, n, m0[n])
         quant_mm("a", 2, 1)
-        squares(0, at(d_lo[1], 1, 2), at(ar_c[0], 0, 2), (1, 0))
+        sum_diffs(1, [at(d_hi[0], 0), at(d_hi[0], 1)], [at(d_hi[1], 0), at(d_hi[1], 1)])
         evac("a", 2)
+        centre0(1)
         evac("a", 3)
-        centre(at(ar_c[1], 2, 2), at(ar_c[1], 0, 2), at(ar_c[1], 4, 2), at(d_hi[0], 0, 2), at(d_hi[1], 0, 2))
-
         squares(1, at(d_hi[1], 0, 2), at(ar_c[1], 0, 2), (0, 1))
-        rsqrt(0)
-        rsqrt(1)
-
-        for t in range(2):
-            m = m_tiles(t)
-            for n in range(3):
-                product(t, n, m[n])
-            for h in range(VH):
-                z_sum(t, m, h)
+        rsqrt(rT[1][:], var_hi[:])
+        cast_w("o", 0, 0, 1)
+        w2_codes, w2_scales = quant_w("o", 0, 0)[0]
+        st = stage[("a", 2, 1)][0]
+        m1 = [sb("m_1_0", [P, V], F32)[:], st[:, 0:V], st[:, V : 2 * V]]
+        for n in ORDER:
+            product(1, n, m1[n])
+        for h in range(VH):
+            z_sum(0, m0, h)
+            z_sum(1, m1, h)
 
         rrT = [sb("rrT%d" % h, [P, H], BF16)[:] for h in range(VH)]
-        m = [sb("m_2_0", [P, V], F32)[:], at(rT[0], 0), at(rT[1], 0)]
-        product(2, 0, m[0])
-        scale(0, 0)
+        m = [rT[0][:, V // 2 : 3 * V // 2], sb("m_2_1", [P, V], F32)[:], sb("m_2_2", [P, V], F32)[:]]
         product(2, 1, m[1])
-        scale(0, 1)
         product(2, 2, m[2])
+        scale(0, 0)
+        scale(0, 1)
+        product(2, 0, m[0])
         for h in range(VH):
             z_sum(2, m, h)
-        m = [coef[(2, 2)], at(win[("a", 2)], 0), at(win[("a", 2)], 1)]
+        m = [coef[(0, 2)], at(win[("a", 2)], 0), at(win[("a", 2)], 1)]
         for h in range(VH):
-            for n in range(3):
+            for n in ORDER:
                 product(3, n, m[n], h)
             z_sum(3, m, h)
 
         for h in range(VH):
             scale(1, h)
             words = rrT[h].bitcast(F32)
-            back = spare[h][:].rearrange("p (u v) -> p u v", u=2)
+            back = spare[h][:, 0 : 2 * P].rearrange("p (u v) -> p u v", u=2)
             for u in range(2):
                 nc.tensor.transpose(back[:, u, :], words[:, u : H // 2 : 2], ident[:])
             rr = sb("rr%d" % h, [P, P * PACK], BF16)

@@ -21,64 +21,61 @@ P = 128
 PACK = 4
 K_PASS = P * PACK
 PASSES = K // K_PASS
-HALF = H // 2
 TILES = H // P
 VH = V // P
 ORDER = (1, 2, 0)
 
 
-def tile_picked_ycovn_corr_p_kernel(
-    tc, x_words, x_scales, w1, w3, w2, offs, pos1, pos2, pos3, out
-):
+def tile_picked_ycovn_corr_p_kernel(tc, x_words, x_scales, w1, w3, w2, offs, pos1, pos2, pos3, out):
     nc = tc.nc
     with ExitStack() as ctx:
         keep = ctx.enter_context(tc.tile_pool(name="keep", bufs=1))
-        mm_ps = ctx.enter_context(tc.psum_pool(name="mm_ps", bufs=3))
-        one_ps = ctx.enter_context(tc.psum_pool(name="one_ps", bufs=1))
+        psum = ctx.enter_context(tc.psum_pool(name="psum", bufs=1))
 
         def sb(name, shape, dtype):
             return keep.tile(shape, dtype, name=name, align_bytes=64)
+
+        def at(tile, lo, n=1):
+            return tile[:, lo * V : (lo + n) * V]
+
+        bank = [psum.tile([P, S], F32, name="bank%d" % i) for i in range(8)]
 
         offs_t = sb("offs_t", [P, S // 16], U16)
         pos_t = [sb("pos_t%d" % i, [P, V // 16], U16) for i in range(3)]
         xw = [sb("xw%d" % g, [P, T], I32) for g in range(PASSES)]
         xs = sb("xs", [P, T], U8)
-
         raw = {}
 
-        def load_w(name, w, lo, width, g):
-            t = sb("raw_%s_%d_%d" % (name, lo, g), [P, PACK * width], F32)
-            rows = w[g * K_PASS : (g + 1) * K_PASS, lo : lo + width]
+        def load_w(name, w, t, tiles, g):
+            width = tiles * P
+            tile = sb("raw_%s_%d_%d" % (name, t, g), [P, PACK * width], F32)
+            rows = w[g * K_PASS : (g + 1) * K_PASS, t * P : t * P + width]
             nc.sync.dma_start(
-                t[:].rearrange("p (j c) -> p j c", j=PACK), rows.rearrange("(p j) c -> p j c", j=PACK)
+                tile[:].rearrange("p (j c) -> p j c", j=PACK), rows.rearrange("(p j) c -> p j c", j=PACK)
             )
-            view = t[:].rearrange("p (j c) -> p j c", j=PACK)
-            for c in range(0, width, P):
-                raw[(name, (lo + c) // P, g)] = (t, view[:, :, c:])
-
-        nc.gpsimd.memset(xs[:].bitcast(I32), 0)
-        nc.sync.dma_start(offs_t[:], offs)
+            raw[(name, t, g)] = tile
 
         def load_x(g):
             nc.sync.dma_start(xw[g][:], x_words[g].rearrange("p n t -> p (n t)").bitcast(I32))
 
+        nc.gpsimd.memset(xs[:].bitcast(I32), 0)
+        nc.sync.dma_start(offs_t[:], offs)
         for q in range(4):
             nc.sync.dma_start(
-                xs[32 * q : 32 * q + 4 * PASSES, :].bitcast(I32),
-                x_scales[:, 4 * q : 4 * q + 4, :].bitcast(I32),
+                xs[32 * q : 32 * q + 4 * PASSES, :].bitcast(I32), x_scales[:, 4 * q : 4 * q + 4, :].bitcast(I32)
             )
         load_x(0)
-        load_w("e", w3, 0, P, 0)
+        load_w("e", w3, 0, 1, 0)
         load_x(1)
-        load_w("e", w3, 0, P, 1)
+        load_w("e", w3, 0, 1, 1)
+        load_w("e", w3, 1, 1, 0)
         for tile, src in zip(pos_t, (pos1, pos2, pos3)):
             nc.sync.dma_start(tile[:], src)
-        for g in range(PASSES):
-            load_w("e", w3, P, P, g)
-        for name, w, hf in (("e", w3, 1), ("a", w1, 0), ("a", w1, 1)):
+        load_w("e", w3, 1, 1, 1)
+        for name, w, t in (("e", w3, 2), ("a", w1, 0), ("a", w1, 2)):
             for g in range(PASSES):
-                load_w(name, w, hf * HALF, HALF, g)
-        load_w("o", w2, 0, N, 0)
+                load_w(name, w, t, 2, g)
+        load_w("o", w2, 0, 1, 0)
 
         warm = sb("warm", [P, 2], F32)
         nc.vector.memset(warm[:, 0:1], 1.0)
@@ -88,152 +85,30 @@ def tile_picked_ycovn_corr_p_kernel(
         make_identity(nc, ident[:])
 
         xg = [sb("xg%d" % g, [P, S], U32) for g in range(PASSES)]
-        SH = S // 2
         xsg = sb("xsg", [P, S], U8)
-
-        def quant(name, grp, width):
-            codes = sb("codes_" + name, [P, width], U32)
-            scales = sb("scales_" + name, [P, width], U8)
-            nc.vector.quantize_mx(out=codes[:].bitcast(FP8X4), scales=scales[:], in_=grp)
-            return codes, scales
-
-        wq = {}
         stage = {}
 
-        def cast_w(name, t, g, tiles, st=None):
-            width = tiles * P
-            if st is None:
-                st = sb("stage_%s_%d_%d" % (name, t, g), [P, 2 * width], F32)[:]
+        def cast(name, t, g):
+            src = raw[(name, t, g)]
+            st = sb("stage_%s_%d_%d" % (name, t, g), [P, src.shape[1]], BF16)
             nc.scalar.copy(
-                st.bitcast(BF16).rearrange("p (c i j) -> p c j i", i=2, j=PACK),
-                raw[(name, t, g)][1][:, :, 0:width].rearrange("p j (c i) -> p c j i", i=2),
+                st[:].rearrange("p (c i j) -> p c j i", i=2, j=PACK),
+                src[:].rearrange("p (j c i) -> p c j i", j=PACK, i=2),
             )
-            stage[(name, t, g)] = (st, tiles)
+            stage[(name, t, g)] = st
 
-        accs = {}
+        def quant(name, src):
+            width = src.shape[1] // PACK
+            codes = sb("codes_" + name, [P, width], U32)
+            scales = sb("scales_" + name, [P, width], U8)
+            nc.vector.quantize_mx(out=codes[:].bitcast(FP8X4), scales=scales[:], in_=src)
+            return codes, scales
 
-        def quant_w(name, t, g):
-            st, tiles = stage[(name, t, g)]
-            codes, scales = quant("%s_%d_%d" % (name, t, g), st.bitcast(BF16), tiles * P)
-            return [(codes[:, i * P : (i + 1) * P], scales[:, i * P : (i + 1) * P]) for i in range(tiles)]
+        acc = {("e", 1): 2, ("e", 2): 3, ("e", 3): 0, ("a", 0): 1, ("a", 1): 2, ("a", 2): 3, ("a", 3): 0}
 
-        def quant_mm(name, t0, g):
-            for i, (codes, scales) in enumerate(quant_w(name, t0, g)):
-                t = t0 + i
-                if g == 0:
-                    accs[(name, t)] = mm_ps.tile([P, S], F32, name="acc")
-                nc.tensor.matmul_mx(
-                    out=accs[(name, t)][:],
-                    lhsT=codes.bitcast(FP8X4),
-                    lhsT_scale=scales,
-                    rhs=xg[g][:].bitcast(FP8X4),
-                    rhs_scale=xsg[4 * g : P, :],
-                    start=(g == 0),
-                    stop=(g == PASSES - 1),
-                )
-
-        win = {}
-
-        def evac(name, t, copy=nc.scalar.copy):
-            w = sb("win_%s_%d" % (name, t), [P, S], F32)
-            copy(w[:], accs[(name, t)][:])
-            win[(name, t)] = w
-
-        def add_transposed(dst, srcs):
-            for i, s in enumerate(srcs):
-                nc.tensor.matmul(
-                    dst, lhsT=s, rhs=ident[:], is_transpose=True, start=(i == 0), stop=(i == len(srcs) - 1)
-                )
-
-        e0 = [sb("e0_%d" % t, [P, V], F32)[:] for t in range(TILES)]
-
-        def pick(t):
-            nc.vector.tensor_copy(e0[t], win[("e", t)][:].indirect(pos_t[0][:]))
-
-        def diff(t, n, dst):
-            nc.vector.tensor_tensor(dst, win[("e", t)][:].indirect(pos_t[n][:]), e0[t], ALU.subtract)
-
-        def sum_diffs(hf, d1, d2):
-            for i in range(2):
-                for h in range(VH):
-                    b = i * VH + h
-                    add_transposed(spare[0][:, b * P : (b + 1) * P], [d[i][:, h * P : (h + 1) * P] for d in (d1, d2)])
-            neg = sb("neg_%d" % hf, [P, 2 * V], F32)
-            nc.scalar.activation(neg[:], spare[0][:], ACT.Copy, scale=-1.0)
-            for b in range(2 * VH):
-                nc.tensor.transpose(spare[1][:, b * P : (b + 1) * P], neg[:, b * P : (b + 1) * P], ident[:])
-
-        def centre0(hf):
-            nc.scalar.copy(c0_t[hf][:], spare[1][:])
-
-        def centre(c1, c2, d1, d2):
-            nc.vector.scalar_tensor_tensor(c1, d1, 2.0, d2, ALU.mult, ALU.subtract)
-            nc.vector.scalar_tensor_tensor(c2, d2, 2.0, d1, ALU.mult, ALU.subtract)
-
-        zT = [one_ps.tile([P, H], F32, name="zT%d" % h) for h in range(VH)]
-        spare = [one_ps.tile([P, S], F32, name="spare%d" % h) for h in range(2)]
-        var_hi = one_ps.tile([P, 2 * V], F32, name="var_hi")
-        rT = [sb("rT_%d" % hf, [P, 2 * V], F32) for hf in range(2)]
-
-        def squares(hf, d2, c1, place):
-            sq = raw[("a", 2, hf)][0]
-            nc.scalar.activation(sq[:, 0 : 2 * V], d2, ACT.Square, scale=math.sqrt(3.0))
-            nc.scalar.activation(sq[:, 2 * V : 4 * V], c1, ACT.Square)
-            for h in range(VH):
-                for i in range(2):
-                    lo = place[i] * V + h * P
-                    dst = zT[h][:, i * P : (i + 1) * P] if hf == 0 else var_hi[:, h * V + i * P : h * V + (i + 1) * P]
-                    add_transposed(dst, [sq[:, o + lo : o + lo + P] for o in (0, 2 * V)])
-
-        def rsqrt(dst, src):
-            nc.scalar.activation(dst, src, ACT.Abs_reciprocal_sqrt, bias=8.1, scale=4.5)
-
-        def product(t, n, dst, h=None):
-            lo, width = (0, V) if h is None else (h * P, P)
-            nc.vector.tensor_tensor(
-                dst[:, lo : lo + width],
-                win[("a", t)][:].indirect(pos_t[n][:, lo // 16 : (lo + width) // 16]),
-                coef[(n, t)][:, lo : lo + width],
-                ALU.mult,
-            )
-
-        def z_sum(t, m, h):
-            add_transposed(zT[h][:, t * P : (t + 1) * P], [m[n][:, h * P : (h + 1) * P] for n in ORDER])
-
-        def scale(hf, h):
-            cols = slice(hf * HALF, (hf + 1) * HALF)
-            nc.vector.tensor_tensor(rrT[h][:, cols], zT[h][:, cols], at(rT[hf], h), ALU.mult)
-
-        def m_tiles(t):
-            return [sb("m_%d_%d" % (t, n), [P, V], F32)[:] for n in range(3)]
-
-        d_lo = [sb("d%d_lo" % n, [P, 3 * V], F32) for n in (1, 2)]
-        d_hi = [sb("d%d_hi" % n, [P, 3 * V], F32) for n in (1, 2)]
-        ar_c = [sb("ar_c%d" % hf, [P, 4 * V], F32) for hf in range(2)]
-        c0_t = [sb("c0_%d" % hf, [P, 2 * V], F32) for hf in range(2)]
-
-        def at(tile, lo, n=1):
-            return tile[:, lo * V : (lo + n) * V]
-
-        coef = {}
-        for (n, t), slot in zip(((1, 1), (1, 0), (2, 0), (2, 1)), range(4)):
-            coef[(n, t)] = at(ar_c[0], slot)
-        for (n, t), slot in zip(((1, 2), (1, 3), (2, 2), (2, 3)), range(4)):
-            coef[(n, t)] = at(ar_c[1], slot)
-        for t in range(TILES):
-            coef[(0, t)] = at(c0_t[t // 2], t % 2)
-
-        def gather_x(g, lo, width):
-            nc.vector.tensor_copy(
-                xg[g][:, lo : lo + width], xw[g][:].bitcast(U32).indirect(offs_t[:, lo // 16 : (lo + width) // 16])
-            )
-
-        first = [spare[h][:, 0:SH] for h in range(2)]
-
-        def first_mm(g, h, codes, scales):
-            cols = slice(h * SH, (h + 1) * SH)
+        def mx(dst, codes, scales, g, cols):
             nc.tensor.matmul_mx(
-                out=first[h],
+                out=dst,
                 lhsT=codes.bitcast(FP8X4),
                 lhsT_scale=scales,
                 rhs=xg[g][:, cols].bitcast(FP8X4),
@@ -242,119 +117,204 @@ def tile_picked_ycovn_corr_p_kernel(
                 stop=(g == PASSES - 1),
             )
 
-        nc.vector.tensor_copy(xsg[:], xs[:].indirect(offs_t[:]))
-        gather_x(0, 0, S)
-        cast_w("e", 0, 0, 1)
-        cast_w("e", 0, 1, 1)
-        ops = quant_w("e", 0, 0)[0]
-        for h in range(2):
-            first_mm(0, h, *ops)
-        gather_x(1, 0, SH)
-        ops = quant_w("e", 0, 1)[0]
-        first_mm(1, 0, *ops)
-        gather_x(1, SH, SH)
-        first_mm(1, 1, *ops)
-        win[("e", 0)] = sb("win_e_0", [P, S], F32)
-        for h in range(2):
-            nc.vector.tensor_copy(win[("e", 0)][:, h * SH : (h + 1) * SH], first[h])
-        cast_w("e", 1, 0, 1, at(d_lo[0], 0))
-        cast_w("e", 1, 1, 1, at(d_lo[1], 2))
+        def quant_mm(name, t0, g):
+            codes, scales = quant("%s_%d_%d" % (name, t0, g), stage[(name, t0, g)][:])
+            for i in range(codes.shape[1] // P):
+                cols = slice(i * P, (i + 1) * P)
+                if (name, t0) == ("e", 0):
+                    for hf in range(2):
+                        mx(bank[hf][:, 0:V], codes[:, cols], scales[:, cols], g, slice(hf * V, (hf + 1) * V))
+                else:
+                    mx(bank[acc[(name, t0 + i)]][:], codes[:, cols], scales[:, cols], g, slice(0, S))
 
-        pick(0)
-        quant_mm("e", 1, 0)
-        diff(0, 1, at(d_lo[0], 0))
-        quant_mm("e", 1, 1)
-        evac("e", 1)
-        cast_w("e", 2, 0, 2, at(ar_c[0], 1, 2))
-        cast_w("e", 2, 1, 2, at(d_lo[0], 1, 2))
-        diff(0, 2, at(d_lo[1], 2))
-        quant_mm("e", 2, 0)
-        centre(coef[(1, 0)], coef[(2, 0)], at(d_lo[0], 0), at(d_lo[1], 2))
+        win = {(name, t): sb("win_%s_%d" % (name, t), [P, S], F32) for name in "ea" for t in range(TILES)}
 
-        cast_w("a", 0, 0, 2, at(d_lo[1], 0, 2))
-        pick(1)
-        quant_mm("e", 2, 1)
-        evac("e", 2)
-        evac("e", 3)
-        diff(1, 1, at(d_lo[0], 1))
-        quant_mm("a", 0, 0)
-        diff(1, 2, at(d_lo[1], 1))
-        cast_w("a", 0, 1, 2)
-        e0[3] = stage[("a", 0, 1)][0][:, 0:V]
-        cast_w("a", 2, 0, 2, at(ar_c[1], 1, 2))
-        pick(2)
-        centre(coef[(1, 1)], coef[(2, 1)], at(d_lo[0], 1), at(d_lo[1], 1))
-        quant_mm("a", 0, 1)
-        evac("a", 0)
-        evac("a", 1)
-        sum_diffs(0, [at(d_lo[0], 0), at(d_lo[0], 1)], [at(d_lo[1], 2), at(d_lo[1], 1)])
-        squares(0, at(d_lo[1], 1, 2), at(ar_c[0], 0, 2), (1, 0))
-        centre0(0)
-        cast_w("a", 2, 1, 2)
-        for h in range(VH):
-            rsqrt(at(rT[0], h), zT[h][:, 0:HALF])
-        pick(3)
-        diff(2, 1, at(d_hi[0], 0))
-        diff(3, 1, at(d_hi[0], 1))
-        diff(2, 2, at(d_hi[1], 0))
-        diff(3, 2, at(d_hi[1], 1))
-        quant_mm("a", 2, 0)
-        centre(at(ar_c[1], 0, 2), at(ar_c[1], 2, 2), at(d_hi[0], 0, 2), at(d_hi[1], 0, 2))
+        def evac(name, t):
+            nc.scalar.copy(win[(name, t)][:], bank[acc[(name, t)]][:])
 
-        m0 = m_tiles(0)
-        for n in ORDER:
-            product(0, n, m0[n])
-        quant_mm("a", 2, 1)
-        sum_diffs(1, [at(d_hi[0], 0), at(d_hi[0], 1)], [at(d_hi[1], 0), at(d_hi[1], 1)])
-        evac("a", 2)
-        centre0(1)
-        evac("a", 3)
-        squares(1, at(d_hi[1], 0, 2), at(ar_c[1], 0, 2), (0, 1))
-        rsqrt(rT[1][:], var_hi[:])
-        cast_w("o", 0, 0, 1)
-        w2_codes, w2_scales = quant_w("o", 0, 0)[0]
-        st = stage[("a", 2, 1)][0]
-        m1 = [sb("m_1_0", [P, V], F32)[:], st[:, 0:V], st[:, V : 2 * V]]
-        for n in ORDER:
-            product(1, n, m1[n])
-        for h in range(VH):
-            z_sum(0, m0, h)
-            z_sum(1, m1, h)
+        def add_transposed(dst, srcs):
+            for i, s in enumerate(srcs):
+                nc.tensor.matmul(
+                    dst, lhsT=s, rhs=ident[:], is_transpose=True, start=(i == 0), stop=(i == len(srcs) - 1)
+                )
 
-        rrT = [sb("rrT%d" % h, [P, H], BF16)[:] for h in range(VH)]
-        m = [rT[0][:, V // 2 : 3 * V // 2], sb("m_2_1", [P, V], F32)[:], sb("m_2_2", [P, V], F32)[:]]
-        product(2, 1, m[1])
-        product(2, 2, m[2])
-        scale(0, 0)
-        scale(0, 1)
-        product(2, 0, m[0])
-        for h in range(VH):
-            z_sum(2, m, h)
-        m = [coef[(0, 2)], at(win[("a", 2)], 0), at(win[("a", 2)], 1)]
-        for h in range(VH):
+        def block(ap, h):
+            return ap[:, h * P : (h + 1) * P]
+
+        e0 = [sb("e0_%d" % t, [P, V], F32)[:] for t in range(TILES)]
+        c0_t = [sb("c0_%d" % hf, [P, 2 * V], F32) for hf in range(2)]
+        dif = {}
+        coef = {}
+        for n in (1, 2):
+            dif[(n, 0)] = at(raw[("e", 1, 1)], n - 1)
+            dif[(n, 1)] = at(raw[("e", 2, 1)], n - 1)
+            coef[(n, 0)] = at(raw[("e", 2, 0)], n - 1)
+            coef[(n, 1)] = at(raw[("a", 0, 0)], n - 1)
+            for t in (2, 3):
+                dif[(n, t)] = at(raw[("a", 0, 1)], 2 * (n - 1) + t - 2)
+                coef[(n, t)] = at(raw[("a", 2, 0)], 2 * (n - 1) + t - 2)
+        for t in range(TILES):
+            coef[(0, t)] = at(c0_t[t // 2], t % 2)
+
+        def pick(t):
+            nc.vector.tensor_copy(e0[t], win[("e", t)][:].indirect(pos_t[0][:]))
+
+        def diff(t, n):
+            nc.vector.tensor_tensor(dif[(n, t)], win[("e", t)][:].indirect(pos_t[n][:]), e0[t], ALU.subtract)
+
+        def centre(c1, c2, d1, d2):
+            nc.vector.scalar_tensor_tensor(c1, d1, 2.0, d2, ALU.mult, ALU.subtract)
+            nc.vector.scalar_tensor_tensor(c2, d2, 2.0, d1, ALU.mult, ALU.subtract)
+
+        def centre_tile(t):
+            centre(coef[(1, t)], coef[(2, t)], dif[(1, t)], dif[(2, t)])
+
+        neg = [sb("neg_%d" % hf, [P, 2 * V], F32) for hf in range(2)]
+
+        def negated_sum(hf):
+            turned = bank[6 + hf]
+            for i in range(2):
+                for h in range(VH):
+                    add_transposed(block(turned, i * VH + h), [block(dif[(n, 2 * hf + i)], h) for n in (1, 2)])
+            nc.scalar.activation(neg[hf][:], turned[:], ACT.Copy, scale=-1.0)
+            for b in range(2 * VH):
+                nc.tensor.transpose(block(bank[4 + hf], b), block(neg[hf], b), ident[:])
+
+        def centre0(hf):
+            nc.scalar.copy(c0_t[hf][:], bank[4 + hf][:])
+
+        sq = [sb("sq_%d" % hf, [P, 4 * V], F32) for hf in range(2)]
+        root = sb("root", [P, VH * H], F32)
+
+        def add_squares(hf):
+            for h in range(VH):
+                for i in range(2):
+                    add_transposed(block(bank[6 + hf], h * 2 + i), [block(at(sq[hf], o + i), h) for o in (0, 2)])
+
+        def inverse_root(hf):
+            nc.scalar.activation(
+                root[:].rearrange("v (h i) -> v h i", h=VH)[:, :, hf * V : (hf + 1) * V],
+                bank[6 + hf][:].rearrange("v (h i) -> v h i", h=VH),
+                ACT.Abs_reciprocal_sqrt,
+                bias=8.1,
+                scale=4.5,
+            )
+
+        m = {(t, n): sb("m_%d_%d" % (t, n), [P, V], F32)[:] for t in range(TILES) for n in range(3) if (t, n) not in ((1, 0), (2, 0))}
+        m[(1, 0)] = dif[(2, 1)]
+        m[(2, 0)] = dif[(2, 3)]
+
+        def z_of(t, h):
+            return block(bank[4 + h], t) if t < TILES - 1 else block(bank[1 + h], 0)
+
+        def products(t):
             for n in ORDER:
-                product(3, n, m[n], h)
-            z_sum(3, m, h)
+                nc.vector.tensor_tensor(m[(t, n)], win[("a", t)][:].indirect(pos_t[n][:]), coef[(n, t)], ALU.mult)
+            for k, n in enumerate(ORDER):
+                for h in range(VH):
+                    nc.tensor.matmul(
+                        z_of(t, h), lhsT=block(m[(t, n)], h), rhs=ident[:], is_transpose=True, start=(k == 0), stop=(k == 2)
+                    )
+
+        rrT = [sb("rrT%d" % h, [P, H], BF16) for h in range(VH)]
+
+        def scale(h, t0, tiles, z):
+            q0, q1 = t0 * 32, (t0 + tiles) * 32
+            nc.vector.tensor_tensor(
+                rrT[h][:].rearrange("v (u p e) -> v u p e", u=2, e=2)[:, :, q0:q1, :],
+                z.rearrange("v (p u e) -> v u p e", u=2, e=2),
+                root[:, h * H + t0 * P : h * H + (t0 + tiles) * P].rearrange("v (p u e) -> v u p e", u=2, e=2),
+                ALU.mult,
+            )
+
+        nc.vector.tensor_copy(xsg[:], xs[:].indirect(offs_t[:]))
+        nc.vector.tensor_copy(xg[0][:], xw[0][:].bitcast(U32).indirect(offs_t[:]))
+        cast("e", 0, 0)
+        quant_mm("e", 0, 0)
+        nc.vector.tensor_copy(xg[1][:], xw[1][:].bitcast(U32).indirect(offs_t[:]))
+        cast("e", 0, 1)
+        quant_mm("e", 0, 1)
+        for hf in range(2):
+            nc.scalar.copy(at(win[("e", 0)], hf), bank[hf][:, 0:V])
+        cast("e", 1, 0)
+        quant_mm("e", 1, 0)
+        pick(0)
+        cast("e", 1, 1)
+        quant_mm("e", 1, 1)
+        diff(0, 1)
+        diff(0, 2)
+        cast("e", 2, 0)
+        quant_mm("e", 2, 0)
+        centre_tile(0)
+        evac("e", 1)
+        pick(1)
+        cast("e", 2, 1)
+        quant_mm("e", 2, 1)
+        diff(1, 1)
+        diff(1, 2)
+        cast("a", 0, 0)
+        quant_mm("a", 0, 0)
+        centre_tile(1)
+        for t in (2, 3):
+            evac("e", t)
+            pick(t)
+        cast("a", 0, 1)
+        quant_mm("a", 0, 1)
+        for n in (1, 2):
+            for t in (2, 3):
+                diff(t, n)
+        cast("a", 2, 0)
+        quant_mm("a", 2, 0)
+        hi_d, hi_c = raw[("a", 0, 1)], raw[("a", 2, 0)]
+        centre(at(hi_c, 0, 2), at(hi_c, 2, 2), at(hi_d, 0, 2), at(hi_d, 2, 2))
+        cast("a", 2, 1)
+        quant_mm("a", 2, 1)
+        negated_sum(0)
+        negated_sum(1)
+        evac("a", 0)
+        centre0(0)
+        centre0(1)
+        products(0)
+        evac("a", 1)
+        for i in range(2):
+            nc.scalar.activation(at(sq[0], i), dif[(2, i)], ACT.Square, scale=math.sqrt(3.0))
+            nc.scalar.activation(at(sq[0], 2 + i), coef[(1, i)], ACT.Square)
+        add_squares(0)
+        products(1)
+        evac("a", 2)
+        nc.scalar.activation(at(sq[1], 0, 2), at(hi_d, 2, 2), ACT.Square, scale=math.sqrt(3.0))
+        nc.scalar.activation(at(sq[1], 2, 2), at(hi_c, 0, 2), ACT.Square)
+        add_squares(1)
+        products(2)
+        evac("a", 3)
+        inverse_root(0)
+        inverse_root(1)
+        products(3)
+        cast("o", 0, 0)
+        for h in range(VH):
+            scale(h, 0, TILES - 1, bank[4 + h][:, 0 : (TILES - 1) * P])
+        for h in range(VH):
+            scale(h, TILES - 1, 1, z_of(TILES - 1, h))
+        w2_codes, w2_scales = quant("w2", stage[("o", 0, 0)][:])
 
         for h in range(VH):
-            scale(1, h)
-            words = rrT[h].bitcast(F32)
-            back = spare[h][:, 0 : 2 * P].rearrange("p (u v) -> p u v", u=2)
+            words = rrT[h][:].bitcast(F32)
+            back = bank[6 if h == 0 else 3][:, 0 : 2 * P].rearrange("p (u v) -> p u v", u=2)
             for u in range(2):
-                nc.tensor.transpose(back[:, u, :], words[:, u : H // 2 : 2], ident[:])
+                nc.tensor.transpose(back[:, u, :], block(words, u), ident[:])
             rr = sb("rr%d" % h, [P, P * PACK], BF16)
             nc.scalar.copy(rr[:].bitcast(F32).rearrange("p (v u) -> p v u", u=2), back.rearrange("p u v -> p v u"))
-            rr_codes, rr_scales = quant("rr%d" % h, rr[:], P)
-            res = mm_ps.tile([P, P], F32, name="acc")
+            rr_codes, rr_scales = quant("rr%d" % h, rr[:])
+            res = block(bank[0 if h == 0 else 7], 0)
             nc.tensor.matmul_mx(
-                out=res[:],
-                lhsT=w2_codes.bitcast(FP8X4),
-                lhsT_scale=w2_scales,
+                out=res,
+                lhsT=w2_codes[:].bitcast(FP8X4),
+                lhsT_scale=w2_scales[:],
                 rhs=rr_codes[:].bitcast(FP8X4),
                 rhs_scale=rr_scales[:],
                 start=True,
                 stop=True,
             )
             res_sb = sb("res_sb%d" % h, [P, P], F32)
-            nc.scalar.copy(res_sb[:], res[:])
-            nc.sync.dma_start(out[:, h * P : (h + 1) * P], res_sb[:])
+            nc.scalar.copy(res_sb[:], res)
+            nc.scalar.dma_start(out[:, h * P : (h + 1) * P], res_sb[:])

@@ -60,21 +60,22 @@ def tile_picked_ycovn_corr_p_kernel(tc, x_words, x_scales, w1, w3, w2, offs, pos
 
         nc.gpsimd.memset(xs[:].bitcast(I32), 0)
         nc.sync.dma_start(offs_t[:], offs)
+        load_x(0)
         for q in range(4):
             nc.sync.dma_start(
                 xs[32 * q : 32 * q + 4 * PASSES, :].bitcast(I32), x_scales[:, 4 * q : 4 * q + 4, :].bitcast(I32)
             )
-        load_x(0)
         load_w("e", w3, 0, 1, 0)
-        load_x(1)
         load_w("e", w3, 0, 1, 1)
+        load_x(1)
         load_w("e", w3, 1, 1, 0)
+        load_w("e", w3, 1, 1, 1)
         for tile, src in zip(pos_t, (pos1, pos2, pos3)):
             nc.sync.dma_start(tile[:], src)
-        load_w("e", w3, 1, 1, 1)
-        for name, w, t in (("e", w3, 2), ("a", w1, 0), ("a", w1, 2)):
-            for g in range(PASSES):
-                load_w(name, w, t, 2, g)
+        for name, w, first in (("e", w3, 2), ("a", w1, 0)):
+            for t in range(first, TILES):
+                for g in range(PASSES):
+                    load_w(name, w, t, 1, g)
         load_w("o", w2, 0, 1, 0)
 
         warm = sb("warm", [P, 2], F32)
@@ -88,11 +89,12 @@ def tile_picked_ycovn_corr_p_kernel(tc, x_words, x_scales, w1, w3, w2, offs, pos
         xsg = sb("xsg", [P, S], U8)
         stage = {}
 
-        def cast(name, t, g):
+        def cast(name, t, g, st=None, copy=nc.scalar.copy):
             src = raw[(name, t, g)]
-            st = sb("stage_%s_%d_%d" % (name, t, g), [P, src.shape[1]], BF16)
-            nc.scalar.copy(
-                st[:].rearrange("p (c i j) -> p c j i", i=2, j=PACK),
+            if st is None:
+                st = sb("stage_%s_%d_%d" % (name, t, g), [P, src.shape[1]], BF16)[:]
+            copy(
+                st.rearrange("p (c i j) -> p c j i", i=2, j=PACK),
                 src[:].rearrange("p (j c i) -> p c j i", j=PACK, i=2),
             )
             stage[(name, t, g)] = st
@@ -117,17 +119,30 @@ def tile_picked_ycovn_corr_p_kernel(tc, x_words, x_scales, w1, w3, w2, offs, pos
                 stop=(g == PASSES - 1),
             )
 
+        first = ((0, 0, V), (1, V, V + P), (4, V + P, S))
+
+        def gather_x(g, lo, hi):
+            nc.vector.tensor_copy(xg[g][:, lo:hi], xw[g][:].bitcast(U32).indirect(offs_t[:, lo // 16 : hi // 16]))
+
         def quant_mm(name, t0, g):
-            codes, scales = quant("%s_%d_%d" % (name, t0, g), stage[(name, t0, g)][:])
+            codes, scales = quant("%s_%d_%d" % (name, t0, g), stage[(name, t0, g)])
             for i in range(codes.shape[1] // P):
                 cols = slice(i * P, (i + 1) * P)
                 if (name, t0) == ("e", 0):
-                    for hf in range(2):
-                        mx(bank[hf][:, 0:V], codes[:, cols], scales[:, cols], g, slice(hf * V, (hf + 1) * V))
+                    for b, lo, hi in first:
+                        if g == 1:
+                            gather_x(1, lo, hi)
+                        mx(bank[b][:, lo:hi], codes[:, cols], scales[:, cols], g, slice(lo, hi))
                 else:
                     mx(bank[acc[(name, t0 + i)]][:], codes[:, cols], scales[:, cols], g, slice(0, S))
 
+        def weights(name, t, g):
+            cast(name, t, g)
+            quant_mm(name, t, g)
+
         win = {(name, t): sb("win_%s_%d" % (name, t), [P, S], F32) for name in "ea" for t in range(TILES)}
+
+        win[("e", 1)] = raw[("e", 2, 1)]
 
         def evac(name, t):
             nc.scalar.copy(win[(name, t)][:], bank[acc[(name, t)]][:])
@@ -145,14 +160,12 @@ def tile_picked_ycovn_corr_p_kernel(tc, x_words, x_scales, w1, w3, w2, offs, pos
         c0_t = [sb("c0_%d" % hf, [P, 2 * V], F32) for hf in range(2)]
         dif = {}
         coef = {}
-        for n in (1, 2):
-            dif[(n, 0)] = at(raw[("e", 1, 1)], n - 1)
-            dif[(n, 1)] = at(raw[("e", 2, 1)], n - 1)
-            coef[(n, 0)] = at(raw[("e", 2, 0)], n - 1)
-            coef[(n, 1)] = at(raw[("a", 0, 0)], n - 1)
-            for t in (2, 3):
-                dif[(n, t)] = at(raw[("a", 0, 1)], 2 * (n - 1) + t - 2)
-                coef[(n, t)] = at(raw[("a", 2, 0)], 2 * (n - 1) + t - 2)
+        dif_on = (sb("dif_0", [P, 2 * V], F32), raw[("e", 3, 1)], raw[("a", 1, 0)], raw[("a", 2, 1)])
+        coef_on = (raw[("e", 2, 0)], raw[("a", 0, 1)], raw[("a", 2, 0)], raw[("a", 3, 1)])
+        for t in range(TILES):
+            for n in (1, 2):
+                dif[(n, t)] = at(dif_on[t], n - 1)
+                coef[(n, t)] = at(coef_on[t], n - 1)
         for t in range(TILES):
             coef[(0, t)] = at(c0_t[t // 2], t % 2)
 
@@ -178,31 +191,35 @@ def tile_picked_ycovn_corr_p_kernel(tc, x_words, x_scales, w1, w3, w2, offs, pos
                     add_transposed(block(turned, i * VH + h), [block(dif[(n, 2 * hf + i)], h) for n in (1, 2)])
             nc.scalar.activation(neg[hf][:], turned[:], ACT.Copy, scale=-1.0)
             for b in range(2 * VH):
-                nc.tensor.transpose(block(bank[4 + hf], b), block(neg[hf], b), ident[:])
+                nc.tensor.transpose(block(turned, b), block(neg[hf], b), ident[:])
 
         def centre0(hf):
-            nc.scalar.copy(c0_t[hf][:], bank[4 + hf][:])
+            nc.scalar.copy(c0_t[hf][:], bank[6 + hf][:])
 
-        sq = [sb("sq_%d" % hf, [P, 4 * V], F32) for hf in range(2)]
+        sq = (raw[("a", 0, 0)], raw[("a", 1, 1)], raw[("a", 3, 0)], sb("sq_3", [P, 2 * V], F32))
         root = sb("root", [P, VH * H], F32)
+
+        var_bank = (6, 1)
+
+        def squares(t):
+            nc.scalar.activation(at(sq[t], 0), dif[(2, t)], ACT.Square, scale=math.sqrt(3.0))
+            nc.scalar.activation(at(sq[t], 1), coef[(1, t)], ACT.Square)
 
         def add_squares(hf):
             for h in range(VH):
                 for i in range(2):
-                    add_transposed(block(bank[6 + hf], h * 2 + i), [block(at(sq[hf], o + i), h) for o in (0, 2)])
+                    add_transposed(block(bank[var_bank[hf]], h * 2 + i), [block(at(sq[2 * hf + i], o), h) for o in range(2)])
 
         def inverse_root(hf):
             nc.scalar.activation(
                 root[:].rearrange("v (h i) -> v h i", h=VH)[:, :, hf * V : (hf + 1) * V],
-                bank[6 + hf][:].rearrange("v (h i) -> v h i", h=VH),
+                bank[var_bank[hf]][:].rearrange("v (h i) -> v h i", h=VH),
                 ACT.Abs_reciprocal_sqrt,
                 bias=8.1,
                 scale=4.5,
             )
 
-        m = {(t, n): sb("m_%d_%d" % (t, n), [P, V], F32)[:] for t in range(TILES) for n in range(3) if (t, n) not in ((1, 0), (2, 0))}
-        m[(1, 0)] = dif[(2, 1)]
-        m[(2, 0)] = dif[(2, 3)]
+        m = {(t, n): sb("m_%d_%d" % (t, n), [P, V], F32)[:] for t in range(TILES) for n in range(3)}
 
         def z_of(t, h):
             return block(bank[4 + h], t) if t < TILES - 1 else block(bank[1 + h], 0)
@@ -227,75 +244,75 @@ def tile_picked_ycovn_corr_p_kernel(tc, x_words, x_scales, w1, w3, w2, offs, pos
                 ALU.mult,
             )
 
+        gather_x(0, 0, S)
         nc.vector.tensor_copy(xsg[:], xs[:].indirect(offs_t[:]))
-        nc.vector.tensor_copy(xg[0][:], xw[0][:].bitcast(U32).indirect(offs_t[:]))
         cast("e", 0, 0)
         quant_mm("e", 0, 0)
-        nc.vector.tensor_copy(xg[1][:], xw[1][:].bitcast(U32).indirect(offs_t[:]))
         cast("e", 0, 1)
         quant_mm("e", 0, 1)
-        for hf in range(2):
-            nc.scalar.copy(at(win[("e", 0)], hf), bank[hf][:, 0:V])
-        cast("e", 1, 0)
+        for b, lo, hi in first:
+            nc.scalar.copy(win[("e", 0)][:, lo:hi], bank[b][:, lo:hi])
+        cast("e", 1, 0, copy=nc.vector.tensor_copy)
         quant_mm("e", 1, 0)
+        cast("e", 1, 1, copy=nc.vector.tensor_copy)
         pick(0)
-        cast("e", 1, 1)
         quant_mm("e", 1, 1)
         diff(0, 1)
         diff(0, 2)
-        cast("e", 2, 0)
-        quant_mm("e", 2, 0)
+        weights("e", 2, 0)
         centre_tile(0)
+        weights("e", 2, 1)
+        weights("e", 3, 0)
         evac("e", 1)
         pick(1)
-        cast("e", 2, 1)
-        quant_mm("e", 2, 1)
+        weights("e", 3, 1)
         diff(1, 1)
         diff(1, 2)
-        cast("a", 0, 0)
-        quant_mm("a", 0, 0)
+        weights("a", 0, 0)
+        weights("a", 0, 1)
         centre_tile(1)
-        for t in (2, 3):
-            evac("e", t)
-            pick(t)
-        cast("a", 0, 1)
-        quant_mm("a", 0, 1)
-        for n in (1, 2):
-            for t in (2, 3):
-                diff(t, n)
-        cast("a", 2, 0)
-        quant_mm("a", 2, 0)
-        hi_d, hi_c = raw[("a", 0, 1)], raw[("a", 2, 0)]
-        centre(at(hi_c, 0, 2), at(hi_c, 2, 2), at(hi_d, 0, 2), at(hi_d, 2, 2))
-        cast("a", 2, 1)
-        quant_mm("a", 2, 1)
+        evac("e", 2)
+        pick(2)
+        weights("a", 1, 0)
+        diff(2, 1)
+        diff(2, 2)
+        squares(0)
+        weights("a", 1, 1)
+        weights("a", 2, 0)
+        centre_tile(2)
         negated_sum(0)
-        negated_sum(1)
+        evac("e", 3)
+        pick(3)
+        weights("a", 2, 1)
+        diff(3, 1)
+        diff(3, 2)
+        squares(1)
+        weights("a", 3, 0)
+        weights("a", 3, 1)
+        centre_tile(3)
         evac("a", 0)
         centre0(0)
-        centre0(1)
-        products(0)
-        evac("a", 1)
-        for i in range(2):
-            nc.scalar.activation(at(sq[0], i), dif[(2, i)], ACT.Square, scale=math.sqrt(3.0))
-            nc.scalar.activation(at(sq[0], 2 + i), coef[(1, i)], ACT.Square)
         add_squares(0)
+        products(0)
+        squares(2)
+        evac("a", 1)
+        negated_sum(1)
         products(1)
-        evac("a", 2)
-        nc.scalar.activation(at(sq[1], 0, 2), at(hi_d, 2, 2), ACT.Square, scale=math.sqrt(3.0))
-        nc.scalar.activation(at(sq[1], 2, 2), at(hi_c, 0, 2), ACT.Square)
+        squares(3)
         add_squares(1)
+        evac("a", 2)
+        inverse_root(0)
+        centre0(1)
         products(2)
         evac("a", 3)
-        inverse_root(0)
         inverse_root(1)
         products(3)
-        cast("o", 0, 0)
+        cast("o", 0, 0, at(sq[3], 1).bitcast(BF16))
         for h in range(VH):
             scale(h, 0, TILES - 1, bank[4 + h][:, 0 : (TILES - 1) * P])
         for h in range(VH):
             scale(h, TILES - 1, 1, z_of(TILES - 1, h))
-        w2_codes, w2_scales = quant("w2", stage[("o", 0, 0)][:])
+        w2_codes, w2_scales = quant("w2", stage[("o", 0, 0)])
 
         for h in range(VH):
             words = rrT[h][:].bitcast(F32)
@@ -317,4 +334,4 @@ def tile_picked_ycovn_corr_p_kernel(tc, x_words, x_scales, w1, w3, w2, offs, pos
             )
             res_sb = sb("res_sb%d" % h, [P, P], F32)
             nc.scalar.copy(res_sb[:], res)
-            nc.scalar.dma_start(out[:, h * P : (h + 1) * P], res_sb[:])
+            (nc.sync if h == 0 else nc.scalar).dma_start(out[:, h * P : (h + 1) * P], res_sb[:])

@@ -70,7 +70,7 @@ def tile_picked_ycovn_corr_p_kernel(tc, x_words, x_scales, w1, w3, w2, offs, pos
         load_x(1)
         load_w("e", w3, 1, 1, 0)
         load_w("e", w3, 1, 1, 1)
-        for tile, src in zip(pos_t, (pos1, pos2, pos3)):
+        for tile, src in reversed(list(zip(pos_t, (pos1, pos2, pos3)))):
             nc.sync.dma_start(tile[:], src)
         for name, w, first in (("e", w3, 2), ("a", w1, 0)):
             for t in range(first, TILES):
@@ -142,7 +142,7 @@ def tile_picked_ycovn_corr_p_kernel(tc, x_words, x_scales, w1, w3, w2, offs, pos
 
         win = {(name, t): sb("win_%s_%d" % (name, t), [P, S], F32) for name in "ea" for t in range(TILES)}
 
-        win[("e", 1)] = raw[("e", 2, 1)]
+        win[("e", 1)] = raw[("e", 2, 0)]
 
         def evac(name, t):
             nc.scalar.copy(win[(name, t)][:], bank[acc[(name, t)]][:])
@@ -160,8 +160,8 @@ def tile_picked_ycovn_corr_p_kernel(tc, x_words, x_scales, w1, w3, w2, offs, pos
         c0_t = [sb("c0_%d" % hf, [P, 2 * V], F32) for hf in range(2)]
         dif = {}
         coef = {}
-        dif_on = (sb("dif_0", [P, 2 * V], F32), raw[("e", 3, 1)], raw[("a", 1, 0)], raw[("a", 2, 1)])
-        coef_on = (raw[("e", 2, 0)], raw[("a", 0, 1)], raw[("a", 2, 0)], raw[("a", 3, 1)])
+        dif_on = (sb("dif_0", [P, 2 * V], F32), raw[("e", 3, 1)], raw[("a", 1, 1)], raw[("a", 3, 1)])
+        coef_on = (raw[("e", 2, 1)], raw[("a", 0, 1)], raw[("a", 2, 1)], sb("coef_3", [P, 2 * V], F32))
         for t in range(TILES):
             for n in (1, 2):
                 dif[(n, t)] = at(dif_on[t], n - 1)
@@ -196,7 +196,7 @@ def tile_picked_ycovn_corr_p_kernel(tc, x_words, x_scales, w1, w3, w2, offs, pos
         def centre0(hf):
             nc.scalar.copy(c0_t[hf][:], bank[6 + hf][:])
 
-        sq = (raw[("a", 0, 0)], raw[("a", 1, 1)], raw[("a", 3, 0)], sb("sq_3", [P, 2 * V], F32))
+        sq = (raw[("a", 2, 0)], raw[("a", 3, 0)], raw[("a", 1, 0)], sb("sq_3", [P, 2 * V], F32))
         root = sb("root", [P, VH * H], F32)
 
         var_bank = (6, 1)
@@ -255,49 +255,41 @@ def tile_picked_ycovn_corr_p_kernel(tc, x_words, x_scales, w1, w3, w2, offs, pos
         cast("e", 1, 0, copy=nc.vector.tensor_copy)
         quant_mm("e", 1, 0)
         cast("e", 1, 1, copy=nc.vector.tensor_copy)
-        pick(0)
         quant_mm("e", 1, 1)
+        pick(0)
         diff(0, 1)
         diff(0, 2)
         weights("e", 2, 0)
-        centre_tile(0)
         weights("e", 2, 1)
-        weights("e", 3, 0)
-        evac("e", 1)
-        pick(1)
-        weights("e", 3, 1)
-        diff(1, 1)
-        diff(1, 2)
-        weights("a", 0, 0)
-        weights("a", 0, 1)
-        centre_tile(1)
-        evac("e", 2)
-        pick(2)
-        weights("a", 1, 0)
-        diff(2, 1)
-        diff(2, 2)
-        squares(0)
-        weights("a", 1, 1)
-        weights("a", 2, 0)
-        centre_tile(2)
+        centre_tile(0)
+        for t, first_w, second_w in ((1, ("e", 3), ("a", 0)), (2, ("a", 1), ("a", 2))):
+            evac("e", t)
+            pick(t)
+            for g in range(PASSES):
+                weights(*first_w, g)
+            diff(t, 1)
+            diff(t, 2)
+            for g in range(PASSES):
+                weights(*second_w, g)
+            centre_tile(t)
         negated_sum(0)
         evac("e", 3)
         pick(3)
-        weights("a", 2, 1)
+        for g in range(PASSES):
+            weights("a", 3, g)
         diff(3, 1)
         diff(3, 2)
-        squares(1)
-        weights("a", 3, 0)
-        weights("a", 3, 1)
-        centre_tile(3)
         evac("a", 0)
+        centre_tile(3)
         centre0(0)
+        squares(0)
+        squares(1)
         add_squares(0)
         products(0)
-        squares(2)
         evac("a", 1)
         negated_sum(1)
         products(1)
+        squares(2)
         squares(3)
         add_squares(1)
         evac("a", 2)

@@ -94,8 +94,8 @@ def tile_picked_ycovn_corr_p_kernel(tc, x_words, x_scales, w1, w3, w2, offs, pos
             if st is None:
                 st = sb("stage_%s_%d_%d" % (name, t, g), [P, src.shape[1]], BF16)[:]
             copy(
-                st.rearrange("p (c i j) -> p c j i", i=2, j=PACK),
-                src[:].rearrange("p (j c i) -> p c j i", j=PACK, i=2),
+                st.rearrange("p (c i j) -> p c j i", i=4, j=PACK),
+                src[:].rearrange("p (j c i) -> p c j i", j=PACK, i=4),
             )
             stage[(name, t, g)] = st
 

@@ -191,15 +191,19 @@ def tile_picked_ycovn_corr_p_kernel(tc, x_words, x_scales, w1, w3, w2, offs, pos
                     add_transposed(block(turned, i * VH + h), [block(dif[(n, 2 * hf + i)], h) for n in (1, 2)])
             nc.scalar.activation(neg[hf][:], turned[:], ACT.Copy, scale=-1.0)
             for b in range(2 * VH):
-                nc.tensor.transpose(block(turned, b), block(neg[hf], b), ident[:])
+                nc.tensor.transpose(block(turned, b) if hf else block(bank[4 + b // VH], b % VH), block(neg[hf], b), ident[:])
 
         def centre0(hf):
-            nc.scalar.copy(c0_t[hf][:], bank[6 + hf][:])
+            if hf:
+                nc.scalar.copy(c0_t[hf][:], bank[6 + hf][:])
+            else:
+                for i in range(2):
+                    nc.scalar.copy(at(c0_t[0], i), bank[4 + i][:, 0:V])
 
         sq = (raw[("a", 2, 0)], raw[("a", 3, 0)], raw[("a", 1, 0)], sb("sq_3", [P, 2 * V], F32))
         root = sb("root", [P, VH * H], F32)
 
-        var_bank = (6, 1)
+        var_bank = (1, 6)
 
         def squares(t):
             nc.scalar.activation(at(sq[t], 0), dif[(2, t)], ACT.Square, scale=math.sqrt(3.0))
@@ -222,7 +226,7 @@ def tile_picked_ycovn_corr_p_kernel(tc, x_words, x_scales, w1, w3, w2, offs, pos
         m = {(t, n): sb("m_%d_%d" % (t, n), [P, V], F32)[:] for t in range(TILES) for n in range(3)}
 
         def z_of(t, h):
-            return block(bank[4 + h], t) if t < TILES - 1 else block(bank[1 + h], 0)
+            return block(bank[4 + h], t) if t < TILES - 1 else block(bank[3 - h], 0)
 
         def products(t):
             for n in ORDER:
@@ -281,10 +285,10 @@ def tile_picked_ycovn_corr_p_kernel(tc, x_words, x_scales, w1, w3, w2, offs, pos
         diff(3, 2)
         evac("a", 0)
         centre_tile(3)
-        centre0(0)
         squares(0)
         squares(1)
         add_squares(0)
+        centre0(0)
         products(0)
         evac("a", 1)
         negated_sum(1)
@@ -308,13 +312,13 @@ def tile_picked_ycovn_corr_p_kernel(tc, x_words, x_scales, w1, w3, w2, offs, pos
 
         for h in range(VH):
             words = rrT[h][:].bitcast(F32)
-            back = bank[6 if h == 0 else 3][:, 0 : 2 * P].rearrange("p (u v) -> p u v", u=2)
+            back = bank[h][:, 0 : 2 * P].rearrange("p (u v) -> p u v", u=2)
             for u in range(2):
                 nc.tensor.transpose(back[:, u, :], block(words, u), ident[:])
             rr = sb("rr%d" % h, [P, P * PACK], BF16)
             nc.scalar.copy(rr[:].bitcast(F32).rearrange("p (v u) -> p v u", u=2), back.rearrange("p u v -> p v u"))
             rr_codes, rr_scales = quant("rr%d" % h, rr[:])
-            res = block(bank[0 if h == 0 else 7], 0)
+            res = block(bank[6 + h], 0)
             nc.tensor.matmul_mx(
                 out=res,
                 lhsT=w2_codes[:].bitcast(FP8X4),

@@ -184,26 +184,27 @@ def tile_picked_ycovn_corr_p_kernel(tc, x_words, x_scales, w1, w3, w2, offs, pos
 
         neg = [sb("neg_%d" % hf, [P, 2 * V], F32) for hf in range(2)]
 
-        def negated_sum(hf):
-            turned = bank[6 + hf]
-            for i in range(2):
+        def turned_sum(tiles, turned):
+            for i, t in enumerate(tiles):
                 for h in range(VH):
-                    add_transposed(block(turned, i * VH + h), [block(dif[(n, 2 * hf + i)], h) for n in (1, 2)])
-            nc.scalar.activation(neg[hf][:], turned[:], ACT.Copy, scale=-1.0)
-            for b in range(2 * VH):
-                nc.tensor.transpose(block(turned, b) if hf else block(bank[4 + b // VH], b % VH), block(neg[hf], b), ident[:])
+                    add_transposed(block(turned, i * VH + h), [block(dif[(n, t)], h) for n in (1, 2)])
 
-        def centre0(hf):
-            if hf:
-                nc.scalar.copy(c0_t[hf][:], bank[6 + hf][:])
-            else:
-                for i in range(2):
-                    nc.scalar.copy(at(c0_t[0], i), bank[4 + i][:, 0:V])
+        def negated_sum(tiles, turned, homes):
+            negated = at(neg[tiles[0] // 2], tiles[0] % 2, len(tiles))
+            nc.scalar.activation(negated, at(turned, 0, len(tiles)), ACT.Copy, scale=-1.0)
+            for i, home in enumerate(homes):
+                for h in range(VH):
+                    nc.tensor.transpose(block(home, h), block(negated, i * VH + h), ident[:])
+
+        home = (bank[4], bank[5], bank[7], bank[6])
+
+        def centre0(t):
+            nc.scalar.copy(coef[(0, t)], at(home[t], 0))
 
         sq = (raw[("a", 2, 0)], raw[("a", 3, 0)], raw[("a", 1, 0)], sb("sq_3", [P, 2 * V], F32))
         root = sb("root", [P, VH * H], F32)
 
-        var_bank = (1, 6)
+        var_bank = (1, 7)
 
         def squares(t):
             nc.scalar.activation(at(sq[t], 0), dif[(2, t)], ACT.Square, scale=math.sqrt(3.0))
@@ -276,34 +277,39 @@ def tile_picked_ycovn_corr_p_kernel(tc, x_words, x_scales, w1, w3, w2, offs, pos
             for g in range(PASSES):
                 weights(*second_w, g)
             centre_tile(t)
-        negated_sum(0)
+        turned_sum((0, 1), bank[6])
+        turned_sum((2,), bank[7])
+        negated_sum((0, 1), bank[6], home[:2])
         evac("e", 3)
         pick(3)
         for g in range(PASSES):
             weights("a", 3, g)
         diff(3, 1)
         diff(3, 2)
+        turned_sum((3,), bank[6])
         evac("a", 0)
         centre_tile(3)
+        negated_sum((2,), bank[7], home[2:3])
         squares(0)
         squares(1)
         add_squares(0)
-        centre0(0)
+        for t in range(3):
+            centre0(t)
         products(0)
         evac("a", 1)
-        negated_sum(1)
-        products(1)
         squares(2)
+        negated_sum((3,), bank[6], home[3:])
+        evac("a", 2)
         squares(3)
         add_squares(1)
-        evac("a", 2)
+        products(1)
         inverse_root(0)
-        centre0(1)
         products(2)
         evac("a", 3)
+        centre0(3)
         inverse_root(1)
         products(3)
-        cast("o", 0, 0, at(sq[3], 1).bitcast(BF16))
+        cast("o", 0, 0, m[(3, 2)].bitcast(BF16))
         for h in range(VH):
             scale(h, 0, TILES - 1, bank[4 + h][:, 0 : (TILES - 1) * P])
         for h in range(VH):

@@ -59,8 +59,8 @@ def tile_picked_ycovn_corr_p_kernel(tc, x_words, x_scales, w1, w3, w2, offs, pos
             nc.sync.dma_start(xw[g][:], x_words[g].rearrange("p n t -> p (n t)").bitcast(I32))
 
         nc.gpsimd.memset(xs[:].bitcast(I32), 0)
-        nc.sync.dma_start(offs_t[:], offs)
         load_x(0)
+        nc.sync.dma_start(offs_t[:], offs)
         for q in range(4):
             nc.sync.dma_start(
                 xs[32 * q : 32 * q + 4 * PASSES, :].bitcast(I32), x_scales[:, 4 * q : 4 * q + 4, :].bitcast(I32)
@@ -136,9 +136,14 @@ def tile_picked_ycovn_corr_p_kernel(tc, x_words, x_scales, w1, w3, w2, offs, pos
                 else:
                     mx(bank[acc[(name, t0 + i)]][:], codes[:, cols], scales[:, cols], g, slice(0, S))
 
-        def weights(name, t, g):
-            cast(name, t, g)
-            quant_mm(name, t, g)
+        def weights(name, t):
+            staged = sb("stage_%s_%d" % (name, t), [P, PASSES * K_PASS], BF16)
+            for g in range(PASSES):
+                cast(name, t, g, staged[:, g * K_PASS : (g + 1) * K_PASS])
+            codes, scales = quant("%s_%d" % (name, t), staged[:])
+            for g in range(PASSES):
+                cols = slice(g * P, (g + 1) * P)
+                mx(bank[acc[(name, t)]][:], codes[:, cols], scales[:, cols], g, slice(0, S))
 
         win = {(name, t): sb("win_%s_%d" % (name, t), [P, S], F32) for name in "ea" for t in range(TILES)}
 
@@ -264,30 +269,26 @@ def tile_picked_ycovn_corr_p_kernel(tc, x_words, x_scales, w1, w3, w2, offs, pos
         pick(0)
         diff(0, 1)
         diff(0, 2)
-        weights("e", 2, 0)
-        weights("e", 2, 1)
+        weights("e", 2)
         centre_tile(0)
         for t, first_w, second_w in ((1, ("e", 3), ("a", 0)), (2, ("a", 1), ("a", 2))):
             evac("e", t)
             pick(t)
-            for g in range(PASSES):
-                weights(*first_w, g)
+            weights(*first_w)
             diff(t, 1)
             diff(t, 2)
-            for g in range(PASSES):
-                weights(*second_w, g)
+            weights(*second_w)
             centre_tile(t)
         turned_sum((0, 1), bank[6])
         turned_sum((2,), bank[7])
-        negated_sum((0, 1), bank[6], home[:2])
         evac("e", 3)
         pick(3)
-        for g in range(PASSES):
-            weights("a", 3, g)
+        weights("a", 3)
         diff(3, 1)
         diff(3, 2)
-        turned_sum((3,), bank[6])
         evac("a", 0)
+        negated_sum((0, 1), bank[6], home[:2])
+        turned_sum((3,), bank[6])
         centre_tile(3)
         negated_sum((2,), bank[7], home[2:3])
         squares(0)

@@ -174,6 +174,9 @@ def tile_picked_ycovn_corr_p_kernel(tc, x_words, x_scales, w1, w3, w2, offs, pos
         for t in range(TILES):
             coef[(0, t)] = at(c0_t[t // 2], t % 2)
 
+        last_c = sb("last_c", [P, 2 * V], F32)
+        coef[(0, 3)], coef[(2, 3)] = at(last_c, 0), at(last_c, 1)
+
         def pick(t):
             nc.vector.tensor_copy(e0[t], win[("e", t)][:].indirect(pos_t[0][:]))
 
@@ -289,7 +292,9 @@ def tile_picked_ycovn_corr_p_kernel(tc, x_words, x_scales, w1, w3, w2, offs, pos
         evac("a", 0)
         negated_sum((0, 1), bank[6], home[:2])
         turned_sum((3,), bank[6])
-        centre_tile(3)
+        for h in range(VH):
+            nc.tensor.transpose(block(bank[6], VH + h), block(dif[(2, 3)], h), ident[:])
+        nc.vector.scalar_tensor_tensor(coef[(1, 3)], dif[(1, 3)], 2.0, dif[(2, 3)], ALU.mult, ALU.subtract)
         negated_sum((2,), bank[7], home[2:3])
         squares(0)
         squares(1)
@@ -298,16 +303,20 @@ def tile_picked_ycovn_corr_p_kernel(tc, x_words, x_scales, w1, w3, w2, offs, pos
             centre0(t)
         products(0)
         evac("a", 1)
-        squares(2)
+        thrice = sb("thrice", [P, V], F32)
+        nc.scalar.activation(thrice[:], at(bank[6], 1), ACT.Copy, scale=3.0)
         negated_sum((3,), bank[6], home[3:])
+        for h in range(VH):
+            add_transposed(block(bank[6], VH + h), [block(thrice, h), block(at(neg[1], 1), h)])
         evac("a", 2)
+        squares(2)
         squares(3)
         add_squares(1)
         products(1)
-        inverse_root(0)
         products(2)
         evac("a", 3)
-        centre0(3)
+        nc.scalar.copy(last_c[:], bank[6][:])
+        inverse_root(0)
         inverse_root(1)
         products(3)
         cast("o", 0, 0, m[(3, 2)].bitcast(BF16))

@@ -22,11 +22,29 @@ PACK = 4
 K_PASS = P * PACK
 PASSES = K // K_PASS
 TILES = H // P
-VH = V // P
+LAST = TILES - 1
+HALVES = V // P
+GROUP = 16
+QUADRANT = 32
+ROWS = 4
+BANKS = 8
+RUN = 4
 ORDER = (1, 2, 0)
 
+ACC_BANK = {("e", 1): 2, ("e", 2): 3, ("e", 3): 0, ("a", 0): 1, ("a", 1): 2, ("a", 2): 3, ("a", 3): 0}
+FIRST_PIECES = ((0, 0, V), (1, V, V + P), (4, V + P, S))
+SUM_BANK = (4, 5)
+LAST_SUM_BANK = (3, 2)
+TRIPS = (((0, 1), 6), ((2,), 7), ((3,), 6))
+C0_BANK = (4, 5, 7, 6)
+VAR_BANK = (1, 7)
+BACK_BANK = (0, 1)
+OUT_BANK = (6, 7)
 
-def tile_picked_ycovn_corr_p_kernel(tc, x_words, x_scales, w1, w3, w2, offs, pos1, pos2, pos3, out):
+
+def tile_picked_ycovn_corr_p_kernel(
+    tc, x_words, x_scales, w1, w3, w2, offs, pos1, pos2, pos3, out
+):
     nc = tc.nc
     with ExitStack() as ctx:
         keep = ctx.enter_context(tc.tile_pool(name="keep", bufs=1))
@@ -35,21 +53,23 @@ def tile_picked_ycovn_corr_p_kernel(tc, x_words, x_scales, w1, w3, w2, offs, pos
         def sb(name, shape, dtype):
             return keep.tile(shape, dtype, name=name, align_bytes=64)
 
-        def at(tile, lo, n=1):
-            return tile[:, lo * V : (lo + n) * V]
+        def slot(tile, i):
+            return tile[:, i * V : (i + 1) * V]
 
-        bank = [psum.tile([P, S], F32, name="bank%d" % i) for i in range(8)]
+        def block(ap, i):
+            return ap[:, i * P : (i + 1) * P]
 
-        offs_t = sb("offs_t", [P, S // 16], U16)
-        pos_t = [sb("pos_t%d" % i, [P, V // 16], U16) for i in range(3)]
+        bank = [psum.tile([P, S], F32, name="bank%d" % i) for i in range(BANKS)]
+
+        offs_t = sb("offs_t", [P, S // GROUP], U16)
+        pos_t = [sb("pos_t%d" % i, [P, V // GROUP], U16) for i in range(3)]
         xw = [sb("xw%d" % g, [P, T], I32) for g in range(PASSES)]
         xs = sb("xs", [P, T], U8)
         raw = {}
 
-        def load_w(name, w, t, tiles, g):
-            width = tiles * P
-            tile = sb("raw_%s_%d_%d" % (name, t, g), [P, PACK * width], F32)
-            rows = w[g * K_PASS : (g + 1) * K_PASS, t * P : t * P + width]
+        def load_w(name, w, t, g):
+            tile = sb("raw_%s_%d_%d" % (name, t, g), [P, PACK * P], F32)
+            rows = w[g * K_PASS : (g + 1) * K_PASS, t * P : (t + 1) * P]
             nc.sync.dma_start(
                 tile[:].rearrange("p (j c) -> p j c", j=PACK), rows.rearrange("(p j) c -> p j c", j=PACK)
             )
@@ -61,22 +81,23 @@ def tile_picked_ycovn_corr_p_kernel(tc, x_words, x_scales, w1, w3, w2, offs, pos
         nc.gpsimd.memset(xs[:].bitcast(I32), 0)
         load_x(0)
         nc.sync.dma_start(offs_t[:], offs)
-        for q in range(4):
+        for q in range(P // QUADRANT):
             nc.sync.dma_start(
-                xs[32 * q : 32 * q + 4 * PASSES, :].bitcast(I32), x_scales[:, 4 * q : 4 * q + 4, :].bitcast(I32)
+                xs[QUADRANT * q : QUADRANT * q + ROWS * PASSES, :].bitcast(I32),
+                x_scales[:, ROWS * q : ROWS * (q + 1), :].bitcast(I32),
             )
-        load_w("e", w3, 0, 1, 0)
-        load_w("e", w3, 0, 1, 1)
+        for g in range(PASSES):
+            load_w("e", w3, 0, g)
         load_x(1)
-        load_w("e", w3, 1, 1, 0)
-        load_w("e", w3, 1, 1, 1)
+        for g in range(PASSES):
+            load_w("e", w3, 1, g)
         for tile, src in reversed(list(zip(pos_t, (pos1, pos2, pos3)))):
             nc.sync.dma_start(tile[:], src)
         for name, w, first in (("e", w3, 2), ("a", w1, 0)):
             for t in range(first, TILES):
                 for g in range(PASSES):
-                    load_w(name, w, t, 1, g)
-        load_w("o", w2, 0, 1, 0)
+                    load_w(name, w, t, g)
+        load_w("o", w2, 0, 0)
 
         warm = sb("warm", [P, 2], F32)
         nc.vector.memset(warm[:, 0:1], 1.0)
@@ -87,254 +108,241 @@ def tile_picked_ycovn_corr_p_kernel(tc, x_words, x_scales, w1, w3, w2, offs, pos
 
         xg = [sb("xg%d" % g, [P, S], U32) for g in range(PASSES)]
         xsg = sb("xsg", [P, S], U8)
-        stage = {}
 
-        def cast(name, t, g, st=None, copy=nc.scalar.copy):
-            src = raw[(name, t, g)]
-            if st is None:
-                st = sb("stage_%s_%d_%d" % (name, t, g), [P, src.shape[1]], BF16)[:]
+        def gather_x(g, lo, hi):
+            window = xw[g][:].bitcast(U32)
+            nc.vector.tensor_copy(xg[g][:, lo:hi], window.indirect(offs_t[:, lo // GROUP : hi // GROUP]))
+
+        def cast(copy, dst, src):
             copy(
-                st.rearrange("p (c i j) -> p c j i", i=4, j=PACK),
-                src[:].rearrange("p (j c i) -> p c j i", j=PACK, i=4),
+                dst.rearrange("p (c run j) -> p c j run", run=RUN, j=PACK),
+                src[:].rearrange("p (j c run) -> p c j run", j=PACK, run=RUN),
             )
-            stage[(name, t, g)] = st
 
-        def quant(name, src):
-            width = src.shape[1] // PACK
-            codes = sb("codes_" + name, [P, width], U32)
-            scales = sb("scales_" + name, [P, width], U8)
+        def quantise(name, src):
+            codes = sb("codes_" + name, [P, src.shape[1] // PACK], U32)
+            scales = sb("scales_" + name, [P, src.shape[1] // PACK], U8)
             nc.vector.quantize_mx(out=codes[:].bitcast(FP8X4), scales=scales[:], in_=src)
             return codes, scales
 
-        acc = {("e", 1): 2, ("e", 2): 3, ("e", 3): 0, ("a", 0): 1, ("a", 1): 2, ("a", 2): 3, ("a", 3): 0}
+        def one_pass(t, g, copy):
+            tag = "e_%d_%d" % (t, g)
+            staged = sb("stage_" + tag, [P, K_PASS], BF16)[:]
+            cast(copy, staged, raw[("e", t, g)])
+            return quantise(tag, staged)
 
-        def mx(dst, codes, scales, g, cols):
+        def project(dst, codes, scales, g, lo, hi):
             nc.tensor.matmul_mx(
-                out=dst,
-                lhsT=codes.bitcast(FP8X4),
-                lhsT_scale=scales,
-                rhs=xg[g][:, cols].bitcast(FP8X4),
-                rhs_scale=xsg[4 * g : P, cols],
+                out=dst[:, lo:hi],
+                lhsT=codes[:].bitcast(FP8X4),
+                lhsT_scale=scales[:],
+                rhs=xg[g][:, lo:hi].bitcast(FP8X4),
+                rhs_scale=xsg[ROWS * g : P, lo:hi],
                 start=(g == 0),
                 stop=(g == PASSES - 1),
             )
 
-        first = ((0, 0, V), (1, V, V + P), (4, V + P, S))
-
-        def gather_x(g, lo, hi):
-            nc.vector.tensor_copy(xg[g][:, lo:hi], xw[g][:].bitcast(U32).indirect(offs_t[:, lo // 16 : hi // 16]))
-
-        def quant_mm(name, t0, g):
-            codes, scales = quant("%s_%d_%d" % (name, t0, g), stage[(name, t0, g)])
-            for i in range(codes.shape[1] // P):
-                cols = slice(i * P, (i + 1) * P)
-                if (name, t0) == ("e", 0):
-                    for b, lo, hi in first:
-                        if g == 1:
-                            gather_x(1, lo, hi)
-                        mx(bank[b][:, lo:hi], codes[:, cols], scales[:, cols], g, slice(lo, hi))
-                else:
-                    mx(bank[acc[(name, t0 + i)]][:], codes[:, cols], scales[:, cols], g, slice(0, S))
-
         def weights(name, t):
-            staged = sb("stage_%s_%d" % (name, t), [P, PASSES * K_PASS], BF16)
+            tag = "%s_%d" % (name, t)
+            staged = sb("stage_" + tag, [P, PASSES * K_PASS], BF16)
             for g in range(PASSES):
-                cast(name, t, g, staged[:, g * K_PASS : (g + 1) * K_PASS])
-            codes, scales = quant("%s_%d" % (name, t), staged[:])
+                cast(nc.scalar.copy, staged[:, g * K_PASS : (g + 1) * K_PASS], raw[(name, t, g)])
+            codes, scales = quantise(tag, staged[:])
             for g in range(PASSES):
-                cols = slice(g * P, (g + 1) * P)
-                mx(bank[acc[(name, t)]][:], codes[:, cols], scales[:, cols], g, slice(0, S))
+                project(bank[ACC_BANK[(name, t)]], block(codes, g), block(scales, g), g, 0, S)
 
-        win = {(name, t): sb("win_%s_%d" % (name, t), [P, S], F32) for name in "ea" for t in range(TILES)}
+        win = {
+            (name, t): raw[("e", 2, 0)] if (name, t) == ("e", 1) else sb("win_%s_%d" % (name, t), [P, S], F32)
+            for name in "ea"
+            for t in range(TILES)
+        }
 
-        win[("e", 1)] = raw[("e", 2, 0)]
-
-        def evac(name, t):
-            nc.scalar.copy(win[(name, t)][:], bank[acc[(name, t)]][:])
+        def empty(name, t):
+            nc.scalar.copy(win[(name, t)][:], bank[ACC_BANK[(name, t)]][:])
 
         def add_transposed(dst, srcs):
-            for i, s in enumerate(srcs):
+            for i, src in enumerate(srcs):
                 nc.tensor.matmul(
-                    dst, lhsT=s, rhs=ident[:], is_transpose=True, start=(i == 0), stop=(i == len(srcs) - 1)
+                    dst, lhsT=src, rhs=ident[:], is_transpose=True, start=(i == 0), stop=(i == len(srcs) - 1)
                 )
 
-        def block(ap, h):
-            return ap[:, h * P : (h + 1) * P]
-
         e0 = [sb("e0_%d" % t, [P, V], F32)[:] for t in range(TILES)]
-        c0_t = [sb("c0_%d" % hf, [P, 2 * V], F32) for hf in range(2)]
-        dif = {}
-        coef = {}
+        c0_t = [sb("c0_%d" % t, [P, V], F32)[:] for t in range(LAST)]
         dif_on = (sb("dif_0", [P, 2 * V], F32), raw[("e", 3, 1)], raw[("a", 1, 1)], raw[("a", 3, 1)])
-        coef_on = (raw[("e", 2, 1)], raw[("a", 0, 1)], raw[("a", 2, 1)], sb("coef_3", [P, 2 * V], F32))
-        for t in range(TILES):
-            for n in (1, 2):
-                dif[(n, t)] = at(dif_on[t], n - 1)
-                coef[(n, t)] = at(coef_on[t], n - 1)
-        for t in range(TILES):
-            coef[(0, t)] = at(c0_t[t // 2], t % 2)
-
+        coef_on = (raw[("e", 2, 1)], raw[("a", 0, 1)], raw[("a", 2, 1)])
+        dif = {(n, t): slot(dif_on[t], n - 1) for n in (1, 2) for t in range(TILES)}
+        coef = {(n, t): slot(coef_on[t], n - 1) for n in (1, 2) for t in range(LAST)}
+        coef.update({(0, t): c0_t[t] for t in range(LAST)})
         last_c = sb("last_c", [P, 2 * V], F32)
-        coef[(0, 3)], coef[(2, 3)] = at(last_c, 0), at(last_c, 1)
+        coef[(0, LAST)], coef[(2, LAST)] = slot(last_c, 0), slot(last_c, 1)
+        coef[(1, LAST)] = sb("coef_3", [P, V], F32)[:]
 
         def pick(t):
             nc.vector.tensor_copy(e0[t], win[("e", t)][:].indirect(pos_t[0][:]))
 
-        def diff(t, n):
-            nc.vector.tensor_tensor(dif[(n, t)], win[("e", t)][:].indirect(pos_t[n][:]), e0[t], ALU.subtract)
+        def differences(t):
+            for n in (1, 2):
+                nc.vector.tensor_tensor(dif[(n, t)], win[("e", t)][:].indirect(pos_t[n][:]), e0[t], ALU.subtract)
 
-        def centre(c1, c2, d1, d2):
-            nc.vector.scalar_tensor_tensor(c1, d1, 2.0, d2, ALU.mult, ALU.subtract)
-            nc.vector.scalar_tensor_tensor(c2, d2, 2.0, d1, ALU.mult, ALU.subtract)
+        def centre(t, which=(1, 2)):
+            for n in which:
+                nc.vector.scalar_tensor_tensor(
+                    coef[(n, t)], dif[(n, t)], 2.0, dif[(3 - n, t)], ALU.mult, ALU.subtract
+                )
 
-        def centre_tile(t):
-            centre(coef[(1, t)], coef[(2, t)], dif[(1, t)], dif[(2, t)])
+        negated = [sb("neg_%d" % pair, [P, 2 * V], F32) for pair in range(2)]
 
-        neg = [sb("neg_%d" % hf, [P, 2 * V], F32) for hf in range(2)]
-
-        def turned_sum(tiles, turned):
+        def turned_sum(trip):
+            tiles, b = TRIPS[trip]
             for i, t in enumerate(tiles):
-                for h in range(VH):
-                    add_transposed(block(turned, i * VH + h), [block(dif[(n, t)], h) for n in (1, 2)])
+                for h in range(HALVES):
+                    add_transposed(block(bank[b], i * HALVES + h), [block(dif[(n, t)], h) for n in (1, 2)])
 
-        def negated_sum(tiles, turned, homes):
-            negated = at(neg[tiles[0] // 2], tiles[0] % 2, len(tiles))
-            nc.scalar.activation(negated, at(turned, 0, len(tiles)), ACT.Copy, scale=-1.0)
-            for i, home in enumerate(homes):
-                for h in range(VH):
-                    nc.tensor.transpose(block(home, h), block(negated, i * VH + h), ident[:])
+        def turn_back(trip):
+            tiles, b = TRIPS[trip]
+            lo = tiles[0] % 2 * V
+            minus = negated[tiles[0] // 2][:, lo : lo + len(tiles) * V]
+            nc.scalar.activation(minus, bank[b][:, 0 : len(tiles) * V], ACT.Copy, scale=-1.0)
+            for i, t in enumerate(tiles):
+                for h in range(HALVES):
+                    nc.tensor.transpose(block(bank[C0_BANK[t]], h), block(minus, i * HALVES + h), ident[:])
 
-        home = (bank[4], bank[5], bank[7], bank[6])
-
-        def centre0(t):
-            nc.scalar.copy(coef[(0, t)], at(home[t], 0))
+        def fetch_c0(t):
+            nc.scalar.copy(coef[(0, t)], slot(bank[C0_BANK[t]], 0))
 
         sq = (raw[("a", 2, 0)], raw[("a", 3, 0)], raw[("a", 1, 0)], sb("sq_3", [P, 2 * V], F32))
-        root = sb("root", [P, VH * H], F32)
-
-        var_bank = (1, 7)
+        root = sb("root", [P, HALVES * H], F32)
 
         def squares(t):
-            nc.scalar.activation(at(sq[t], 0), dif[(2, t)], ACT.Square, scale=math.sqrt(3.0))
-            nc.scalar.activation(at(sq[t], 1), coef[(1, t)], ACT.Square)
+            nc.scalar.activation(slot(sq[t], 0), dif[(2, t)], ACT.Square, scale=math.sqrt(3.0))
+            nc.scalar.activation(slot(sq[t], 1), coef[(1, t)], ACT.Square)
 
-        def add_squares(hf):
-            for h in range(VH):
+        def variance(pair):
+            for h in range(HALVES):
                 for i in range(2):
-                    add_transposed(block(bank[var_bank[hf]], h * 2 + i), [block(at(sq[2 * hf + i], o), h) for o in range(2)])
+                    terms = [block(slot(sq[2 * pair + i], which), h) for which in range(2)]
+                    add_transposed(block(bank[VAR_BANK[pair]], 2 * h + i), terms)
 
-        def inverse_root(hf):
+        def inverse_root(pair):
             nc.scalar.activation(
-                root[:].rearrange("v (h i) -> v h i", h=VH)[:, :, hf * V : (hf + 1) * V],
-                bank[var_bank[hf]][:].rearrange("v (h i) -> v h i", h=VH),
+                root[:].rearrange("v (h i) -> v h i", h=HALVES)[:, :, pair * 2 * P : (pair + 1) * 2 * P],
+                bank[VAR_BANK[pair]][:].rearrange("v (h i) -> v h i", h=HALVES),
                 ACT.Abs_reciprocal_sqrt,
                 bias=8.1,
                 scale=4.5,
             )
 
-        m = {(t, n): sb("m_%d_%d" % (t, n), [P, V], F32)[:] for t in range(TILES) for n in range(3)}
+        prod = {(t, n): sb("m_%d_%d" % (t, n), [P, V], F32)[:] for t in range(TILES) for n in range(3)}
 
         def z_of(t, h):
-            return block(bank[4 + h], t) if t < TILES - 1 else block(bank[3 - h], 0)
+            return block(bank[SUM_BANK[h]], t) if t < LAST else block(bank[LAST_SUM_BANK[h]], 0)
 
         def products(t):
             for n in ORDER:
-                nc.vector.tensor_tensor(m[(t, n)], win[("a", t)][:].indirect(pos_t[n][:]), coef[(n, t)], ALU.mult)
-            for k, n in enumerate(ORDER):
-                for h in range(VH):
+                nc.vector.tensor_tensor(prod[(t, n)], win[("a", t)][:].indirect(pos_t[n][:]), coef[(n, t)], ALU.mult)
+            for n in ORDER:
+                for h in range(HALVES):
                     nc.tensor.matmul(
-                        z_of(t, h), lhsT=block(m[(t, n)], h), rhs=ident[:], is_transpose=True, start=(k == 0), stop=(k == 2)
+                        z_of(t, h),
+                        lhsT=block(prod[(t, n)], h),
+                        rhs=ident[:],
+                        is_transpose=True,
+                        start=(n == ORDER[0]),
+                        stop=(n == ORDER[-1]),
                     )
 
-        rrT = [sb("rrT%d" % h, [P, H], BF16) for h in range(VH)]
+        rr_turned = [sb("rrT%d" % h, [P, H], BF16) for h in range(HALVES)]
 
-        def scale(h, t0, tiles, z):
-            q0, q1 = t0 * 32, (t0 + tiles) * 32
+        def scale(h, first, tiles, z):
+            lo, hi = first * P, (first + tiles) * P
             nc.vector.tensor_tensor(
-                rrT[h][:].rearrange("v (u p e) -> v u p e", u=2, e=2)[:, :, q0:q1, :],
-                z.rearrange("v (p u e) -> v u p e", u=2, e=2),
-                root[:, h * H + t0 * P : h * H + (t0 + tiles) * P].rearrange("v (p u e) -> v u p e", u=2, e=2),
+                rr_turned[h][:].rearrange("v (u p s) -> v u p s", u=2, s=2)[:, :, lo // PACK : hi // PACK, :],
+                z.rearrange("v (p u s) -> v u p s", u=2, s=2),
+                root[:, h * H + lo : h * H + hi].rearrange("v (p u s) -> v u p s", u=2, s=2),
                 ALU.mult,
             )
 
         gather_x(0, 0, S)
         nc.vector.tensor_copy(xsg[:], xs[:].indirect(offs_t[:]))
-        cast("e", 0, 0)
-        quant_mm("e", 0, 0)
-        cast("e", 0, 1)
-        quant_mm("e", 0, 1)
-        for b, lo, hi in first:
+        codes, scales = one_pass(0, 0, nc.scalar.copy)
+        for b, lo, hi in FIRST_PIECES:
+            project(bank[b], codes, scales, 0, lo, hi)
+        codes, scales = one_pass(0, 1, nc.scalar.copy)
+        for b, lo, hi in FIRST_PIECES:
+            gather_x(1, lo, hi)
+            project(bank[b], codes, scales, 1, lo, hi)
+        for b, lo, hi in FIRST_PIECES:
             nc.scalar.copy(win[("e", 0)][:, lo:hi], bank[b][:, lo:hi])
-        cast("e", 1, 0, copy=nc.vector.tensor_copy)
-        quant_mm("e", 1, 0)
-        cast("e", 1, 1, copy=nc.vector.tensor_copy)
-        quant_mm("e", 1, 1)
+        for g in range(PASSES):
+            project(bank[ACC_BANK[("e", 1)]], *one_pass(1, g, nc.vector.tensor_copy), g, 0, S)
+
         pick(0)
-        diff(0, 1)
-        diff(0, 2)
+        differences(0)
         weights("e", 2)
-        centre_tile(0)
-        for t, first_w, second_w in ((1, ("e", 3), ("a", 0)), (2, ("a", 1), ("a", 2))):
-            evac("e", t)
+        centre(0)
+        for t, after_pick, after_differences in ((1, ("e", 3), ("a", 0)), (2, ("a", 1), ("a", 2))):
+            empty("e", t)
             pick(t)
-            weights(*first_w)
-            diff(t, 1)
-            diff(t, 2)
-            weights(*second_w)
-            centre_tile(t)
-        turned_sum((0, 1), bank[6])
-        turned_sum((2,), bank[7])
-        evac("e", 3)
-        pick(3)
-        weights("a", 3)
-        diff(3, 1)
-        diff(3, 2)
-        evac("a", 0)
-        negated_sum((0, 1), bank[6], home[:2])
-        turned_sum((3,), bank[6])
-        for h in range(VH):
-            nc.tensor.transpose(block(bank[6], VH + h), block(dif[(2, 3)], h), ident[:])
-        nc.vector.scalar_tensor_tensor(coef[(1, 3)], dif[(1, 3)], 2.0, dif[(2, 3)], ALU.mult, ALU.subtract)
-        negated_sum((2,), bank[7], home[2:3])
+            weights(*after_pick)
+            differences(t)
+            weights(*after_differences)
+            centre(t)
+        turned_sum(0)
+        turned_sum(1)
+        empty("e", LAST)
+        pick(LAST)
+        weights("a", LAST)
+        differences(LAST)
+
+        empty("a", 0)
+        turn_back(0)
+        turned_sum(2)
+        last_bank = bank[C0_BANK[LAST]]
+        for h in range(HALVES):
+            nc.tensor.transpose(block(last_bank, HALVES + h), block(dif[(2, LAST)], h), ident[:])
+        centre(LAST, (1,))
+        turn_back(1)
         squares(0)
         squares(1)
-        add_squares(0)
-        for t in range(3):
-            centre0(t)
+        variance(0)
+        for t in range(LAST):
+            fetch_c0(t)
         products(0)
-        evac("a", 1)
+        empty("a", 1)
         thrice = sb("thrice", [P, V], F32)
-        nc.scalar.activation(thrice[:], at(bank[6], 1), ACT.Copy, scale=3.0)
-        negated_sum((3,), bank[6], home[3:])
-        for h in range(VH):
-            add_transposed(block(bank[6], VH + h), [block(thrice, h), block(at(neg[1], 1), h)])
-        evac("a", 2)
+        nc.scalar.activation(thrice[:], slot(last_bank, 1), ACT.Copy, scale=3.0)
+        turn_back(2)
+        for h in range(HALVES):
+            add_transposed(block(last_bank, HALVES + h), [block(thrice, h), block(slot(negated[1], 1), h)])
+        empty("a", 2)
         squares(2)
-        squares(3)
-        add_squares(1)
+        squares(LAST)
+        variance(1)
         products(1)
         products(2)
-        evac("a", 3)
-        nc.scalar.copy(last_c[:], bank[6][:])
+        empty("a", LAST)
+        nc.scalar.copy(last_c[:], last_bank[:])
         inverse_root(0)
         inverse_root(1)
-        products(3)
-        cast("o", 0, 0, m[(3, 2)].bitcast(BF16))
-        for h in range(VH):
-            scale(h, 0, TILES - 1, bank[4 + h][:, 0 : (TILES - 1) * P])
-        for h in range(VH):
-            scale(h, TILES - 1, 1, z_of(TILES - 1, h))
-        w2_codes, w2_scales = quant("w2", stage[("o", 0, 0)])
+        products(LAST)
 
-        for h in range(VH):
-            words = rrT[h][:].bitcast(F32)
-            back = bank[h][:, 0 : 2 * P].rearrange("p (u v) -> p u v", u=2)
+        w2_staged = prod[(LAST, 2)].bitcast(BF16)
+        cast(nc.scalar.copy, w2_staged, raw[("o", 0, 0)])
+        for h in range(HALVES):
+            scale(h, 0, LAST, bank[SUM_BANK[h]][:, 0 : LAST * P])
+        for h in range(HALVES):
+            scale(h, LAST, 1, z_of(LAST, h))
+        w2_codes, w2_scales = quantise("w2", w2_staged)
+
+        for h, store in zip(range(HALVES), (nc.sync, nc.scalar)):
+            words = rr_turned[h][:].bitcast(F32)
+            back = bank[BACK_BANK[h]][:, 0 : 2 * P].rearrange("p (u v) -> p u v", u=2)
             for u in range(2):
                 nc.tensor.transpose(back[:, u, :], block(words, u), ident[:])
             rr = sb("rr%d" % h, [P, P * PACK], BF16)
             nc.scalar.copy(rr[:].bitcast(F32).rearrange("p (v u) -> p v u", u=2), back.rearrange("p u v -> p v u"))
-            rr_codes, rr_scales = quant("rr%d" % h, rr[:])
-            res = block(bank[6 + h], 0)
+            rr_codes, rr_scales = quantise("rr%d" % h, rr[:])
+            res = block(bank[OUT_BANK[h]], 0)
             nc.tensor.matmul_mx(
                 out=res,
                 lhsT=w2_codes[:].bitcast(FP8X4),
@@ -346,4 +354,4 @@ def tile_picked_ycovn_corr_p_kernel(tc, x_words, x_scales, w1, w3, w2, offs, pos
             )
             res_sb = sb("res_sb%d" % h, [P, P], F32)
             nc.scalar.copy(res_sb[:], res)
-            (nc.sync if h == 0 else nc.scalar).dma_start(out[:, h * P : (h + 1) * P], res_sb[:])
+            store.dma_start(block(out, h), res_sb[:])

@@ -31,15 +31,31 @@ BANKS = 8
 RUN = 4
 ORDER = (1, 2, 0)
 
-ACC_BANK = {("e", 1): 2, ("e", 2): 3, ("e", 3): 0, ("a", 0): 1, ("a", 1): 2, ("a", 2): 3, ("a", 3): 0}
+RAW_BYTES = 2048
+LATER = (("e", 2), ("a", 0), ("e", 3), ("a", 1), ("a", 2), ("a", 3))
+ACC_BANK = {("e", 1): 2, ("e", 2): 3, ("a", 0): 2, ("e", 3): 3, ("a", 1): 0, ("a", 2): 2, ("a", 3): 3}
 FIRST_PIECES = ((0, 0, V), (1, V, V + P), (4, V + P, S))
 SUM_BANK = (4, 5)
 LAST_SUM_BANK = (3, 2)
-TRIPS = (((0, 1), 6), ((2,), 7), ((3,), 6))
-C0_BANK = (4, 5, 7, 6)
-VAR_BANK = (1, 7)
+TURN_BANK, RETURN_BANK = 6, 7
+VAR_BANK = (1, 0)
 BACK_BANK = (0, 1)
 OUT_BANK = (6, 7)
+BOTH = ()
+DIF_HOLD = {
+    (1, 0): None, (2, 0): None,
+    (1, 1): (("a", 0, 0), "mid"), (2, 1): (("a", 0, 1), "mid"),
+    (1, 2): (("e", 3, 1), "mid"), (2, 2): (("e", 3, 1), "high"),
+    (1, 3): (("a", 3, 1), "mid"), (2, 3): (("a", 3, 1), "high"),
+}
+COEF_HOLD = {
+    (1, 0): (("e", 2, 1), "mid"), (2, 0): (("a", 0, 0), "low"),
+    (1, 1): (("e", 3, 1), "low"), (2, 1): (("e", 3, 0), "mid"),
+    (1, 2): (("a", 2, 1), "low"), (2, 2): (("a", 2, 1), "mid"),
+    (1, 3): (("e", 3, 1), "mid"), (2, 3): (("e", 3, 1), "high"),
+    (0, 0): None, (0, 1): None, (0, 2): None, (0, 3): None,
+}
+SQ_HOLD = {0: (("a", 3, 0), "low"), 1: (("a", 3, 0), "high"), 2: (("a", 3, 1), "low"), 3: None}
 
 
 def tile_picked_ycovn_corr_p_kernel(
@@ -48,6 +64,7 @@ def tile_picked_ycovn_corr_p_kernel(
     nc = tc.nc
     with ExitStack() as ctx:
         keep = ctx.enter_context(tc.tile_pool(name="keep", bufs=1))
+        shared = ctx.enter_context(tc.tile_pool(name="shared", bufs=1))
         psum = ctx.enter_context(tc.psum_pool(name="psum", bufs=1))
 
         def sb(name, shape, dtype):
@@ -66,9 +83,17 @@ def tile_picked_ycovn_corr_p_kernel(
         xw = [sb("xw%d" % g, [P, T], I32) for g in range(PASSES)]
         xs = sb("xs", [P, T], U8)
         raw = {}
+        place = {}
+
+        def after(key, where, name, cols):
+            start = {"low": RAW_BYTES // 4 - 4 * cols, "mid": RAW_BYTES // 4, "high": 3 * RAW_BYTES // 4}[where]
+            return shared.tile([P, cols], F32, name=name, offset=place[key] + start, align_bytes=64)
 
         def load_w(name, w, t, g):
-            tile = sb("raw_%s_%d_%d" % (name, t, g), [P, PACK * P], F32)
+            place[(name, t, g)] = (3 * len(place) + 1) * RAW_BYTES
+            tile = shared.tile(
+                [P, PACK * P], F32, name="raw_%s_%d_%d" % (name, t, g), offset=place[(name, t, g)], align_bytes=64
+            )
             rows = w[g * K_PASS : (g + 1) * K_PASS, t * P : (t + 1) * P]
             nc.sync.dma_start(
                 tile[:].rearrange("p (j c) -> p j c", j=PACK), rows.rearrange("(p j) c -> p j c", j=PACK)
@@ -93,10 +118,9 @@ def tile_picked_ycovn_corr_p_kernel(
             load_w("e", w3, 1, g)
         for tile, src in reversed(list(zip(pos_t, (pos1, pos2, pos3)))):
             nc.sync.dma_start(tile[:], src)
-        for name, w, first in (("e", w3, 2), ("a", w1, 0)):
-            for t in range(first, TILES):
-                for g in range(PASSES):
-                    load_w(name, w, t, g)
+        for name, t in LATER:
+            for g in range(PASSES):
+                load_w(name, w3 if name == "e" else w1, t, g)
         load_w("o", w2, 0, 0)
 
         warm = sb("warm", [P, 2], F32)
@@ -142,20 +166,22 @@ def tile_picked_ycovn_corr_p_kernel(
                 stop=(g == PASSES - 1),
             )
 
-        def weights(name, t):
-            tag = "%s_%d" % (name, t)
-            staged = sb("stage_" + tag, [P, PASSES * K_PASS], BF16)
+        def stage(name, t):
+            staged = sb("stage_%s_%d" % (name, t), [P, PASSES * K_PASS], BF16)
             for g in range(PASSES):
                 cast(nc.scalar.copy, staged[:, g * K_PASS : (g + 1) * K_PASS], raw[(name, t, g)])
-            codes, scales = quantise(tag, staged[:])
+            return staged
+
+        def multiply(name, t, staged):
+            codes, scales = quantise("%s_%d" % (name, t), staged[:])
             for g in range(PASSES):
                 project(bank[ACC_BANK[(name, t)]], block(codes, g), block(scales, g), g, 0, S)
 
-        win = {
-            (name, t): raw[("e", 2, 0)] if (name, t) == ("e", 1) else sb("win_%s_%d" % (name, t), [P, S], F32)
-            for name in "ea"
-            for t in range(TILES)
-        }
+        def weights(name, t):
+            multiply(name, t, stage(name, t))
+
+        win = {(name, t): sb("win_%s_%d" % (name, t), [P, S], F32) for name, t in (("e", 0),) + LATER}
+        win[("e", 1)] = after(("e", 2, 0), "low", "win_e_1", S)
 
         def empty(name, t):
             nc.scalar.copy(win[(name, t)][:], bank[ACC_BANK[(name, t)]][:])
@@ -167,61 +193,67 @@ def tile_picked_ycovn_corr_p_kernel(
                 )
 
         e0 = [sb("e0_%d" % t, [P, V], F32)[:] for t in range(TILES)]
-        c0_t = [sb("c0_%d" % t, [P, V], F32)[:] for t in range(LAST)]
-        dif_on = (sb("dif_0", [P, 2 * V], F32), raw[("e", 3, 1)], raw[("a", 1, 1)], raw[("a", 3, 1)])
-        coef_on = (raw[("e", 2, 1)], raw[("a", 0, 1)], raw[("a", 2, 1)])
-        dif = {(n, t): slot(dif_on[t], n - 1) for n in (1, 2) for t in range(TILES)}
-        coef = {(n, t): slot(coef_on[t], n - 1) for n in (1, 2) for t in range(LAST)}
-        coef.update({(0, t): c0_t[t] for t in range(LAST)})
-        last_c = sb("last_c", [P, 2 * V], F32)
-        coef[(0, LAST)], coef[(2, LAST)] = slot(last_c, 0), slot(last_c, 1)
-        coef[(1, LAST)] = sb("coef_3", [P, V], F32)[:]
+        dif, coef, sq = {}, {}, {}
+
+        def lay(table, key, name, hold, cols=V):
+            tile = sb(name, [P, cols], F32) if hold is None else after(hold[0], hold[1], name, cols)
+            table[key] = tile[:]
+
+        for (n, t), hold in DIF_HOLD.items():
+            lay(dif, (n, t), "d%d_%d" % (n, t), hold)
+        for (n, t), hold in COEF_HOLD.items():
+            lay(coef, (n, t), "c%d_%d" % (n, t), hold)
+        for t, hold in SQ_HOLD.items():
+            lay(sq, t, "sq_%d" % t, hold, 2 * V)
 
         def pick(t):
             nc.vector.tensor_copy(e0[t], win[("e", t)][:].indirect(pos_t[0][:]))
 
-        def differences(t):
-            for n in (1, 2):
-                nc.vector.tensor_tensor(dif[(n, t)], win[("e", t)][:].indirect(pos_t[n][:]), e0[t], ALU.subtract)
+        def difference(t, n):
+            nc.vector.tensor_tensor(dif[(n, t)], win[("e", t)][:].indirect(pos_t[n][:]), e0[t], ALU.subtract)
 
-        def centre(t, which=(1, 2)):
-            for n in which:
-                nc.vector.scalar_tensor_tensor(
-                    coef[(n, t)], dif[(n, t)], 2.0, dif[(3 - n, t)], ALU.mult, ALU.subtract
-                )
+        def centre(t, n):
+            if n == 2 and t in BOTH:
+                return
+            nc.vector.scalar_tensor_tensor(coef[(n, t)], dif[(n, t)], 2.0, dif[(3 - n, t)], ALU.mult, ALU.subtract)
 
-        negated = [sb("neg_%d" % pair, [P, 2 * V], F32) for pair in range(2)]
+        negated = [sb("neg_%d" % t, [P, V], F32) for t in range(TILES)]
+        thrice = {t: sb("thrice_%d" % t, [P, V], F32) for t in BOTH}
+        for t in BOTH:
+            both = sb("both_%d" % t, [P, 2 * V], F32)
+            coef[(0, t)], coef[(2, t)], coef[("both", t)] = slot(both, 0), slot(both, 1), both[:]
 
-        def turned_sum(trip):
-            tiles, b = TRIPS[trip]
-            for i, t in enumerate(tiles):
+        def turn(t):
+            for h in range(HALVES):
+                add_transposed(block(bank[TURN_BANK], h), [block(dif[(n, t)], h) for n in (1, 2)])
+            if t in BOTH:
                 for h in range(HALVES):
-                    add_transposed(block(bank[b], i * HALVES + h), [block(dif[(n, t)], h) for n in (1, 2)])
+                    add_transposed(block(bank[TURN_BANK], HALVES + h), [block(dif[(2, t)], h)])
 
-        def turn_back(trip):
-            tiles, b = TRIPS[trip]
-            lo = tiles[0] % 2 * V
-            minus = negated[tiles[0] // 2][:, lo : lo + len(tiles) * V]
-            nc.scalar.activation(minus, bank[b][:, 0 : len(tiles) * V], ACT.Copy, scale=-1.0)
-            for i, t in enumerate(tiles):
+        def turn_back(t):
+            nc.scalar.activation(negated[t][:], slot(bank[TURN_BANK], 0), ACT.Copy, scale=-1.0)
+            if t in BOTH:
+                nc.scalar.activation(thrice[t][:], slot(bank[TURN_BANK], 1), ACT.Copy, scale=3.0)
+            for h in range(HALVES):
+                nc.tensor.transpose(block(bank[RETURN_BANK], h), block(negated[t], h), ident[:])
+            if t in BOTH:
                 for h in range(HALVES):
-                    nc.tensor.transpose(block(bank[C0_BANK[t]], h), block(minus, i * HALVES + h), ident[:])
+                    add_transposed(block(bank[RETURN_BANK], HALVES + h), [block(thrice[t], h), block(negated[t], h)])
 
-        def fetch_c0(t):
-            nc.scalar.copy(coef[(0, t)], slot(bank[C0_BANK[t]], 0))
+        def fetch(t):
+            if t in BOTH:
+                nc.scalar.copy(coef[("both", t)], bank[RETURN_BANK][:])
+            else:
+                nc.scalar.copy(coef[(0, t)], slot(bank[RETURN_BANK], 0))
 
-        sq = (raw[("a", 2, 0)], raw[("a", 3, 0)], raw[("a", 1, 0)], sb("sq_3", [P, 2 * V], F32))
         root = sb("root", [P, HALVES * H], F32)
 
         def squares(t):
             nc.scalar.activation(slot(sq[t], 0), dif[(2, t)], ACT.Square, scale=math.sqrt(3.0))
             nc.scalar.activation(slot(sq[t], 1), coef[(1, t)], ACT.Square)
-
-        def variance(pair):
             for h in range(HALVES):
-                for i in range(2):
-                    terms = [block(slot(sq[2 * pair + i], which), h) for which in range(2)]
-                    add_transposed(block(bank[VAR_BANK[pair]], 2 * h + i), terms)
+                terms = [block(slot(sq[t], which), h) for which in range(2)]
+                add_transposed(block(bank[VAR_BANK[t // 2]], 2 * h + t % 2), terms)
 
         def inverse_root(pair):
             nc.scalar.activation(
@@ -237,19 +269,19 @@ def tile_picked_ycovn_corr_p_kernel(
         def z_of(t, h):
             return block(bank[SUM_BANK[h]], t) if t < LAST else block(bank[LAST_SUM_BANK[h]], 0)
 
-        def products(t):
-            for n in ORDER:
-                nc.vector.tensor_tensor(prod[(t, n)], win[("a", t)][:].indirect(pos_t[n][:]), coef[(n, t)], ALU.mult)
-            for n in ORDER:
-                for h in range(HALVES):
-                    nc.tensor.matmul(
-                        z_of(t, h),
-                        lhsT=block(prod[(t, n)], h),
-                        rhs=ident[:],
-                        is_transpose=True,
-                        start=(n == ORDER[0]),
-                        stop=(n == ORDER[-1]),
-                    )
+        def product(t, n):
+            nc.vector.tensor_tensor(prod[(t, n)], win[("a", t)][:].indirect(pos_t[n][:]), coef[(n, t)], ALU.mult)
+
+        def add_up(t, n):
+            for h in range(HALVES):
+                nc.tensor.matmul(
+                    z_of(t, h),
+                    lhsT=block(prod[(t, n)], h),
+                    rhs=ident[:],
+                    is_transpose=True,
+                    start=(n == ORDER[0]),
+                    stop=(n == ORDER[-1]),
+                )
 
         rr_turned = [sb("rrT%d" % h, [P, H], BF16) for h in range(HALVES)]
 
@@ -277,54 +309,72 @@ def tile_picked_ycovn_corr_p_kernel(
             project(bank[ACC_BANK[("e", 1)]], *one_pass(1, g, nc.vector.tensor_copy), g, 0, S)
 
         pick(0)
-        differences(0)
+        difference(0, 1)
+        difference(0, 2)
         weights("e", 2)
-        centre(0)
-        for t, after_pick, after_differences in ((1, ("e", 3), ("a", 0)), (2, ("a", 1), ("a", 2))):
-            empty("e", t)
-            pick(t)
-            weights(*after_pick)
-            differences(t)
-            weights(*after_differences)
-            centre(t)
-        turned_sum(0)
-        turned_sum(1)
-        empty("e", LAST)
-        pick(LAST)
-        weights("a", LAST)
-        differences(LAST)
-
-        empty("a", 0)
+        centre(0, 1)
+        empty("e", 1)
+        pick(1)
+        turn(0)
+        staged = stage("a", 0)
+        centre(0, 2)
+        difference(1, 1)
+        multiply("a", 0, staged)
+        difference(1, 2)
         turn_back(0)
-        turned_sum(2)
-        last_bank = bank[C0_BANK[LAST]]
-        for h in range(HALVES):
-            nc.tensor.transpose(block(last_bank, HALVES + h), block(dif[(2, LAST)], h), ident[:])
-        centre(LAST, (1,))
+        empty("e", 2)
+        pick(2)
+        turn(1)
+        staged = stage("e", 3)
+        centre(1, 2)
+        multiply("e", 3, staged)
+        centre(1, 1)
+        difference(2, 1)
+        difference(2, 2)
+        fetch(0)
+        weights("a", 1)
+        empty("a", 0)
+        product(0, 1)
+        product(0, 2)
         turn_back(1)
+        turn(2)
+        weights("a", 2)
+        centre(2, 1)
+        centre(2, 2)
+        product(0, 0)
+        empty("e", 3)
+        pick(3)
+        weights("a", 3)
+        difference(3, 1)
+        difference(3, 2)
+        empty("a", 1)
+        fetch(1)
+        product(1, 1)
+        product(1, 2)
+        turn_back(2)
+        turn(3)
         squares(0)
         squares(1)
-        variance(0)
-        for t in range(LAST):
-            fetch_c0(t)
-        products(0)
-        empty("a", 1)
-        thrice = sb("thrice", [P, V], F32)
-        nc.scalar.activation(thrice[:], slot(last_bank, 1), ACT.Copy, scale=3.0)
-        turn_back(2)
-        for h in range(HALVES):
-            add_transposed(block(last_bank, HALVES + h), [block(thrice, h), block(slot(negated[1], 1), h)])
-        empty("a", 2)
         squares(2)
-        squares(LAST)
-        variance(1)
-        products(1)
-        products(2)
-        empty("a", LAST)
-        nc.scalar.copy(last_c[:], last_bank[:])
+        centre(3, 1)
+        centre(3, 2)
+        product(1, 0)
+        fetch(2)
+        empty("a", 2)
+        product(2, 1)
+        product(2, 2)
+        turn_back(3)
+        product(2, 0)
+        empty("a", 3)
+        fetch(3)
+        squares(3)
         inverse_root(0)
         inverse_root(1)
-        products(LAST)
+        for n in ORDER:
+            product(3, n)
+        for t in range(TILES):
+            for n in ORDER:
+                add_up(t, n)
 
         w2_staged = prod[(LAST, 2)].bitcast(BF16)
         cast(nc.scalar.copy, w2_staged, raw[("o", 0, 0)])

@@ -31,31 +31,18 @@ BANKS = 8
 RUN = 4
 ORDER = (1, 2, 0)
 
-RAW_BYTES = 2048
-LATER = (("e", 2), ("a", 0), ("e", 3), ("a", 1), ("a", 2), ("a", 3))
-ACC_BANK = {("e", 1): 2, ("e", 2): 3, ("a", 0): 2, ("e", 3): 3, ("a", 1): 0, ("a", 2): 2, ("a", 3): 3}
+LATER = (("e", 2), ("e", 3), ("a", 0), ("a", 1), ("a", 2), ("a", 3))
+ACC_BANK = {("e", 1): 2, ("e", 2): 3, ("e", 3): 0, ("a", 0): 0, ("a", 1): 3, ("a", 2): 2, ("a", 3): 3}
 FIRST_PIECES = ((0, 0, V), (1, V, V + P), (4, V + P, S))
 SUM_BANK = (4, 5)
-LAST_SUM_BANK = (3, 2)
+LAST_SUM_BANK = (2, 3)
 TURN_BANK, RETURN_BANK = 6, 7
 VAR_BANK = (1, 0)
 BACK_BANK = (0, 1)
 OUT_BANK = (6, 7)
-BOTH = ()
-DIF_HOLD = {
-    (1, 0): None, (2, 0): None,
-    (1, 1): (("a", 0, 0), "mid"), (2, 1): (("a", 0, 1), "mid"),
-    (1, 2): (("e", 3, 1), "mid"), (2, 2): (("e", 3, 1), "high"),
-    (1, 3): (("a", 3, 1), "mid"), (2, 3): (("a", 3, 1), "high"),
-}
-COEF_HOLD = {
-    (1, 0): (("e", 2, 1), "mid"), (2, 0): (("a", 0, 0), "low"),
-    (1, 1): (("e", 3, 1), "low"), (2, 1): (("e", 3, 0), "mid"),
-    (1, 2): (("a", 2, 1), "low"), (2, 2): (("a", 2, 1), "mid"),
-    (1, 3): (("e", 3, 1), "mid"), (2, 3): (("e", 3, 1), "high"),
-    (0, 0): None, (0, 1): None, (0, 2): None, (0, 3): None,
-}
-SQ_HOLD = {0: (("a", 3, 0), "low"), 1: (("a", 3, 0), "high"), 2: (("a", 3, 1), "low"), 3: None}
+KIB = 1024
+RAW_AT = {("e", 2, 0): 2 * KIB, ("a", 2, 1): 48 * KIB, ("a", 3, 0): 52 * KIB, ("a", 3, 1): 56 * KIB}
+TRIP = ()
 
 
 def tile_picked_ycovn_corr_p_kernel(
@@ -83,17 +70,19 @@ def tile_picked_ycovn_corr_p_kernel(
         xw = [sb("xw%d" % g, [P, T], I32) for g in range(PASSES)]
         xs = sb("xs", [P, T], U8)
         raw = {}
-        place = {}
 
-        def after(key, where, name, cols):
-            start = {"low": RAW_BYTES // 4 - 4 * cols, "mid": RAW_BYTES // 4, "high": 3 * RAW_BYTES // 4}[where]
-            return shared.tile([P, cols], F32, name=name, offset=place[key] + start, align_bytes=64)
+        def at(offset, name, cols, dtype=F32):
+            return shared.tile([P, cols], dtype, name=name, offset=offset, align_bytes=64)
+
+        picked = [sb("e_0", [P, 3 * V], F32), sb("e_1", [P, 3 * V], F32), sb("e_2", [P, 3 * V], F32), sb("e_3", [P, 3 * V], F32)]
 
         def load_w(name, w, t, g):
-            place[(name, t, g)] = (3 * len(place) + 1) * RAW_BYTES
-            tile = shared.tile(
-                [P, PACK * P], F32, name="raw_%s_%d_%d" % (name, t, g), offset=place[(name, t, g)], align_bytes=64
-            )
+            if (name, t, g) == ("a", 0, 1):
+                tile = picked[2][:, V : 3 * V]
+            elif (name, t, g) in RAW_AT:
+                tile = at(RAW_AT[(name, t, g)], "raw_%s_%d_%d" % (name, t, g), PACK * P)
+            else:
+                tile = sb("raw_%s_%d_%d" % (name, t, g), [P, PACK * P], F32)
             rows = w[g * K_PASS : (g + 1) * K_PASS, t * P : (t + 1) * P]
             nc.sync.dma_start(
                 tile[:].rearrange("p (j c) -> p j c", j=PACK), rows.rearrange("(p j) c -> p j c", j=PACK)
@@ -143,9 +132,17 @@ def tile_picked_ycovn_corr_p_kernel(
                 src[:].rearrange("p (j c run) -> p c j run", j=PACK, run=RUN),
             )
 
+        CODES_AT = {"e_1_1": 36 * KIB, "a_0": 68 * KIB, "a_1": 62 * KIB + 512}
+
         def quantise(name, src):
-            codes = sb("codes_" + name, [P, src.shape[1] // PACK], U32)
-            scales = sb("scales_" + name, [P, src.shape[1] // PACK], U8)
+            if name in CODES_AT:
+                codes = at(CODES_AT[name], "codes_" + name, src.shape[1] // PACK, U32)
+            else:
+                codes = sb("codes_" + name, [P, src.shape[1] // PACK], U32)
+            if name == "a_1":
+                scales = at(72 * KIB, "scales_a_1", src.shape[1] // PACK, U8)
+            else:
+                scales = sb("scales_" + name, [P, src.shape[1] // PACK], U8)
             nc.vector.quantize_mx(out=codes[:].bitcast(FP8X4), scales=scales[:], in_=src)
             return codes, scales
 
@@ -166,14 +163,22 @@ def tile_picked_ycovn_corr_p_kernel(
                 stop=(g == PASSES - 1),
             )
 
-        def stage(name, t):
-            staged = sb("stage_%s_%d" % (name, t), [P, PASSES * K_PASS], BF16)
+        STAGE_AT = {("e", 3): 36 * KIB, ("a", 0): 6 * KIB, ("a", 1): 30 * KIB, ("a", 2): 64 * KIB, ("a", 3): 72 * KIB}
+
+        def stage(name, t, copies=(nc.scalar.copy, nc.scalar.copy)):
+            tag = "stage_%s_%d" % (name, t)
+            if (name, t) in STAGE_AT:
+                staged = at(STAGE_AT[(name, t)], tag, PASSES * K_PASS, BF16)
+            else:
+                staged = sb(tag, [P, PASSES * K_PASS], BF16)
             for g in range(PASSES):
-                cast(nc.scalar.copy, staged[:, g * K_PASS : (g + 1) * K_PASS], raw[(name, t, g)])
+                cast(copies[g], staged[:, g * K_PASS : (g + 1) * K_PASS], raw[(name, t, g)])
             return staged
 
         def multiply(name, t, staged):
-            codes, scales = quantise("%s_%d" % (name, t), staged[:])
+            passes(name, t, *quantise("%s_%d" % (name, t), staged[:]))
+
+        def passes(name, t, codes, scales):
             for g in range(PASSES):
                 project(bank[ACC_BANK[(name, t)]], block(codes, g), block(scales, g), g, 0, S)
 
@@ -181,7 +186,7 @@ def tile_picked_ycovn_corr_p_kernel(
             multiply(name, t, stage(name, t))
 
         win = {(name, t): sb("win_%s_%d" % (name, t), [P, S], F32) for name, t in (("e", 0),) + LATER}
-        win[("e", 1)] = after(("e", 2, 0), "low", "win_e_1", S)
+        win[("e", 1)] = at(KIB, "win_e_1", S)
 
         def empty(name, t):
             nc.scalar.copy(win[(name, t)][:], bank[ACC_BANK[(name, t)]][:])
@@ -192,67 +197,55 @@ def tile_picked_ycovn_corr_p_kernel(
                     dst, lhsT=src, rhs=ident[:], is_transpose=True, start=(i == 0), stop=(i == len(srcs) - 1)
                 )
 
-        e0 = [sb("e0_%d" % t, [P, V], F32)[:] for t in range(TILES)]
-        dif, coef, sq = {}, {}, {}
+        coef = [at(7 * KIB, "c_0", 3 * V), sb("c_1", [P, 3 * V], F32), sb("c_2", [P, 3 * V], F32), at(31 * KIB, "c_3", 3 * V)]
+        mean = [sb("mean_0", [P, V], F32), sb("mean_1", [P, V], F32)]
+        turned = [sb("turned_0", [P, 2 * V], F32)] + [at(o * KIB + 64, "turned_%d" % o, 2 * V) for o in (28, 62, 42)]
+        sq = [at(o * KIB, "sq_%d" % t, 3 * V) for t, o in enumerate((68, 52, 56))] + [sb("sq_3", [P, 3 * V], F32)]
 
-        def lay(table, key, name, hold, cols=V):
-            tile = sb(name, [P, cols], F32) if hold is None else after(hold[0], hold[1], name, cols)
-            table[key] = tile[:]
-
-        for (n, t), hold in DIF_HOLD.items():
-            lay(dif, (n, t), "d%d_%d" % (n, t), hold)
-        for (n, t), hold in COEF_HOLD.items():
-            lay(coef, (n, t), "c%d_%d" % (n, t), hold)
-        for t, hold in SQ_HOLD.items():
-            lay(sq, t, "sq_%d" % t, hold, 2 * V)
-
-        def pick(t):
-            nc.vector.tensor_copy(e0[t], win[("e", t)][:].indirect(pos_t[0][:]))
-
-        def difference(t, n):
-            nc.vector.tensor_tensor(dif[(n, t)], win[("e", t)][:].indirect(pos_t[n][:]), e0[t], ALU.subtract)
-
-        def centre(t, n):
-            if n == 2 and t in BOTH:
-                return
-            nc.vector.scalar_tensor_tensor(coef[(n, t)], dif[(n, t)], 2.0, dif[(3 - n, t)], ALU.mult, ALU.subtract)
-
-        negated = [sb("neg_%d" % t, [P, V], F32) for t in range(TILES)]
-        thrice = {t: sb("thrice_%d" % t, [P, V], F32) for t in BOTH}
-        for t in BOTH:
-            both = sb("both_%d" % t, [P, 2 * V], F32)
-            coef[(0, t)], coef[(2, t)], coef[("both", t)] = slot(both, 0), slot(both, 1), both[:]
+        def pick(t, n):
+            nc.vector.tensor_copy(slot(picked[t], n), win[("e", t)][:].indirect(pos_t[n][:]))
 
         def turn(t):
             for h in range(HALVES):
-                add_transposed(block(bank[TURN_BANK], h), [block(dif[(n, t)], h) for n in (1, 2)])
-            if t in BOTH:
+                add_transposed(block(bank[TURN_BANK], h), [block(slot(picked[t], n), h) for n in range(3)])
+            if t in TRIP:
                 for h in range(HALVES):
-                    add_transposed(block(bank[TURN_BANK], HALVES + h), [block(dif[(2, t)], h)])
+                    add_transposed(block(bank[TURN_BANK], HALVES + h), [block(slot(picked[t], 0), h)])
 
         def turn_back(t):
-            nc.scalar.activation(negated[t][:], slot(bank[TURN_BANK], 0), ACT.Copy, scale=-1.0)
-            if t in BOTH:
-                nc.scalar.activation(thrice[t][:], slot(bank[TURN_BANK], 1), ACT.Copy, scale=3.0)
+            nc.scalar.activation(slot(turned[t], 0), slot(bank[TURN_BANK], 0), ACT.Copy, scale=-1.0 / 3.0)
+            if t in TRIP:
+                nc.scalar.copy(slot(turned[t], 1), slot(bank[TURN_BANK], 1))
             for h in range(HALVES):
-                nc.tensor.transpose(block(bank[RETURN_BANK], h), block(negated[t], h), ident[:])
-            if t in BOTH:
+                nc.tensor.transpose(block(bank[RETURN_BANK], h), block(turned[t], h), ident[:])
+            if t in TRIP:
                 for h in range(HALVES):
-                    add_transposed(block(bank[RETURN_BANK], HALVES + h), [block(thrice[t], h), block(negated[t], h)])
+                    add_transposed(block(bank[RETURN_BANK], HALVES + h), [block(turned[t], HALVES + h), block(turned[t], h)])
+
+        def thirds(ap, lo):
+            return ap[:, lo * V : 3 * V].rearrange("p (n v) -> p n v", v=V)
 
         def fetch(t):
-            if t in BOTH:
-                nc.scalar.copy(coef[("both", t)], bank[RETURN_BANK][:])
-            else:
-                nc.scalar.copy(coef[(0, t)], slot(bank[RETURN_BANK], 0))
+            nc.scalar.copy(mean[t][:], slot(bank[RETURN_BANK], 0))
+
+        def centre_gpsimd(t):
+            nc.gpsimd.tensor_tensor(
+                thirds(coef[t], 0), thirds(picked[t], 0), mean[t][:].unsqueeze(1).to_broadcast([P, 3, V]), ALU.add
+            )
+
+        def centre_vector(t):
+            lo = 1 if t in TRIP else 0
+            minus = slot(bank[RETURN_BANK], 0).unsqueeze(1).to_broadcast([P, 3 - lo, V])
+            nc.vector.tensor_tensor(thirds(coef[t], lo), thirds(picked[t], lo), minus, ALU.add)
+            if t in TRIP:
+                nc.scalar.copy(slot(coef[t], 0), slot(bank[RETURN_BANK], 1))
 
         root = sb("root", [P, HALVES * H], F32)
 
         def squares(t):
-            nc.scalar.activation(slot(sq[t], 0), dif[(2, t)], ACT.Square, scale=math.sqrt(3.0))
-            nc.scalar.activation(slot(sq[t], 1), coef[(1, t)], ACT.Square)
+            nc.scalar.activation(sq[t][:], coef[t][:], ACT.Square)
             for h in range(HALVES):
-                terms = [block(slot(sq[t], which), h) for which in range(2)]
+                terms = [block(slot(sq[t], n), h) for n in range(3)]
                 add_transposed(block(bank[VAR_BANK[t // 2]], 2 * h + t % 2), terms)
 
         def inverse_root(pair):
@@ -260,17 +253,21 @@ def tile_picked_ycovn_corr_p_kernel(
                 root[:].rearrange("v (h i) -> v h i", h=HALVES)[:, :, pair * 2 * P : (pair + 1) * 2 * P],
                 bank[VAR_BANK[pair]][:].rearrange("v (h i) -> v h i", h=HALVES),
                 ACT.Abs_reciprocal_sqrt,
-                bias=8.1,
-                scale=4.5,
+                bias=0.9,
+                scale=3.0,
             )
 
-        prod = {(t, n): sb("m_%d_%d" % (t, n), [P, V], F32)[:] for t in range(TILES) for n in range(3)}
+        prod = {(t, n): sb("m_%d_%d" % (t, n), [P, V], F32)[:] for t in range(1, TILES) for n in range(3)}
+        first = at(59 * KIB + 128, "m_0", 3 * V)
+        prod.update({(0, n): slot(first, n) for n in range(3)})
 
         def z_of(t, h):
             return block(bank[SUM_BANK[h]], t) if t < LAST else block(bank[LAST_SUM_BANK[h]], 0)
 
         def product(t, n):
-            nc.vector.tensor_tensor(prod[(t, n)], win[("a", t)][:].indirect(pos_t[n][:]), coef[(n, t)], ALU.mult)
+            nc.vector.tensor_tensor(
+                prod[(t, n)], win[("a", t)][:].indirect(pos_t[n][:]), slot(coef[t], n), ALU.mult
+            )
 
         def add_up(t, n):
             for h in range(HALVES):
@@ -308,71 +305,66 @@ def tile_picked_ycovn_corr_p_kernel(
         for g in range(PASSES):
             project(bank[ACC_BANK[("e", 1)]], *one_pass(1, g, nc.vector.tensor_copy), g, 0, S)
 
-        pick(0)
-        difference(0, 1)
-        difference(0, 2)
+        for n in range(3):
+            pick(0, n)
         weights("e", 2)
-        centre(0, 1)
         empty("e", 1)
-        pick(1)
         turn(0)
-        staged = stage("a", 0)
-        centre(0, 2)
-        difference(1, 1)
-        multiply("a", 0, staged)
-        difference(1, 2)
-        turn_back(0)
-        empty("e", 2)
-        pick(2)
-        turn(1)
+        for n in range(3):
+            pick(1, n)
         staged = stage("e", 3)
-        centre(1, 2)
+        turn_back(0)
+        turn(1)
         multiply("e", 3, staged)
-        centre(1, 1)
-        difference(2, 1)
-        difference(2, 2)
+        staged = stage("a", 0, (nc.scalar.copy, nc.vector.tensor_copy))
+        empty("e", 2)
         fetch(0)
-        weights("a", 1)
-        empty("a", 0)
-        product(0, 1)
-        product(0, 2)
         turn_back(1)
-        turn(2)
-        weights("a", 2)
-        centre(2, 1)
-        centre(2, 2)
-        product(0, 0)
+        pick(2, 0)
+        held = quantise("a_0", staged[:])
+        centre_gpsimd(0)
+        pick(2, 1)
+        pick(2, 2)
         empty("e", 3)
-        pick(3)
-        weights("a", 3)
-        difference(3, 1)
-        difference(3, 2)
-        empty("a", 1)
+        turn(2)
+        passes("a", 0, *held)
         fetch(1)
-        product(1, 1)
-        product(1, 2)
+        centre_gpsimd(1)
+        for n in range(3):
+            pick(3, n)
+        staged = stage("a", 1)
         turn_back(2)
         turn(3)
+        centre_vector(2)
+        empty("a", 0)
+        multiply("a", 1, staged)
         squares(0)
-        squares(1)
-        squares(2)
-        centre(3, 1)
-        centre(3, 2)
-        product(1, 0)
-        fetch(2)
-        empty("a", 2)
-        product(2, 1)
-        product(2, 2)
+        for n in ORDER:
+            product(0, n)
+        staged = stage("a", 2)
         turn_back(3)
-        product(2, 0)
+        empty("a", 1)
+        multiply("a", 2, staged)
+        centre_vector(3)
+        for n in ORDER:
+            add_up(0, n)
+        staged = stage("a", 3)
+        product(1, 1)
+        multiply("a", 3, staged)
+        squares(1)
+        empty("a", 2)
+        product(1, 2)
+        product(1, 0)
+        squares(2)
         empty("a", 3)
-        fetch(3)
         squares(3)
+        for n in ORDER:
+            product(2, n)
         inverse_root(0)
         inverse_root(1)
         for n in ORDER:
             product(3, n)
-        for t in range(TILES):
+        for t in range(1, TILES):
             for n in ORDER:
                 add_up(t, n)
 

@@ -31,18 +31,40 @@ BANKS = 8
 RUN = 4
 ORDER = (1, 2, 0)
 
-LATER = (("e", 2), ("e", 3), ("a", 0), ("a", 1), ("a", 2), ("a", 3))
-ACC_BANK = {("e", 1): 2, ("e", 2): 3, ("e", 3): 0, ("a", 0): 0, ("a", 1): 3, ("a", 2): 2, ("a", 3): 3}
+LATER = (("e", 2), ("a", 0), ("e", 3), ("a", 1), ("a", 2), ("a", 3))
+ACC_BANK = {("e", 1): 2, ("e", 2): 3, ("a", 0): 2, ("e", 3): 3, ("a", 1): 2, ("a", 2): 3, ("a", 3): 2}
 FIRST_PIECES = ((0, 0, V), (1, V, V + P), (4, V + P, S))
 SUM_BANK = (4, 5)
-LAST_SUM_BANK = (2, 3)
-TURN_BANK, RETURN_BANK = 6, 7
-VAR_BANK = (1, 0)
+LAST_SUM_BANK = (3, 2)
+TURN_BANK, RETURN_BANK = (6, 6, 0, 6), (7, 1, 7, 7)
+VAR_BANK = (0, 0, 1, 6)
 BACK_BANK = (0, 1)
 OUT_BANK = (6, 7)
-KIB = 1024
-RAW_AT = {("e", 2, 0): 2 * KIB, ("a", 2, 1): 48 * KIB, ("a", 3, 0): 52 * KIB, ("a", 3, 1): 56 * KIB}
-TRIP = ()
+WARM = {}
+PLAIN = 2
+BOTH = (3,)
+SLOT = 9216
+SHARE = {
+    "win_e_1": ("raw_e_2_0", "low"),
+    "stage_a_0": ("codes_e_1_1", "low"),
+    "c_0": ("stage_a_0", "low"),
+    "win_e_2": ("raw_a_0_0", "low"),
+    "stage_e_3": ("turned_0", "low"),
+    "stage_a_1": ("codes_a_0", "low"),
+    "c_1": ("stage_a_1", "low"),
+    "m_0_0": ("raw_a_1_1", "low"),
+    "win_e_3": ("raw_a_1_0", "low"),
+    "e0_3": ("turned_2", "low"),
+    "stage_a_2": ("turned_2", "high"),
+    "dif_3": ("raw_a_2_1", "low"),
+    "stage_a_3": ("raw_a_2_0", "high"),
+    "win_a_1": ("raw_a_3_0", "low"),
+    "sq_0": ("raw_a_3_1", "low"),
+    "sq_1": ("raw_a_3_1", "high"),
+    "sq_2": ("raw_a_3_0", "high"),
+    "m_2_2": ("turned_3", "low"),
+    "m_2_0": ("turned_3", "high"),
+}
 
 
 def tile_picked_ycovn_corr_p_kernel(
@@ -54,7 +76,21 @@ def tile_picked_ycovn_corr_p_kernel(
         shared = ctx.enter_context(tc.tile_pool(name="shared", bufs=1))
         psum = ctx.enter_context(tc.psum_pool(name="psum", bufs=1))
 
+        hosts = sorted(set(host for host, where in SHARE.values()) - set(SHARE))
+        size = {F32: 4, BF16: 2, U32: 4, U8: 1}
+        ends = {}
+
         def sb(name, shape, dtype):
+            if name in hosts:
+                start = hosts.index(name) * SLOT + 4096
+                ends[name] = (start, start + shape[1] * size[dtype])
+                return shared.tile(shape, dtype, name=name, offset=start, align_bytes=64)
+            if name in SHARE:
+                host, where = SHARE[name]
+                lo, hi = ends[host]
+                start = {"low": lo + 64 - shape[1] * size[dtype], "mid": lo + 64, "high": hi - 64}[where]
+                ends[name] = (start, start + shape[1] * size[dtype])
+                return shared.tile(shape, dtype, name=name, offset=start, align_bytes=64)
             return keep.tile(shape, dtype, name=name, align_bytes=64)
 
         def slot(tile, i):
@@ -71,18 +107,8 @@ def tile_picked_ycovn_corr_p_kernel(
         xs = sb("xs", [P, T], U8)
         raw = {}
 
-        def at(offset, name, cols, dtype=F32):
-            return shared.tile([P, cols], dtype, name=name, offset=offset, align_bytes=64)
-
-        picked = [sb("e_0", [P, 3 * V], F32), sb("e_1", [P, 3 * V], F32), sb("e_2", [P, 3 * V], F32), sb("e_3", [P, 3 * V], F32)]
-
         def load_w(name, w, t, g):
-            if (name, t, g) == ("a", 0, 1):
-                tile = picked[2][:, V : 3 * V]
-            elif (name, t, g) in RAW_AT:
-                tile = at(RAW_AT[(name, t, g)], "raw_%s_%d_%d" % (name, t, g), PACK * P)
-            else:
-                tile = sb("raw_%s_%d_%d" % (name, t, g), [P, PACK * P], F32)
+            tile = sb("raw_%s_%d_%d" % (name, t, g), [P, PACK * P], F32)
             rows = w[g * K_PASS : (g + 1) * K_PASS, t * P : (t + 1) * P]
             nc.sync.dma_start(
                 tile[:].rearrange("p (j c) -> p j c", j=PACK), rows.rearrange("(p j) c -> p j c", j=PACK)
@@ -132,17 +158,9 @@ def tile_picked_ycovn_corr_p_kernel(
                 src[:].rearrange("p (j c run) -> p c j run", j=PACK, run=RUN),
             )
 
-        CODES_AT = {"e_1_1": 36 * KIB, "a_0": 68 * KIB, "a_1": 62 * KIB + 512}
-
         def quantise(name, src):
-            if name in CODES_AT:
-                codes = at(CODES_AT[name], "codes_" + name, src.shape[1] // PACK, U32)
-            else:
-                codes = sb("codes_" + name, [P, src.shape[1] // PACK], U32)
-            if name == "a_1":
-                scales = at(72 * KIB, "scales_a_1", src.shape[1] // PACK, U8)
-            else:
-                scales = sb("scales_" + name, [P, src.shape[1] // PACK], U8)
+            codes = sb("codes_" + name, [P, src.shape[1] // PACK], U32)
+            scales = sb("scales_" + name, [P, src.shape[1] // PACK], U8)
             nc.vector.quantize_mx(out=codes[:].bitcast(FP8X4), scales=scales[:], in_=src)
             return codes, scales
 
@@ -163,33 +181,48 @@ def tile_picked_ycovn_corr_p_kernel(
                 stop=(g == PASSES - 1),
             )
 
-        STAGE_AT = {("e", 3): 36 * KIB, ("a", 0): 6 * KIB, ("a", 1): 30 * KIB, ("a", 2): 64 * KIB, ("a", 3): 72 * KIB}
+        made = {}
 
-        def stage(name, t, copies=(nc.scalar.copy, nc.scalar.copy)):
-            tag = "stage_%s_%d" % (name, t)
-            if (name, t) in STAGE_AT:
-                staged = at(STAGE_AT[(name, t)], tag, PASSES * K_PASS, BF16)
-            else:
-                staged = sb(tag, [P, PASSES * K_PASS], BF16)
+        def keep_warm(dst, codes, scales, g):
+            nc.tensor.matmul_mx(
+                out=dst[:],
+                lhsT=codes[:].bitcast(FP8X4),
+                lhsT_scale=scales[:],
+                rhs=xg[g][:].bitcast(FP8X4),
+                rhs_scale=xsg[ROWS * g : P, :],
+                start=True,
+                stop=True,
+            )
+
+        def stage(name, t):
+            staged = sb("stage_%s_%d" % (name, t), [P, PASSES * K_PASS], BF16)
             for g in range(PASSES):
-                cast(copies[g], staged[:, g * K_PASS : (g + 1) * K_PASS], raw[(name, t, g)])
+                cast(nc.scalar.copy, staged[:, g * K_PASS : (g + 1) * K_PASS], raw[(name, t, g)])
             return staged
 
         def multiply(name, t, staged):
-            passes(name, t, *quantise("%s_%d" % (name, t), staged[:]))
+            codes, scales = quantise("%s_%d" % (name, t), staged[:])
+            made[(name, t)] = (codes, scales)
+            if (name, t) != ("a", LAST):
+                passes(name, t)
 
-        def passes(name, t, codes, scales):
+        def passes(name, t):
+            codes, scales = made[(name, t)]
             for g in range(PASSES):
                 project(bank[ACC_BANK[(name, t)]], block(codes, g), block(scales, g), g, 0, S)
+            if (name, t) in WARM:
+                keep_warm(bank[WARM[(name, t)]], block(codes, 0), block(scales, 0), 0)
 
         def weights(name, t):
             multiply(name, t, stage(name, t))
 
-        win = {(name, t): sb("win_%s_%d" % (name, t), [P, S], F32) for name, t in (("e", 0),) + LATER}
-        win[("e", 1)] = at(KIB, "win_e_1", S)
+        win = {}
 
         def empty(name, t):
+            win[(name, t)] = sb("win_%s_%d" % (name, t), [P, S], F32)
             nc.scalar.copy(win[(name, t)][:], bank[ACC_BANK[(name, t)]][:])
+
+        win[("e", 0)] = sb("win_e_0", [P, S], F32)
 
         def add_transposed(dst, srcs):
             for i, src in enumerate(srcs):
@@ -197,88 +230,114 @@ def tile_picked_ycovn_corr_p_kernel(
                     dst, lhsT=src, rhs=ident[:], is_transpose=True, start=(i == 0), stop=(i == len(srcs) - 1)
                 )
 
-        coef = [at(7 * KIB, "c_0", 3 * V), sb("c_1", [P, 3 * V], F32), sb("c_2", [P, 3 * V], F32), at(31 * KIB, "c_3", 3 * V)]
-        mean = [sb("mean_0", [P, V], F32), sb("mean_1", [P, V], F32)]
-        turned = [sb("turned_0", [P, 2 * V], F32)] + [at(o * KIB + 64, "turned_%d" % o, 2 * V) for o in (28, 62, 42)]
-        sq = [at(o * KIB, "sq_%d" % t, 3 * V) for t, o in enumerate((68, 52, 56))] + [sb("sq_3", [P, 3 * V], F32)]
+        got, coef, turned = {}, {}, {}
 
-        def pick(t, n):
-            nc.vector.tensor_copy(slot(picked[t], n), win[("e", t)][:].indirect(pos_t[n][:]))
+        def entries(n, lo, hi):
+            return pos_t[n][:, lo // GROUP : hi // GROUP]
+
+        def pick(t, cuts=(0, V)):
+            got[(t, 0)] = sb("e0_%d" % t, [P, V], F32)[:]
+            for lo, hi in zip(cuts, cuts[1:]):
+                nc.vector.tensor_copy(got[(t, 0)][:, lo:hi], win[("e", t)][:].indirect(entries(0, lo, hi)))
+
+        def differences(t, cuts=(0, V)):
+            got[t] = sb("dif_%d" % t, [P, 2 * V], F32)[:]
+            for n in (1, 2):
+                got[(t, n)] = slot(got[t], n - 1)
+                for lo, hi in zip(cuts, cuts[1:]) if n == 1 else ((0, V),):
+                    nc.vector.tensor_tensor(
+                        got[(t, n)][:, lo:hi], win[("e", t)][:].indirect(entries(n, lo, hi)), got[(t, 0)][:, lo:hi], ALU.subtract
+                    )
+
+        def pick_all(t):
+            got[t] = sb("e_%d" % t, [P, 3 * V], F32)[:]
+            for n in range(3):
+                got[(t, n)] = slot(got[t], n)
+                nc.vector.tensor_copy(got[(t, n)], win[("e", t)][:].indirect(pos_t[n][:]))
 
         def turn(t):
+            terms = range(3) if t == PLAIN else (1, 2)
             for h in range(HALVES):
-                add_transposed(block(bank[TURN_BANK], h), [block(slot(picked[t], n), h) for n in range(3)])
-            if t in TRIP:
+                add_transposed(block(bank[TURN_BANK[t]], h), [block(got[(t, n)], h) for n in terms])
+            if t in BOTH:
                 for h in range(HALVES):
-                    add_transposed(block(bank[TURN_BANK], HALVES + h), [block(slot(picked[t], 0), h)])
+                    add_transposed(block(bank[TURN_BANK[t]], HALVES + h), [block(got[(t, 2)], h)])
 
         def turn_back(t):
-            nc.scalar.activation(slot(turned[t], 0), slot(bank[TURN_BANK], 0), ACT.Copy, scale=-1.0 / 3.0)
-            if t in TRIP:
-                nc.scalar.copy(slot(turned[t], 1), slot(bank[TURN_BANK], 1))
+            turned[t] = sb("turned_%d" % t, [P, 2 * V], F32)
+            nc.scalar.activation(slot(turned[t], 0), slot(bank[TURN_BANK[t]], 0), ACT.Copy, scale=-1.0 / 3.0)
+            if t in BOTH:
+                nc.scalar.copy(slot(turned[t], 1), slot(bank[TURN_BANK[t]], 1))
             for h in range(HALVES):
-                nc.tensor.transpose(block(bank[RETURN_BANK], h), block(turned[t], h), ident[:])
-            if t in TRIP:
+                nc.tensor.transpose(block(bank[RETURN_BANK[t]], h), block(turned[t], h), ident[:])
+            if t in BOTH:
                 for h in range(HALVES):
-                    add_transposed(block(bank[RETURN_BANK], HALVES + h), [block(turned[t], HALVES + h), block(turned[t], h)])
-
-        def thirds(ap, lo):
-            return ap[:, lo * V : 3 * V].rearrange("p (n v) -> p n v", v=V)
+                    add_transposed(block(bank[RETURN_BANK[t]], HALVES + h), [block(turned[t], HALVES + h), block(turned[t], h)])
 
         def fetch(t):
-            nc.scalar.copy(mean[t][:], slot(bank[RETURN_BANK], 0))
+            wide = 2 if t in BOTH else 1
+            tile = sb("fetched_%d" % t, [P, wide * V], F32)
+            nc.scalar.copy(tile[:], bank[RETURN_BANK[t]][:, 0 : wide * V])
+            coef[(t, 0)] = slot(tile, 0)
+            if t in BOTH:
+                coef[(t, 2)] = slot(tile, 1)
 
-        def centre_gpsimd(t):
-            nc.gpsimd.tensor_tensor(
-                thirds(coef[t], 0), thirds(picked[t], 0), mean[t][:].unsqueeze(1).to_broadcast([P, 3, V]), ALU.add
+        def runs(ap):
+            return ap.rearrange("p (n v) -> p n v", v=V)
+
+        def centre(engine, t, minus, first, count):
+            tile = sb("c_%d" % t, [P, count * V], F32)
+            engine.tensor_tensor(
+                runs(tile[:]), runs(got[t][:, 0 : count * V]), minus.unsqueeze(1).to_broadcast([P, count, V]), ALU.add
             )
-
-        def centre_vector(t):
-            lo = 1 if t in TRIP else 0
-            minus = slot(bank[RETURN_BANK], 0).unsqueeze(1).to_broadcast([P, 3 - lo, V])
-            nc.vector.tensor_tensor(thirds(coef[t], lo), thirds(picked[t], lo), minus, ALU.add)
-            if t in TRIP:
-                nc.scalar.copy(slot(coef[t], 0), slot(bank[RETURN_BANK], 1))
+            for i in range(count):
+                coef[(t, first + i)] = slot(tile, i)
 
         root = sb("root", [P, HALVES * H], F32)
 
         def squares(t):
-            nc.scalar.activation(sq[t][:], coef[t][:], ACT.Square)
+            count = 3 if t == PLAIN else 2
+            sq = sb("sq_%d" % t, [P, count * V], F32)
+            if t == PLAIN:
+                for n in range(3):
+                    nc.scalar.activation(slot(sq, n), coef[(t, n)], ACT.Square)
+            else:
+                nc.scalar.activation(slot(sq, 0), got[(t, 2)], ACT.Square, scale=math.sqrt(0.5))
+                nc.scalar.activation(slot(sq, 1), coef[(t, 1)], ACT.Square, scale=math.sqrt(1.5))
             for h in range(HALVES):
-                terms = [block(slot(sq[t], n), h) for n in range(3)]
-                add_transposed(block(bank[VAR_BANK[t // 2]], 2 * h + t % 2), terms)
+                terms = [block(slot(sq, n), h) for n in range(count)]
+                add_transposed(block(bank[VAR_BANK[t]], 2 * h + t % 2), terms)
 
-        def inverse_root(pair):
+        def inverse_root(first, tiles):
+            lo = first % 2 * P
             nc.scalar.activation(
-                root[:].rearrange("v (h i) -> v h i", h=HALVES)[:, :, pair * 2 * P : (pair + 1) * 2 * P],
-                bank[VAR_BANK[pair]][:].rearrange("v (h i) -> v h i", h=HALVES),
+                root[:].rearrange("v (h i) -> v h i", h=HALVES)[:, :, first * P : (first + tiles) * P],
+                bank[VAR_BANK[first]][:].rearrange("v (h i) -> v h i", h=HALVES)[:, :, lo : lo + tiles * P],
                 ACT.Abs_reciprocal_sqrt,
                 bias=0.9,
                 scale=3.0,
             )
 
-        prod = {(t, n): sb("m_%d_%d" % (t, n), [P, V], F32)[:] for t in range(1, TILES) for n in range(3)}
-        first = at(59 * KIB + 128, "m_0", 3 * V)
-        prod.update({(0, n): slot(first, n) for n in range(3)})
+        prod = {}
 
         def z_of(t, h):
             return block(bank[SUM_BANK[h]], t) if t < LAST else block(bank[LAST_SUM_BANK[h]], 0)
 
         def product(t, n):
-            nc.vector.tensor_tensor(
-                prod[(t, n)], win[("a", t)][:].indirect(pos_t[n][:]), slot(coef[t], n), ALU.mult
-            )
+            prod[(t, n)] = sb("m_%d_%d" % (t, n), [P, V], F32)[:]
+            nc.vector.tensor_tensor(prod[(t, n)], win[("a", t)][:].indirect(pos_t[n][:]), coef[(t, n)], ALU.mult)
 
-        def add_up(t, n):
-            for h in range(HALVES):
-                nc.tensor.matmul(
-                    z_of(t, h),
-                    lhsT=block(prod[(t, n)], h),
-                    rhs=ident[:],
-                    is_transpose=True,
-                    start=(n == ORDER[0]),
-                    stop=(n == ORDER[-1]),
-                )
+        def add_up(t):
+            for n in ORDER:
+                for h in range(HALVES):
+                    nc.tensor.matmul(
+                        z_of(t, h),
+                        lhsT=block(prod[(t, n)], h),
+                        rhs=ident[:],
+                        is_transpose=True,
+                        start=(n == ORDER[0]),
+                        stop=(n == ORDER[-1]),
+                    )
 
         rr_turned = [sb("rrT%d" % h, [P, H], BF16) for h in range(HALVES)]
 
@@ -303,70 +362,71 @@ def tile_picked_ycovn_corr_p_kernel(
         for b, lo, hi in FIRST_PIECES:
             nc.scalar.copy(win[("e", 0)][:, lo:hi], bank[b][:, lo:hi])
         for g in range(PASSES):
-            project(bank[ACC_BANK[("e", 1)]], *one_pass(1, g, nc.vector.tensor_copy), g, 0, S)
+            codes, scales = one_pass(1, g, nc.vector.tensor_copy)
+            project(bank[ACC_BANK[("e", 1)]], codes, scales, g, 0, S)
+        if ("e", 1) in WARM:
+            keep_warm(bank[WARM[("e", 1)]], codes, scales, 1)
 
-        for n in range(3):
-            pick(0, n)
+        pick(0)
+        differences(0)
         weights("e", 2)
         empty("e", 1)
         turn(0)
-        for n in range(3):
-            pick(1, n)
-        staged = stage("e", 3)
+        pick(1, (0, P, V))
+        differences(1, (0, P, V))
+        staged = stage("a", 0)
         turn_back(0)
         turn(1)
-        multiply("e", 3, staged)
-        staged = stage("a", 0, (nc.scalar.copy, nc.vector.tensor_copy))
+        multiply("a", 0, staged)
         empty("e", 2)
         fetch(0)
+        centre(nc.gpsimd, 0, coef[(0, 0)], 1, 2)
+        pick_all(2)
         turn_back(1)
-        pick(2, 0)
-        held = quantise("a_0", staged[:])
-        centre_gpsimd(0)
-        pick(2, 1)
-        pick(2, 2)
-        empty("e", 3)
         turn(2)
-        passes("a", 0, *held)
-        fetch(1)
-        centre_gpsimd(1)
-        for n in range(3):
-            pick(3, n)
+        weights("e", 3)
+        empty("a", 0)
+        product(0, 1)
+        product(0, 2)
         staged = stage("a", 1)
         turn_back(2)
-        turn(3)
-        centre_vector(2)
-        empty("a", 0)
         multiply("a", 1, staged)
-        squares(0)
-        for n in ORDER:
-            product(0, n)
-        staged = stage("a", 2)
-        turn_back(3)
+        fetch(1)
+        centre(nc.gpsimd, 1, coef[(1, 0)], 1, 2)
+        product(0, 0)
+        centre(nc.vector, 2, slot(bank[RETURN_BANK[2]], 0), 0, 3)
+        empty("e", 3)
+        pick(3)
+        weights("a", 2)
+        differences(3)
+        turn(3)
+        weights("a", 3)
         empty("a", 1)
-        multiply("a", 2, staged)
-        centre_vector(3)
-        for n in ORDER:
-            add_up(0, n)
-        staged = stage("a", 3)
+        turn_back(3)
+        passes("a", 3)
+        add_up(0)
         product(1, 1)
-        multiply("a", 3, staged)
-        squares(1)
-        empty("a", 2)
         product(1, 2)
+        squares(0)
+        empty("a", 2)
         product(1, 0)
+        add_up(1)
+        product(2, 1)
+        centre(nc.vector, 3, slot(bank[RETURN_BANK[3]], 0), 1, 1)
+        fetch(3)
+        squares(1)
         squares(2)
         empty("a", 3)
+        inverse_root(0, 2)
+        inverse_root(2, 1)
+        product(2, 2)
+        product(2, 0)
+        add_up(2)
         squares(3)
-        for n in ORDER:
-            product(2, n)
-        inverse_root(0)
-        inverse_root(1)
+        inverse_root(3, 1)
         for n in ORDER:
             product(3, n)
-        for t in range(1, TILES):
-            for n in ORDER:
-                add_up(t, n)
+        add_up(3)
 
         w2_staged = prod[(LAST, 2)].bitcast(BF16)
         cast(nc.scalar.copy, w2_staged, raw[("o", 0, 0)])

@@ -40,7 +40,7 @@ TURN_BANK, RETURN_BANK = (6, 6, 0, 6), (7, 1, 7, 7)
 VAR_BANK = (0, 0, 1, 6)
 BACK_BANK = (0, 1)
 OUT_BANK = (6, 7)
-WARM = {}
+WARM = {("e", 1): 5, ("a", 0): 5, ("a", 1): 6}
 PLAIN = 2
 BOTH = (3,)
 SLOT = 9216
@@ -364,8 +364,8 @@ def tile_picked_ycovn_corr_p_kernel(
         for g in range(PASSES):
             codes, scales = one_pass(1, g, nc.vector.tensor_copy)
             project(bank[ACC_BANK[("e", 1)]], codes, scales, g, 0, S)
-        if ("e", 1) in WARM:
-            keep_warm(bank[WARM[("e", 1)]], codes, scales, 1)
+            if ("e", 1) in WARM and g == 0:
+                keep_warm(bank[WARM[("e", 1)]], codes, scales, 0)
 
         pick(0)
         differences(0)

@@ -40,7 +40,7 @@ TURN_BANK, RETURN_BANK = (6, 6, 0, 6), (7, 1, 7, 7)
 VAR_BANK = (0, 0, 1, 6)
 BACK_BANK = (0, 1)
 OUT_BANK = (6, 7)
-WARM = {("e", 1): 5, ("a", 0): 5, ("a", 1): 6}
+WARM = {("e", 1): 5, ("e", 2): 5, ("a", 0): 5, ("a", 1): 6}
 PLAIN = 2
 BOTH = (3,)
 SLOT = 9216
@@ -62,8 +62,7 @@ SHARE = {
     "sq_0": ("raw_a_3_1", "low"),
     "sq_1": ("raw_a_3_1", "high"),
     "sq_2": ("raw_a_3_0", "high"),
-    "m_2_2": ("turned_3", "low"),
-    "m_2_0": ("turned_3", "high"),
+    "c_3": ("raw_a_3_1", "mid"),
 }
 
 
@@ -265,9 +264,9 @@ def tile_picked_ycovn_corr_p_kernel(
 
         def turn_back(t):
             turned[t] = sb("turned_%d" % t, [P, 2 * V], F32)
-            nc.scalar.activation(slot(turned[t], 0), slot(bank[TURN_BANK[t]], 0), ACT.Copy, scale=-1.0 / 3.0)
+            nc.scalar.activation(slot(turned[t], 0), slot(bank[TURN_BANK[t]], 0), ACT.Copy, scale=-1.0 if t == LAST else -1.0 / 3.0)
             if t in BOTH:
-                nc.scalar.copy(slot(turned[t], 1), slot(bank[TURN_BANK[t]], 1))
+                nc.scalar.activation(slot(turned[t], 1), slot(bank[TURN_BANK[t]], 1), ACT.Copy, scale=3.0)
             for h in range(HALVES):
                 nc.tensor.transpose(block(bank[RETURN_BANK[t]], h), block(turned[t], h), ident[:])
             if t in BOTH:
@@ -303,7 +302,7 @@ def tile_picked_ycovn_corr_p_kernel(
                     nc.scalar.activation(slot(sq, n), coef[(t, n)], ACT.Square)
             else:
                 nc.scalar.activation(slot(sq, 0), got[(t, 2)], ACT.Square, scale=math.sqrt(0.5))
-                nc.scalar.activation(slot(sq, 1), coef[(t, 1)], ACT.Square, scale=math.sqrt(1.5))
+                nc.scalar.activation(slot(sq, 1), coef[(t, 1)], ACT.Square, scale=math.sqrt(1.5 / 9.0 if t == LAST else 1.5))
             for h in range(HALVES):
                 terms = [block(slot(sq, n), h) for n in range(count)]
                 add_transposed(block(bank[VAR_BANK[t]], 2 * h + t % 2), terms)
@@ -314,8 +313,8 @@ def tile_picked_ycovn_corr_p_kernel(
                 root[:].rearrange("v (h i) -> v h i", h=HALVES)[:, :, first * P : (first + tiles) * P],
                 bank[VAR_BANK[first]][:].rearrange("v (h i) -> v h i", h=HALVES)[:, :, lo : lo + tiles * P],
                 ACT.Abs_reciprocal_sqrt,
-                bias=0.9,
-                scale=3.0,
+                bias=8.1 if first == LAST else 0.9,
+                scale=27.0 if first == LAST else 3.0,
             )
 
         prod = {}
@@ -364,14 +363,14 @@ def tile_picked_ycovn_corr_p_kernel(
         for g in range(PASSES):
             codes, scales = one_pass(1, g, nc.vector.tensor_copy)
             project(bank[ACC_BANK[("e", 1)]], codes, scales, g, 0, S)
-            if ("e", 1) in WARM and g == 0:
-                keep_warm(bank[WARM[("e", 1)]], codes, scales, 0)
+        if ("e", 1) in WARM:
+            keep_warm(bank[WARM[("e", 1)]], codes, scales, 1)
 
-        pick(0)
-        differences(0)
+        pick(0, (0, P, V))
+        differences(0, (0, P, V))
+        turn(0)
         weights("e", 2)
         empty("e", 1)
-        turn(0)
         pick(1, (0, P, V))
         differences(1, (0, P, V))
         staged = stage("a", 0)
@@ -401,6 +400,10 @@ def tile_picked_ycovn_corr_p_kernel(
         differences(3)
         turn(3)
         weights("a", 3)
+        coef[(LAST, 1)] = sb("c_3", [P, V], F32)[:]
+        nc.vector.scalar_tensor_tensor(
+            coef[(LAST, 1)], got[(LAST, 1)], 2.0, got[(LAST, 2)], ALU.mult, ALU.subtract
+        )
         empty("a", 1)
         turn_back(3)
         passes("a", 3)
@@ -412,17 +415,16 @@ def tile_picked_ycovn_corr_p_kernel(
         product(1, 0)
         add_up(1)
         product(2, 1)
-        centre(nc.vector, 3, slot(bank[RETURN_BANK[3]], 0), 1, 1)
-        fetch(3)
         squares(1)
         squares(2)
+        squares(3)
         empty("a", 3)
         inverse_root(0, 2)
         inverse_root(2, 1)
+        fetch(3)
         product(2, 2)
         product(2, 0)
         add_up(2)
-        squares(3)
         inverse_root(3, 1)
         for n in ORDER:
             product(3, n)

@@ -360,8 +360,8 @@ def tile_picked_ycovn_corr_p_kernel(
             project(bank[b], codes, scales, 1, lo, hi)
         for b, lo, hi in FIRST_PIECES:
             nc.scalar.copy(win[("e", 0)][:, lo:hi], bank[b][:, lo:hi])
-        for g in range(PASSES):
-            codes, scales = one_pass(1, g, nc.vector.tensor_copy)
+        for g, copy in enumerate((nc.scalar.copy, nc.vector.tensor_copy)):
+            codes, scales = one_pass(1, g, copy)
             project(bank[ACC_BANK[("e", 1)]], codes, scales, g, 0, S)
         if ("e", 1) in WARM:
             keep_warm(bank[WARM[("e", 1)]], codes, scales, 1)

@@ -42,14 +42,15 @@ BACK_BANK = (0, 1)
 OUT_BANK = (6, 7)
 WARM = {("e", 1): 5, ("e", 2): 5, ("a", 0): 5, ("a", 1): 6}
 PLAIN = 2
+ON_GPSIMD = (("a", 0, 0),)
 BOTH = (3,)
 SLOT = 9216
 SHARE = {
     "win_e_1": ("raw_e_2_0", "low"),
-    "stage_a_0": ("codes_e_1_1", "low"),
+    "stage_a_0": ("e0_0", "low"),
     "c_0": ("stage_a_0", "low"),
-    "win_e_2": ("raw_a_0_0", "low"),
-    "stage_e_3": ("turned_0", "low"),
+    "stage_e_3": ("codes_e_2", "low"),
+    "fetched_0": ("codes_e_2", "high"),
     "stage_a_1": ("codes_a_0", "low"),
     "c_1": ("stage_a_1", "low"),
     "m_0_0": ("raw_a_1_1", "low"),
@@ -157,6 +158,9 @@ def tile_picked_ycovn_corr_p_kernel(
                 src[:].rearrange("p (j c run) -> p c j run", j=PACK, run=RUN),
             )
 
+        def gpsimd_copy(dst, src):
+            nc.gpsimd.tensor_scalar(dst, src, 1.0, 0.0, ALU.mult, ALU.add)
+
         def quantise(name, src):
             codes = sb("codes_" + name, [P, src.shape[1] // PACK], U32)
             scales = sb("scales_" + name, [P, src.shape[1] // PACK], U8)
@@ -193,10 +197,11 @@ def tile_picked_ycovn_corr_p_kernel(
                 stop=True,
             )
 
-        def stage(name, t):
-            staged = sb("stage_%s_%d" % (name, t), [P, PASSES * K_PASS], BF16)
-            for g in range(PASSES):
-                cast(nc.scalar.copy, staged[:, g * K_PASS : (g + 1) * K_PASS], raw[(name, t, g)])
+        def stage(name, t, staged=None, which=(0, 1)):
+            if staged is None:
+                staged = sb("stage_%s_%d" % (name, t), [P, PASSES * K_PASS], BF16)
+            for g in which:
+                cast(gpsimd_copy if (name, t, g) in ON_GPSIMD else nc.scalar.copy, staged[:, g * K_PASS : (g + 1) * K_PASS], raw[(name, t, g)])
             return staged
 
         def multiply(name, t, staged):
@@ -229,7 +234,7 @@ def tile_picked_ycovn_corr_p_kernel(
                     dst, lhsT=src, rhs=ident[:], is_transpose=True, start=(i == 0), stop=(i == len(srcs) - 1)
                 )
 
-        got, coef, turned = {}, {}, {}
+        got, coef, turned, centred = {}, {}, {}, {}
 
         def entries(n, lo, hi):
             return pos_t[n][:, lo // GROUP : hi // GROUP]
@@ -286,6 +291,7 @@ def tile_picked_ycovn_corr_p_kernel(
 
         def centre(engine, t, minus, first, count):
             tile = sb("c_%d" % t, [P, count * V], F32)
+            centred[t] = tile
             engine.tensor_tensor(
                 runs(tile[:]), runs(got[t][:, 0 : count * V]), minus.unsqueeze(1).to_broadcast([P, count, V]), ALU.add
             )
@@ -294,17 +300,23 @@ def tile_picked_ycovn_corr_p_kernel(
 
         root = sb("root", [P, HALVES * H], F32)
 
+        early = {}
+
+        def square_early(t):
+            early[t] = sb("sq_early_%d" % t, [P, V], F32)[:]
+            nc.scalar.activation(early[t], got[(t, 2)], ACT.Square, scale=math.sqrt(0.5))
+
         def squares(t):
             count = 3 if t == PLAIN else 2
             sq = sb("sq_%d" % t, [P, count * V], F32)
             if t == PLAIN:
-                for n in range(3):
-                    nc.scalar.activation(slot(sq, n), coef[(t, n)], ACT.Square)
+                nc.scalar.activation(sq[:], centred[t][:], ACT.Square)
             else:
-                nc.scalar.activation(slot(sq, 0), got[(t, 2)], ACT.Square, scale=math.sqrt(0.5))
+                if t not in early:
+                    nc.scalar.activation(slot(sq, 0), got[(t, 2)], ACT.Square, scale=math.sqrt(0.5))
                 nc.scalar.activation(slot(sq, 1), coef[(t, 1)], ACT.Square, scale=math.sqrt(1.5 / 9.0 if t == LAST else 1.5))
             for h in range(HALVES):
-                terms = [block(slot(sq, n), h) for n in range(count)]
+                terms = [block(early[t] if n == 0 and t in early else slot(sq, n), h) for n in range(count)]
                 add_transposed(block(bank[VAR_BANK[t]], 2 * h + t % 2), terms)
 
         def inverse_root(first, tiles):
@@ -371,6 +383,7 @@ def tile_picked_ycovn_corr_p_kernel(
         turn(0)
         weights("e", 2)
         empty("e", 1)
+        square_early(0)
         pick(1, (0, P, V))
         differences(1, (0, P, V))
         staged = stage("a", 0)
@@ -378,12 +391,13 @@ def tile_picked_ycovn_corr_p_kernel(
         turn(1)
         multiply("a", 0, staged)
         empty("e", 2)
+        staged = stage("e", 3, which=(0,))
         fetch(0)
         centre(nc.gpsimd, 0, coef[(0, 0)], 1, 2)
         pick_all(2)
         turn_back(1)
         turn(2)
-        weights("e", 3)
+        multiply("e", 3, stage("e", 3, staged, (1,)))
         empty("a", 0)
         product(0, 1)
         product(0, 2)

@@ -64,6 +64,7 @@ SHARE = {
     "sq_1": ("raw_a_3_1", "high"),
     "sq_2": ("raw_a_3_0", "high"),
     "c_3": ("raw_a_3_1", "mid"),
+    "sq_early_0": ("raw_e_2_1", "low"),
 }
 
 

@@ -42,8 +42,9 @@ BACK_BANK = (0, 1)
 OUT_BANK = (6, 7)
 WARM = {("e", 1): 5, ("e", 2): 5, ("a", 0): 5, ("a", 1): 6}
 PLAIN = 2
+LAST_ORDER = (1, 0, 2)
 ON_GPSIMD = (("a", 0, 0),)
-BOTH = (3,)
+BOTH = ()
 SLOT = 9216
 SHARE = {
     "win_e_1": ("raw_e_2_0", "low"),
@@ -59,11 +60,12 @@ SHARE = {
     "stage_a_2": ("turned_2", "high"),
     "dif_3": ("raw_a_2_1", "low"),
     "stage_a_3": ("raw_a_2_0", "high"),
-    "win_a_1": ("raw_a_3_0", "low"),
-    "sq_0": ("raw_a_3_1", "low"),
+    "win_a_1": ("raw_a_3_1", "low"),
+    "sq_0": ("raw_a_3_0", "low"),
     "sq_1": ("raw_a_3_1", "high"),
     "sq_2": ("raw_a_3_0", "high"),
-    "c_3": ("raw_a_3_1", "mid"),
+    "c_3_1": ("raw_a_3_1", "mid"),
+    "c_3_2": ("stage_a_2", "high"),
     "sq_early_0": ("raw_e_2_1", "low"),
 }
 
@@ -337,18 +339,25 @@ def tile_picked_ycovn_corr_p_kernel(
 
         def product(t, n):
             prod[(t, n)] = sb("m_%d_%d" % (t, n), [P, V], F32)[:]
-            nc.vector.tensor_tensor(prod[(t, n)], win[("a", t)][:].indirect(pos_t[n][:]), coef[(t, n)], ALU.mult)
+            src = picked[(t, n)] if (t, n) in picked else win[("a", t)][:].indirect(pos_t[n][:])
+            nc.vector.tensor_tensor(prod[(t, n)], src, coef[(t, n)], ALU.mult)
 
-        def add_up(t):
-            for n in ORDER:
+        picked = {}
+
+        def pick_a(t, n):
+            picked[(t, n)] = sb("a_%d_%d" % (t, n), [P, V], F32)[:]
+            nc.scalar.activation(picked[(t, n)], win[("a", t)][:].indirect(pos_t[n][:]), ACT.Copy)
+
+        def add_up(t, order=ORDER):
+            for n in order:
                 for h in range(HALVES):
                     nc.tensor.matmul(
                         z_of(t, h),
                         lhsT=block(prod[(t, n)], h),
                         rhs=ident[:],
                         is_transpose=True,
-                        start=(n == ORDER[0]),
-                        stop=(n == ORDER[-1]),
+                        start=(n == order[0]),
+                        stop=(n == order[-1]),
                     )
 
         rr_turned = [sb("rrT%d" % h, [P, H], BF16) for h in range(HALVES)]
@@ -413,39 +422,40 @@ def tile_picked_ycovn_corr_p_kernel(
         pick(3)
         weights("a", 2)
         differences(3)
-        turn(3)
         weights("a", 3)
-        coef[(LAST, 1)] = sb("c_3", [P, V], F32)[:]
-        nc.vector.scalar_tensor_tensor(
-            coef[(LAST, 1)], got[(LAST, 1)], 2.0, got[(LAST, 2)], ALU.mult, ALU.subtract
-        )
+        for n, first, second, factor in ((1, 1, 2, 2.0), (2, 2, 1, 2.0), (0, 1, 2, -1.0)):
+            coef[(LAST, n)] = sb("c_3_%d" % n, [P, V], F32)[:]
+            nc.vector.scalar_tensor_tensor(
+                coef[(LAST, n)], got[(LAST, first)], factor, got[(LAST, second)], ALU.mult, ALU.subtract
+            )
+        squares(2)
+        squares(0)
         empty("a", 1)
-        turn_back(3)
         passes("a", 3)
         add_up(0)
+        squares(1)
         product(1, 1)
+        pick_a(1, 0)
         product(1, 2)
-        squares(0)
         empty("a", 2)
         product(1, 0)
         add_up(1)
-        product(2, 1)
-        squares(1)
-        squares(2)
         squares(3)
+        pick_a(2, 0)
+        product(2, 1)
         empty("a", 3)
-        inverse_root(0, 2)
         inverse_root(2, 1)
-        fetch(3)
+        pick_a(3, 2)
+        inverse_root(0, 2)
         product(2, 2)
         product(2, 0)
         add_up(2)
         inverse_root(3, 1)
-        for n in ORDER:
+        for n in LAST_ORDER:
             product(3, n)
-        add_up(3)
+        add_up(3, LAST_ORDER)
 
-        w2_staged = prod[(LAST, 2)].bitcast(BF16)
+        w2_staged = prod[(LAST, 1)].bitcast(BF16)
         cast(nc.scalar.copy, w2_staged, raw[("o", 0, 0)])
         for h in range(HALVES):
             scale(h, 0, LAST, bank[SUM_BANK[h]][:, 0 : LAST * P])

@@ -31,23 +31,28 @@ BANKS = 8
 RUN = 4
 ORDER = (1, 2, 0)
 
+LAST_ORDER = (1, 0, 2)
+PLAIN = 2
+ON_GPSIMD = (("a", 0, 0),)
+
 LATER = (("e", 2), ("a", 0), ("e", 3), ("a", 1), ("a", 2), ("a", 3))
+
 ACC_BANK = {("e", 1): 2, ("e", 2): 3, ("a", 0): 2, ("e", 3): 3, ("a", 1): 2, ("a", 2): 3, ("a", 3): 2}
 FIRST_PIECES = ((0, 0, V), (1, V, V + P), (4, V + P, S))
 SUM_BANK = (4, 5)
 LAST_SUM_BANK = (3, 2)
-TURN_BANK, RETURN_BANK = (6, 6, 0, 6), (7, 1, 7, 7)
+TURN_BANK, RETURN_BANK = (6, 6, 0), (7, 1, 7)
 VAR_BANK = (0, 0, 1, 6)
 BACK_BANK = (0, 1)
 OUT_BANK = (6, 7)
-WARM = {("e", 1): 5, ("e", 2): 5, ("a", 0): 5, ("a", 1): 6}
-PLAIN = 2
-LAST_ORDER = (1, 0, 2)
-ON_GPSIMD = (("a", 0, 0),)
-BOTH = ()
+WARM = {("e", 1): 5, ("e", 2): 5}
+
+OVERLAP = 64
+MARGIN = 4096
 SLOT = 9216
 SHARE = {
     "win_e_1": ("raw_e_2_0", "low"),
+    "sq_early_0": ("raw_e_2_1", "low"),
     "stage_a_0": ("e0_0", "low"),
     "c_0": ("stage_a_0", "low"),
     "stage_e_3": ("codes_e_2", "low"),
@@ -60,13 +65,12 @@ SHARE = {
     "stage_a_2": ("turned_2", "high"),
     "dif_3": ("raw_a_2_1", "low"),
     "stage_a_3": ("raw_a_2_0", "high"),
+    "c_3_1": ("raw_a_3_1", "mid"),
+    "c_3_2": ("stage_a_2", "high"),
     "win_a_1": ("raw_a_3_1", "low"),
     "sq_0": ("raw_a_3_0", "low"),
     "sq_1": ("raw_a_3_1", "high"),
     "sq_2": ("raw_a_3_0", "high"),
-    "c_3_1": ("raw_a_3_1", "mid"),
-    "c_3_2": ("stage_a_2", "high"),
-    "sq_early_0": ("raw_e_2_1", "low"),
 }
 
 
@@ -84,17 +88,17 @@ def tile_picked_ycovn_corr_p_kernel(
         ends = {}
 
         def sb(name, shape, dtype):
+            if name not in hosts and name not in SHARE:
+                return keep.tile(shape, dtype, name=name, align_bytes=OVERLAP)
+            width = shape[1] * size[dtype]
             if name in hosts:
-                start = hosts.index(name) * SLOT + 4096
-                ends[name] = (start, start + shape[1] * size[dtype])
-                return shared.tile(shape, dtype, name=name, offset=start, align_bytes=64)
-            if name in SHARE:
+                start = hosts.index(name) * SLOT + MARGIN
+            else:
                 host, where = SHARE[name]
                 lo, hi = ends[host]
-                start = {"low": lo + 64 - shape[1] * size[dtype], "mid": lo + 64, "high": hi - 64}[where]
-                ends[name] = (start, start + shape[1] * size[dtype])
-                return shared.tile(shape, dtype, name=name, offset=start, align_bytes=64)
-            return keep.tile(shape, dtype, name=name, align_bytes=64)
+                start = {"low": lo + OVERLAP - width, "mid": lo + OVERLAP, "high": hi - OVERLAP}[where]
+            ends[name] = (start, start + width)
+            return shared.tile(shape, dtype, name=name, offset=start, align_bytes=OVERLAP)
 
         def slot(tile, i):
             return tile[:, i * V : (i + 1) * V]
@@ -204,7 +208,8 @@ def tile_picked_ycovn_corr_p_kernel(
             if staged is None:
                 staged = sb("stage_%s_%d" % (name, t), [P, PASSES * K_PASS], BF16)
             for g in which:
-                cast(gpsimd_copy if (name, t, g) in ON_GPSIMD else nc.scalar.copy, staged[:, g * K_PASS : (g + 1) * K_PASS], raw[(name, t, g)])
+                copy = gpsimd_copy if (name, t, g) in ON_GPSIMD else nc.scalar.copy
+                cast(copy, staged[:, g * K_PASS : (g + 1) * K_PASS], raw[(name, t, g)])
             return staged
 
         def multiply(name, t, staged):
@@ -266,28 +271,16 @@ def tile_picked_ycovn_corr_p_kernel(
             terms = range(3) if t == PLAIN else (1, 2)
             for h in range(HALVES):
                 add_transposed(block(bank[TURN_BANK[t]], h), [block(got[(t, n)], h) for n in terms])
-            if t in BOTH:
-                for h in range(HALVES):
-                    add_transposed(block(bank[TURN_BANK[t]], HALVES + h), [block(got[(t, 2)], h)])
 
         def turn_back(t):
-            turned[t] = sb("turned_%d" % t, [P, 2 * V], F32)
-            nc.scalar.activation(slot(turned[t], 0), slot(bank[TURN_BANK[t]], 0), ACT.Copy, scale=-1.0 if t == LAST else -1.0 / 3.0)
-            if t in BOTH:
-                nc.scalar.activation(slot(turned[t], 1), slot(bank[TURN_BANK[t]], 1), ACT.Copy, scale=3.0)
+            turned[t] = sb("turned_%d" % t, [P, V], F32)
+            nc.scalar.activation(slot(turned[t], 0), slot(bank[TURN_BANK[t]], 0), ACT.Copy, scale=-1.0 / 3.0)
             for h in range(HALVES):
                 nc.tensor.transpose(block(bank[RETURN_BANK[t]], h), block(turned[t], h), ident[:])
-            if t in BOTH:
-                for h in range(HALVES):
-                    add_transposed(block(bank[RETURN_BANK[t]], HALVES + h), [block(turned[t], HALVES + h), block(turned[t], h)])
 
         def fetch(t):
-            wide = 2 if t in BOTH else 1
-            tile = sb("fetched_%d" % t, [P, wide * V], F32)
-            nc.scalar.copy(tile[:], bank[RETURN_BANK[t]][:, 0 : wide * V])
-            coef[(t, 0)] = slot(tile, 0)
-            if t in BOTH:
-                coef[(t, 2)] = slot(tile, 1)
+            coef[(t, 0)] = sb("fetched_%d" % t, [P, V], F32)[:]
+            nc.scalar.copy(coef[(t, 0)], slot(bank[RETURN_BANK[t]], 0))
 
         def runs(ap):
             return ap.rearrange("p (n v) -> p n v", v=V)

import math
from contextlib import ExitStack

import concourse.mybir as mybir
from concourse.masks import make_identity

K, T, S, V, H, N = 1024, 1024, 512, 256, 512, 128
FLOPS = 2 * (2 * K * H * S + H * N * V)

F32 = mybir.dt.float32
BF16 = mybir.dt.bfloat16
I32 = mybir.dt.int32
U32 = mybir.dt.uint32
U16 = mybir.dt.uint16
U8 = mybir.dt.uint8
FP8X4 = mybir.dt.float8_e4m3fn_x4
ALU = mybir.AluOpType
ACT = mybir.ActivationFunctionType

P = 128
PACK = 4
K_PASS = P * PACK
PASSES = K // K_PASS
TILES = H // P
LAST = TILES - 1
HALVES = V // P
GROUP = 16
QUADRANT = 32
ROWS = 4
BANKS = 8
RUN = 4
ORDER = (1, 2, 0)

LAST_ORDER = (1, 0, 2)
PLAIN = 2
ON_GPSIMD = (("a", 0, 0),)

LATER = (("e", 2), ("a", 0), ("e", 3), ("a", 1), ("a", 2), ("a", 3))

ACC_BANK = {("e", 1): 2, ("e", 2): 3, ("a", 0): 2, ("e", 3): 3, ("a", 1): 2, ("a", 2): 3, ("a", 3): 2}
FIRST_PIECES = ((0, 0, V), (1, V, V + P), (4, V + P, S))
SUM_BANK = (4, 5)
LAST_SUM_BANK = (3, 2)
TURN_BANK, RETURN_BANK = (6, 6, 0), (7, 1, 7)
VAR_BANK = (0, 0, 1, 6)
BACK_BANK = (0, 1)
OUT_BANK = (6, 7)
WARM = {("e", 1): 5, ("e", 2): 5}

OVERLAP = 64
MARGIN = 4096
SLOT = 9216
SHARE = {
    "win_e_1": ("raw_e_2_0", "low"),
    "sq_early_0": ("raw_e_2_1", "low"),
    "stage_a_0": ("e0_0", "low"),
    "c_0": ("stage_a_0", "low"),
    "stage_e_3": ("codes_e_2", "low"),
    "fetched_0": ("codes_e_2", "high"),
    "stage_a_1": ("codes_a_0", "low"),
    "c_1": ("stage_a_1", "low"),
    "m_0_0": ("raw_a_1_1", "low"),
    "win_e_3": ("raw_a_1_0", "low"),
    "e0_3": ("turned_2", "low"),
    "stage_a_2": ("turned_2", "high"),
    "dif_3": ("raw_a_2_1", "low"),
    "stage_a_3": ("raw_a_2_0", "high"),
    "c_3_1": ("raw_a_3_1", "mid"),
    "c_3_2": ("stage_a_2", "high"),
    "win_a_1": ("raw_a_3_1", "low"),
    "sq_0": ("raw_a_3_0", "low"),
    "sq_1": ("raw_a_3_1", "high"),
    "sq_2": ("raw_a_3_0", "high"),
}


def tile_picked_ycovn_corr_p_kernel(
    tc, x_words, x_scales, w1, w3, w2, offs, pos1, pos2, pos3, out
):
    nc = tc.nc
    with ExitStack() as ctx:
        keep = ctx.enter_context(tc.tile_pool(name="keep", bufs=1))
        shared = ctx.enter_context(tc.tile_pool(name="shared", bufs=1))
        psum = ctx.enter_context(tc.psum_pool(name="psum", bufs=1))

        hosts = sorted(set(host for host, where in SHARE.values()) - set(SHARE))
        size = {F32: 4, BF16: 2, U32: 4, U8: 1}
        ends = {}

        def sb(name, shape, dtype):
            if name not in hosts and name not in SHARE:
                return keep.tile(shape, dtype, name=name, align_bytes=OVERLAP)
            width = shape[1] * size[dtype]
            if name in hosts:
                start = hosts.index(name) * SLOT + MARGIN
            else:
                host, where = SHARE[name]
                lo, hi = ends[host]
                start = {"low": lo + OVERLAP - width, "mid": lo + OVERLAP, "high": hi - OVERLAP}[where]
            ends[name] = (start, start + width)
            return shared.tile(shape, dtype, name=name, offset=start, align_bytes=OVERLAP)

        def slot(tile, i):
            return tile[:, i * V : (i + 1) * V]

        def block(ap, i):
            return ap[:, i * P : (i + 1) * P]

        bank = [psum.tile([P, S], F32, name="bank%d" % i) for i in range(BANKS)]

        offs_t = sb("offs_t", [P, S // GROUP], U16)
        pos_t = [sb("pos_t%d" % i, [P, V // GROUP], U16) for i in range(3)]
        xw = [sb("xw%d" % g, [P, T], I32) for g in range(PASSES)]
        xs = sb("xs", [P, T], U8)
        raw = {}

        def load_w(name, w, t, g):
            tile = sb("raw_%s_%d_%d" % (name, t, g), [P, PACK * P], F32)
            rows = w[g * K_PASS : (g + 1) * K_PASS, t * P : (t + 1) * P]
            nc.sync.dma_start(
                tile[:].rearrange("p (j c) -> p j c", j=PACK), rows.rearrange("(p j) c -> p j c", j=PACK)
            )
            raw[(name, t, g)] = tile

        def load_x(g):
            nc.sync.dma_start(xw[g][:], x_words[g].rearrange("p n t -> p (n t)").bitcast(I32))

        nc.gpsimd.memset(xs[:].bitcast(I32), 0)
        load_x(0)
        nc.sync.dma_start(offs_t[:], offs)
        for q in range(P // QUADRANT):
            nc.sync.dma_start(
                xs[QUADRANT * q : QUADRANT * q + ROWS * PASSES, :].bitcast(I32),
                x_scales[:, ROWS * q : ROWS * (q + 1), :].bitcast(I32),
            )
        for g in range(PASSES):
            load_w("e", w3, 0, g)
        load_x(1)
        for g in range(PASSES):
            load_w("e", w3, 1, g)
        for tile, src in reversed(list(zip(pos_t, (pos1, pos2, pos3)))):
            nc.sync.dma_start(tile[:], src)
        for name, t in LATER:
            for g in range(PASSES):
                load_w(name, w3 if name == "e" else w1, t, g)
        load_w("o", w2, 0, 0)

        warm = sb("warm", [P, 2], F32)
        nc.vector.memset(warm[:, 0:1], 1.0)
        nc.scalar.activation(warm[:, 1:2], warm[:, 0:1], ACT.Abs_reciprocal_sqrt)

        ident = sb("ident", [P, P], F32)
        make_identity(nc, ident[:])

        xg = [sb("xg%d" % g, [P, S], U32) for g in range(PASSES)]
        xsg = sb("xsg", [P, S], U8)

        def gather_x(g, lo, hi):
            window = xw[g][:].bitcast(U32)
            nc.vector.tensor_copy(xg[g][:, lo:hi], window.indirect(offs_t[:, lo // GROUP : hi // GROUP]))

        def cast(copy, dst, src):
            copy(
                dst.rearrange("p (c run j) -> p c j run", run=RUN, j=PACK),
                src[:].rearrange("p (j c run) -> p c j run", j=PACK, run=RUN),
            )

        def gpsimd_copy(dst, src):
            nc.gpsimd.tensor_scalar(dst, src, 1.0, 0.0, ALU.mult, ALU.add)

        def quantise(name, src):
            codes = sb("codes_" + name, [P, src.shape[1] // PACK], U32)
            scales = sb("scales_" + name, [P, src.shape[1] // PACK], U8)
            nc.vector.quantize_mx(out=codes[:].bitcast(FP8X4), scales=scales[:], in_=src)
            return codes, scales

        def one_pass(t, g, copy):
            tag = "e_%d_%d" % (t, g)
            staged = sb("stage_" + tag, [P, K_PASS], BF16)[:]
            cast(copy, staged, raw[("e", t, g)])
            return quantise(tag, staged)

        def project(dst, codes, scales, g, lo, hi):
            nc.tensor.matmul_mx(
                out=dst[:, lo:hi],
                lhsT=codes[:].bitcast(FP8X4),
                lhsT_scale=scales[:],
                rhs=xg[g][:, lo:hi].bitcast(FP8X4),
                rhs_scale=xsg[ROWS * g : P, lo:hi],
                start=(g == 0),
                stop=(g == PASSES - 1),
            )

        made = {}

        def keep_warm(dst, codes, scales, g):
            nc.tensor.matmul_mx(
                out=dst[:],
                lhsT=codes[:].bitcast(FP8X4),
                lhsT_scale=scales[:],
                rhs=xg[g][:].bitcast(FP8X4),
                rhs_scale=xsg[ROWS * g : P, :],
                start=True,
                stop=True,
            )

        def stage(name, t, staged=None, which=(0, 1)):
            if staged is None:
                staged = sb("stage_%s_%d" % (name, t), [P, PASSES * K_PASS], BF16)
            for g in which:
                copy = gpsimd_copy if (name, t, g) in ON_GPSIMD else nc.scalar.copy
                cast(copy, staged[:, g * K_PASS : (g + 1) * K_PASS], raw[(name, t, g)])
            return staged

        def multiply(name, t, staged):
            codes, scales = quantise("%s_%d" % (name, t), staged[:])
            made[(name, t)] = (codes, scales)
            if (name, t) != ("a", LAST):
                passes(name, t)

        def passes(name, t):
            codes, scales = made[(name, t)]
            for g in range(PASSES):
                project(bank[ACC_BANK[(name, t)]], block(codes, g), block(scales, g), g, 0, S)
            if (name, t) in WARM:
                keep_warm(bank[WARM[(name, t)]], block(codes, 0), block(scales, 0), 0)

        def weights(name, t):
            multiply(name, t, stage(name, t))

        win = {}

        def empty(name, t):
            win[(name, t)] = sb("win_%s_%d" % (name, t), [P, S], F32)
            nc.scalar.copy(win[(name, t)][:], bank[ACC_BANK[(name, t)]][:])

        win[("e", 0)] = sb("win_e_0", [P, S], F32)

        def add_transposed(dst, srcs):
            for i, src in enumerate(srcs):
                nc.tensor.matmul(
                    dst, lhsT=src, rhs=ident[:], is_transpose=True, start=(i == 0), stop=(i == len(srcs) - 1)
                )

        got, coef, turned, centred = {}, {}, {}, {}

        def entries(n, lo, hi):
            return pos_t[n][:, lo // GROUP : hi // GROUP]

        def pick(t, cuts=(0, V)):
            got[(t, 0)] = sb("e0_%d" % t, [P, V], F32)[:]
            for lo, hi in zip(cuts, cuts[1:]):
                nc.vector.tensor_copy(got[(t, 0)][:, lo:hi], win[("e", t)][:].indirect(entries(0, lo, hi)))

        def differences(t, cuts=(0, V)):
            got[t] = sb("dif_%d" % t, [P, 2 * V], F32)[:]
            for n in (1, 2):
                got[(t, n)] = slot(got[t], n - 1)
                for lo, hi in zip(cuts, cuts[1:]) if n == 1 else ((0, V),):
                    nc.vector.tensor_tensor(
                        got[(t, n)][:, lo:hi], win[("e", t)][:].indirect(entries(n, lo, hi)), got[(t, 0)][:, lo:hi], ALU.subtract
                    )

        def pick_all(t):
            got[t] = sb("e_%d" % t, [P, 3 * V], F32)[:]
            for n in range(3):
                got[(t, n)] = slot(got[t], n)
                nc.vector.tensor_copy(got[(t, n)], win[("e", t)][:].indirect(pos_t[n][:]))

        def turn(t):
            terms = range(3) if t == PLAIN else (1, 2)
            for h in range(HALVES):
                add_transposed(block(bank[TURN_BANK[t]], h), [block(got[(t, n)], h) for n in terms])

        def turn_back(t):
            turned[t] = sb("turned_%d" % t, [P, V], F32)
            nc.scalar.activation(slot(turned[t], 0), slot(bank[TURN_BANK[t]], 0), ACT.Copy, scale=-1.0 / 3.0)
            for h in range(HALVES):
                nc.tensor.transpose(block(bank[RETURN_BANK[t]], h), block(turned[t], h), ident[:])

        def fetch(t):
            coef[(t, 0)] = sb("fetched_%d" % t, [P, V], F32)[:]
            nc.scalar.copy(coef[(t, 0)], slot(bank[RETURN_BANK[t]], 0))

        def runs(ap):
            return ap.rearrange("p (n v) -> p n v", v=V)

        def centre(engine, t, minus, first, count):
            tile = sb("c_%d" % t, [P, count * V], F32)
            centred[t] = tile
            engine.tensor_tensor(
                runs(tile[:]), runs(got[t][:, 0 : count * V]), minus.unsqueeze(1).to_broadcast([P, count, V]), ALU.add
            )
            for i in range(count):
                coef[(t, first + i)] = slot(tile, i)

        root = sb("root", [P, HALVES * H], F32)

        early = {}

        def square_early(t):
            early[t] = sb("sq_early_%d" % t, [P, V], F32)[:]
            nc.scalar.activation(early[t], got[(t, 2)], ACT.Square, scale=math.sqrt(0.5))

        def squares(t):
            count = 3 if t == PLAIN else 2
            sq = sb("sq_%d" % t, [P, count * V], F32)
            if t == PLAIN:
                nc.scalar.activation(sq[:], centred[t][:], ACT.Square)
            else:
                if t not in early:
                    nc.scalar.activation(slot(sq, 0), got[(t, 2)], ACT.Square, scale=math.sqrt(0.5))
                nc.scalar.activation(slot(sq, 1), coef[(t, 1)], ACT.Square, scale=math.sqrt(1.5 / 9.0 if t == LAST else 1.5))
            for h in range(HALVES):
                terms = [block(early[t] if n == 0 and t in early else slot(sq, n), h) for n in range(count)]
                add_transposed(block(bank[VAR_BANK[t]], 2 * h + t % 2), terms)

        def inverse_root(first, tiles):
            lo = first % 2 * P
            nc.scalar.activation(
                root[:].rearrange("v (h i) -> v h i", h=HALVES)[:, :, first * P : (first + tiles) * P],
                bank[VAR_BANK[first]][:].rearrange("v (h i) -> v h i", h=HALVES)[:, :, lo : lo + tiles * P],
                ACT.Abs_reciprocal_sqrt,
                bias=8.1 if first == LAST else 0.9,
                scale=27.0 if first == LAST else 3.0,
            )

        prod = {}

        def z_of(t, h):
            return block(bank[SUM_BANK[h]], t) if t < LAST else block(bank[LAST_SUM_BANK[h]], 0)

        def product(t, n):
            prod[(t, n)] = sb("m_%d_%d" % (t, n), [P, V], F32)[:]
            src = picked[(t, n)] if (t, n) in picked else win[("a", t)][:].indirect(pos_t[n][:])
            nc.vector.tensor_tensor(prod[(t, n)], src, coef[(t, n)], ALU.mult)

        picked = {}

        def pick_a(t, n):
            picked[(t, n)] = sb("a_%d_%d" % (t, n), [P, V], F32)[:]
            nc.scalar.activation(picked[(t, n)], win[("a", t)][:].indirect(pos_t[n][:]), ACT.Copy)

        def add_up(t, order=ORDER):
            for n in order:
                for h in range(HALVES):
                    nc.tensor.matmul(
                        z_of(t, h),
                        lhsT=block(prod[(t, n)], h),
                        rhs=ident[:],
                        is_transpose=True,
                        start=(n == order[0]),
                        stop=(n == order[-1]),
                    )

        rr_turned = [sb("rrT%d" % h, [P, H], BF16) for h in range(HALVES)]

        def scale(h, first, tiles, z):
            lo, hi = first * P, (first + tiles) * P
            nc.vector.tensor_tensor(
                rr_turned[h][:].rearrange("v (u p s) -> v u p s", u=2, s=2)[:, :, lo // PACK : hi // PACK, :],
                z.rearrange("v (p u s) -> v u p s", u=2, s=2),
                root[:, h * H + lo : h * H + hi].rearrange("v (p u s) -> v u p s", u=2, s=2),
                ALU.mult,
            )

        gather_x(0, 0, S)
        nc.vector.tensor_copy(xsg[:], xs[:].indirect(offs_t[:]))
        codes, scales = one_pass(0, 0, nc.scalar.copy)
        for b, lo, hi in FIRST_PIECES:
            project(bank[b], codes, scales, 0, lo, hi)
        codes, scales = one_pass(0, 1, nc.scalar.copy)
        for b, lo, hi in FIRST_PIECES:
            gather_x(1, lo, hi)
            project(bank[b], codes, scales, 1, lo, hi)
        for b, lo, hi in FIRST_PIECES:
            nc.scalar.copy(win[("e", 0)][:, lo:hi], bank[b][:, lo:hi])
        for g, copy in enumerate((nc.scalar.copy, nc.vector.tensor_copy)):
            codes, scales = one_pass(1, g, copy)
            project(bank[ACC_BANK[("e", 1)]], codes, scales, g, 0, S)
        if ("e", 1) in WARM:
            keep_warm(bank[WARM[("e", 1)]], codes, scales, 1)

        pick(0, (0, P, V))
        differences(0, (0, P, V))
        turn(0)
        weights("e", 2)
        empty("e", 1)
        square_early(0)
        pick(1, (0, P, V))
        differences(1, (0, P, V))
        staged = stage("a", 0)
        turn_back(0)
        turn(1)
        multiply("a", 0, staged)
        empty("e", 2)
        staged = stage("e", 3, which=(0,))
        fetch(0)
        centre(nc.gpsimd, 0, coef[(0, 0)], 1, 2)
        pick_all(2)
        turn_back(1)
        turn(2)
        multiply("e", 3, stage("e", 3, staged, (1,)))
        empty("a", 0)
        product(0, 1)
        product(0, 2)
        staged = stage("a", 1)
        turn_back(2)
        multiply("a", 1, staged)
        fetch(1)
        centre(nc.gpsimd, 1, coef[(1, 0)], 1, 2)
        product(0, 0)
        centre(nc.vector, 2, slot(bank[RETURN_BANK[2]], 0), 0, 3)
        empty("e", 3)
        pick(3)
        weights("a", 2)
        differences(3)
        weights("a", 3)
        for n, first, second, factor in ((1, 1, 2, 2.0), (2, 2, 1, 2.0), (0, 1, 2, -1.0)):
            coef[(LAST, n)] = sb("c_3_%d" % n, [P, V], F32)[:]
            nc.vector.scalar_tensor_tensor(
                coef[(LAST, n)], got[(LAST, first)], factor, got[(LAST, second)], ALU.mult, ALU.subtract
            )
        squares(2)
        squares(0)
        empty("a", 1)
        passes("a", 3)
        add_up(0)
        squares(1)
        product(1, 1)
        pick_a(1, 0)
        product(1, 2)
        empty("a", 2)
        product(1, 0)
        add_up(1)
        squares(3)
        pick_a(2, 0)
        product(2, 1)
        empty("a", 3)
        inverse_root(2, 1)
        pick_a(3, 2)
        inverse_root(0, 2)
        product(2, 2)
        product(2, 0)
        add_up(2)
        inverse_root(3, 1)
        for n in LAST_ORDER:
            product(3, n)
        add_up(3, LAST_ORDER)

        w2_staged = prod[(LAST, 1)].bitcast(BF16)
        cast(nc.scalar.copy, w2_staged, raw[("o", 0, 0)])
        for h in range(HALVES):
            scale(h, 0, LAST, bank[SUM_BANK[h]][:, 0 : LAST * P])
        for h in range(HALVES):
            scale(h, LAST, 1, z_of(LAST, h))
        w2_codes, w2_scales = quantise("w2", w2_staged)

        for h, store in zip(range(HALVES), (nc.sync, nc.scalar)):
            words = rr_turned[h][:].bitcast(F32)
            back = bank[BACK_BANK[h]][:, 0 : 2 * P].rearrange("p (u v) -> p u v", u=2)
            for u in range(2):
                nc.tensor.transpose(back[:, u, :], block(words, u), ident[:])
            rr = sb("rr%d" % h, [P, P * PACK], BF16)
            nc.scalar.copy(rr[:].bitcast(F32).rearrange("p (v u) -> p v u", u=2), back.rearrange("p u v -> p v u"))
            rr_codes, rr_scales = quantise("rr%d" % h, rr[:])
            res = block(bank[OUT_BANK[h]], 0)
            nc.tensor.matmul_mx(
                out=res,
                lhsT=w2_codes[:].bitcast(FP8X4),
                lhsT_scale=w2_scales[:],
                rhs=rr_codes[:].bitcast(FP8X4),
                rhs_scale=rr_scales[:],
                start=True,
                stop=True,
            )
            res_sb = sb("res_sb%d" % h, [P, P], F32)
            nc.scalar.copy(res_sb[:], res)
            store.dma_start(block(out, h), res_sb[:])
